import numpy as np
import ml_dtypes


def mxq(x, axis, fmt="e4m3"):
    dtype, down = {"e4m3": (ml_dtypes.float8_e4m3fn, 7), "e5m2": (ml_dtypes.float8_e5m2, 14)}[fmt]
    v = np.moveaxis(np.asarray(x, np.float32).astype(ml_dtypes.bfloat16).astype(np.float64), axis, -1)
    blocks = v.reshape(v.shape[:-1] + (-1, 32))
    amax = np.abs(blocks).max(-1, keepdims=True)
    byte = np.maximum(np.where(amax > 0, np.frexp(amax)[1] - 1 + 127, 0) - down, 1)
    scale = np.exp2(byte - 127.0)
    codes = (blocks / scale).astype(np.float32).astype(dtype).astype(np.float64)
    return np.moveaxis((codes * scale).reshape(v.shape), -1, axis)


WIDE = False


def mx_kscale(k):
    if not WIDE:
        return np.ones(k)
    levels = np.array([10, -10, 5, -5, 0])
    if k % 512:
        return np.exp2(np.random.permutation(np.resize(levels, k // 32))).repeat(32)
    a = np.empty((k // 512, 16))
    for p in range(k // 512):
        a[p, :8] = np.random.permutation(np.resize(levels, 8))
        for g in range(8):
            far = levels[np.abs(levels - a[p, g]) >= 10]
            a[p, g + 8] = far[np.random.randint(len(far))]
    return np.exp2(a.ravel()).repeat(32)


def f64(x):
    return np.asarray(x).astype(np.float64)


def striped(idx):
    return np.tile(idx.reshape(-1, 16).T, (8, 1)).astype(np.uint16)


def unstriped(offs):
    return offs[:16].T.reshape(-1).astype(np.int64)


def striped8(idx):
    return np.concatenate([x.reshape(-1, 16).T for x in idx]).astype(np.uint16)


def runs(offs, k):
    lists = np.stack([offs[16 * r : 16 * r + 16].T.reshape(-1) for r in range(8)]).astype(np.int64)
    return lists[np.arange(k) % 512 // 64]


def pack_weight(w):
    k, n = w.shape
    w = f64(np.asarray(w, np.float32).astype(ml_dtypes.bfloat16)).reshape(k // 32, 32, n)
    amax = np.abs(w).max(1)
    byte = np.clip(np.where(amax > 0, np.frexp(amax)[1] - 1 + 127 - 7, 1), 1, 254)
    scaled = (w * np.exp2(127.0 - byte)[:, None, :]).reshape(k, n).astype(np.float32)
    words = np.ascontiguousarray(scaled.reshape(k // 512, 128, 4, n).transpose(0, 1, 3, 2)).astype(ml_dtypes.float8_e4m3fn).view(np.uint8)
    return words, np.ascontiguousarray(byte.astype(np.uint8).reshape(k // 512, 16, n))


def unpack_weight(words, scales):
    g, p, n, _ = words.shape
    vals = np.ascontiguousarray(words).view(ml_dtypes.float8_e4m3fn).astype(np.float64) * np.repeat(np.exp2(scales.astype(np.float64) - 127.0), 8, axis=1)[..., None]
    return vals.transpose(0, 1, 3, 2).reshape(g * 512, n)


E2M1 = np.array([0.0, 0.5, 1.0, 1.5, 2.0, 3.0, 4.0, 6.0, -0.0, -0.5, -1.0, -1.5, -2.0, -3.0, -4.0, -6.0])


def pack_fp4(w):
    k, n = w.shape
    w = f64(np.asarray(w, np.float32).astype(ml_dtypes.bfloat16)).reshape(k // 32, 32, n)
    amax = np.abs(w).max(1)
    mant, ex = np.frexp(amax / 6.0)
    byte = np.clip(np.where(amax > 0, np.where(mant > 0.5, ex, ex - 1) + 127, 1), 1, 254)
    scaled = (w * np.exp2(127.0 - byte)[:, None, :]).reshape(k, n).astype(np.float32)
    c = np.ascontiguousarray(scaled.reshape(k // 512, 128, 4, n).transpose(0, 1, 3, 2)).astype(ml_dtypes.float4_e2m1fn).view(np.uint8) & 0xF
    words = (c[..., 0::2] | (c[..., 1::2] << 4)).reshape(k // 512, 128, 2 * n)
    return np.ascontiguousarray(words), np.ascontiguousarray(byte.astype(np.uint8).reshape(k // 512, 16, n))


def unpack_fp4(words, scales):
    g, _, n = scales.shape
    words = np.ascontiguousarray(words).reshape(g, 128, n, 2)
    nib = np.empty((g, 128, n, 4), np.uint8)
    nib[..., 0::2] = words & 0xF
    nib[..., 1::2] = words >> 4
    vals = E2M1[nib] * np.repeat(np.exp2(scales.astype(np.float64) - 127.0), 8, axis=1)[..., None]
    return vals.transpose(0, 1, 3, 2).reshape(g * 512, n)


def gelu(v):
    return 0.5 * v * (1.0 + np.tanh(np.sqrt(2.0 / np.pi) * (v + 0.044715 * v**3)))

def planes(y):
    n, m = y.shape
    v = y.astype(np.float32).astype(ml_dtypes.bfloat16).astype(np.float64).reshape(n // 32, 32, m)
    top = np.abs(v).max(1)
    byte = np.clip(np.where(top > 0, np.frexp(top)[1] - 1 + 127 - 7, 1), 1, 254)
    codes = (v * np.exp2(127.0 - byte)[:, None, :]).reshape(n, m).astype(np.float32).astype(ml_dtypes.float8_e4m3fn).view(np.uint8)
    words = codes.reshape(n // 512, 128, 4, m).transpose(0, 1, 3, 2)
    return np.ascontiguousarray(words), np.ascontiguousarray(byte.astype(np.uint8).reshape(n // 512, 16, m))


K, T, S, N, H, U = 1024, 2048, 512, 512, 512, 512


def setup_inputs():
    n = np.random.standard_normal
    s = mx_kscale(K)[:, None]
    u = mx_kscale(H)
    packed_xT = pack_weight(n((K, T)) * s)
    packed_w1 = pack_fp4(n((K, H)) / np.sqrt(K) / s)
    packed_w2 = pack_fp4(n((H, N)) / np.sqrt(H) / u[:, None])
    return {
        "x_words": packed_xT[0],
        "x_scales": packed_xT[1],
        "w1_words": packed_w1[0],
        "w1_scales": packed_w1[1],
        "mu": (0.5 * n((H, U))).astype(np.float32),
        "rs": (np.random.uniform(0.5, 1.5, (H, U)) * u[:, None]).astype(np.float32),
        "w2_words": packed_w2[0],
        "w2_scales": packed_w2[1],
        "offs": striped(np.random.permutation(T)[:S]),
        "cl": striped8(np.stack([np.random.permutation(U)[(U * np.random.uniform(0, 1, S) ** 4).astype(np.int64)] for _ in range(8)])),
    }


def reference(x_words, x_scales, w1_words, w1_scales, mu, rs, w2_words, w2_scales, offs, cl):
    xq = unpack_weight(x_words, x_scales)[:, unstriped(offs)]
    y = unpack_fp4(w1_words, w1_scales).T @ xq
    z = gelu((y - (f64(mu)[np.arange(H)[:, None], runs(cl, H)])) * (f64(rs)[np.arange(H)[:, None], runs(cl, H)]))
    out_0 = unpack_fp4(w2_words, w2_scales).T @ mxq(z, 0, "e4m3")
    return (out_0,) + planes(out_0)

@@ -1,0 +1,206 @@
+from contextlib import ExitStack
+
+import concourse.mybir as mybir
+
+F32 = mybir.dt.float32
+BF16 = mybir.dt.bfloat16
+I32 = mybir.dt.int32
+U32 = mybir.dt.uint32
+U16 = mybir.dt.uint16
+U8 = mybir.dt.uint8
+FP8X4 = mybir.dt.float8_e4m3fn_x4
+FP4X4 = mybir.dt.float4_e2m1fn_x4
+ALU = mybir.AluOpType
+ACT = mybir.ActivationFunctionType
+
+K, T, S, N, H, U = 1024, 2048, 512, 512, 512, 512
+FLOPS = 2 * K * H * S + 2 * H * N * S
+
+P = 128
+PACK = 4
+PASSES = K // (P * PACK)
+QUADS = 4
+UNIT = 128
+CHUNKS = ((0, 1), (2,), (3,))
+
+
+def tile_picked_clnorm_gelu_po_kernel(
+    tc, x_words, x_scales, w1_words, w1_scales, mu, rs, w2_words, w2_scales, offs, cl, out_0, out_1, out_2
+):
+    nc = tc.nc
+    with ExitStack() as ctx:
+        keep = ctx.enter_context(tc.tile_pool(name="keep", bufs=1))
+        psum = ctx.enter_context(tc.psum_pool(name="psum", bufs=1))
+
+        offs_sb = keep.tile([P, S // 16], U16, name="offs_sb")
+        cl_sb = keep.tile([P, S // 16], U16, name="cl_sb")
+        w1s_raw = keep.tile([P, PASSES * H], U8, name="w1s_raw", align_bytes=64)
+        w2s_raw = keep.tile([P, N], U8, name="w2s_raw", align_bytes=64)
+        xs_second = keep.tile([P, S], U8, name="xs_second", align_bytes=64)
+        xs_picked = keep.tile([P, S], U8, name="xs_picked", align_bytes=64)
+        w1w = keep.tile([P, PASSES * 2 * H], U8, name="w1w", align_bytes=64)
+        x_win = [keep.tile([P, T], I32, name=f"x_win{g}", tag=f"x_win{g}", align_bytes=64) for g in range(PASSES)]
+
+        with tc.tile_pool(name="head", bufs=1) as head:
+            xs_win = head.tile([P, T], U8, name="xs_win", align_bytes=64)
+            w1w_raw = head.tile([P, PASSES * 2 * H], U8, name="w1w_raw", align_bytes=64)
+            for plane in (xs_win, w1s_raw, w2s_raw, xs_second):
+                nc.vector.memset(plane[:].bitcast(I32), 0)
+
+            nc.sync.dma_start(offs_sb[:], offs)
+            nc.sync.dma_start(cl_sb[:], cl)
+            for g in range(PASSES):
+                nc.sync.dma_start(out=w1w_raw[:, g * 2 * H : (g + 1) * 2 * H].bitcast(I32), in_=w1_words[g].bitcast(I32))
+            for q in range(QUADS):
+                nc.scalar.dma_start(
+                    out=xs_win[32 * q : 32 * q + 4 * PASSES, :].bitcast(I32),
+                    in_=x_scales[:, 4 * q : 4 * q + 4, :].bitcast(I32),
+                )
+            for g in range(PASSES):
+                nc.sync.dma_start(out=x_win[g][:], in_=x_words[g].rearrange("p n t -> p (n t)").bitcast(I32))
+            for q in range(QUADS):
+                nc.gpsimd.dma_start(
+                    out=w1s_raw[32 * q : 32 * q + 4, :].bitcast(I32).rearrange("r (g c) -> r g c", g=PASSES),
+                    in_=w1_scales[:, 4 * q : 4 * q + 4, :].bitcast(I32).rearrange("g r c -> r g c"),
+                )
+            for q in range(QUADS):
+                nc.gpsimd.dma_start(
+                    out=w2s_raw[32 * q : 32 * q + 4, :].bitcast(I32),
+                    in_=w2_scales[0, 4 * q : 4 * q + 4, :].bitcast(I32),
+                )
+
+            nc.vector.tensor_copy(
+                out=w1w[:].rearrange("p (g t m b) -> p g t m b", g=PASSES, t=PACK, b=2),
+                in_=w1w_raw[:].rearrange("p (g m t b) -> p g t m b", g=PASSES, t=PACK, b=2),
+            )
+            nc.vector.tensor_copy(out=xs_picked[:], in_=xs_win[:].indirect(offs_sb[:]))
+
+        last = 32 * (QUADS - 1) + 4
+        nc.scalar.dma_start(out=xs_second[0:last, :].bitcast(I32), in_=xs_picked[4 : 4 + last, :].bitcast(I32))
+
+        tables = ctx.enter_context(tc.tile_pool(name="tables", bufs=1))
+        w2w_raw = tables.tile([P, 2 * N], U8, name="w2w_raw", tag="w2w_raw", align_bytes=64)
+        mu_rows = mu.rearrange("(p t) u -> p t u", t=PACK)
+        rs_rows = rs.rearrange("(p t) u -> p t u", t=PACK)
+        mu_win = [tables.tile([P, U], F32, name=f"mu_win{t}", align_bytes=64) for t in range(PACK)]
+        rs_win = [tables.tile([P, U], F32, name=f"rs_win{t}", align_bytes=64) for t in range(PACK)]
+        nc.sync.dma_start(out=w2w_raw[:].bitcast(I32), in_=w2_words[0].bitcast(I32))
+        for pair in range(PACK // 2):
+            for win, rows in ((mu_win, mu_rows), (rs_win, rs_rows)):
+                for t in (2 * pair, 2 * pair + 1):
+                    nc.sync.dma_start(out=win[t][:], in_=rows[:, t, :])
+
+        x_picked = [keep.tile([P, S], U32, name=f"x_picked{g}", align_bytes=64) for g in range(PASSES)]
+        nc.vector.tensor_copy(out=x_picked[0][:], in_=x_win[0][:].bitcast(U32).indirect(offs_sb[:]))
+        w1s = keep.tile([P, PASSES * H], U8, name="w1s", align_bytes=64)
+        nc.vector.tensor_copy(
+            out=w1s[:].rearrange("p (g t m) -> p g t m", g=PASSES, t=PACK),
+            in_=w1s_raw[:].rearrange("p (g m t) -> p g t m", g=PASSES, t=PACK),
+        )
+        nc.vector.tensor_copy(out=x_picked[1][:], in_=x_win[1][:].bitcast(U32).indirect(offs_sb[:]))
+
+        x_planes = (xs_picked, xs_second)
+        y_ps = [psum.tile([P, S], F32, name=f"y_ps{t}") for t in range(PACK)]
+        for g in range(PASSES):
+            for t in range(PACK):
+                c0 = g * H + t * P
+                nc.tensor.matmul_mx(
+                    out=y_ps[t][:],
+                    lhsT=w1w[:, 2 * c0 : 2 * (c0 + P)].bitcast(FP4X4),
+                    lhsT_scale=w1s[:, c0 : c0 + P],
+                    rhs=x_picked[g][:].bitcast(FP8X4),
+                    rhs_scale=x_planes[g][:],
+                    start=(g == 0),
+                    stop=(g == PASSES - 1),
+                )
+
+        w2w = keep.tile([P, 2 * N], U8, name="w2w", tag=f"x_win{PASSES - 1}", align_bytes=64)
+        nc.vector.tensor_copy(
+            out=w2w[:].rearrange("p (t m b) -> p t m b", t=PACK, b=2),
+            in_=w2w_raw[:].rearrange("p (m t b) -> p t m b", t=PACK, b=2),
+        )
+        w2s = tables.tile([P, N], U8, name="w2s", tag="w2w_raw", align_bytes=64)
+        nc.vector.tensor_copy(
+            out=w2s[:].rearrange("p (t m) -> p t m", t=PACK),
+            in_=w2s_raw[:].rearrange("p (m t) -> p t m", t=PACK),
+        )
+
+        first = len(CHUNKS[0]) * UNIT
+        y_sb = [keep.tile([P, S], F32, name=f"y_sb{t}") for t in range(PACK)]
+        for lo, hi in ((0, first), (first, S)):
+            for t in range(PACK):
+                nc.scalar.copy(out=y_sb[t][:, lo:hi], in_=y_ps[t][:, lo:hi])
+
+        out_rows = out_0.rearrange("(p t) j -> p t j", t=PACK)
+        out_words = out_1[0].rearrange("p n t -> p (n t)").bitcast(I32)
+        o_scales = keep.tile([P, S], U8, name="o_scales", align_bytes=64)
+        z = {}
+        o_bf = {}
+
+        def cols(u):
+            return slice(u * UNIT, (u + 1) * UNIT)
+
+        def normalise_pair(chunk, pair, normed, tag):
+            lo, hi = chunk[0] * UNIT, (chunk[-1] + 1) * UNIT
+            lists = cl_sb[:, lo // 16 : hi // 16]
+            diff = keep.tile([P, 2, hi - lo], F32, name=f"diff{chunk[0]}_{pair}", tag=tag, align_bytes=64)
+            for i in range(2):
+                t = 2 * pair + i
+                nc.vector.tensor_tensor(diff[:, i, :], mu_win[t][:].indirect(lists), y_sb[t][:, lo:hi], ALU.subtract)
+            for i in range(2):
+                t = 2 * pair + i
+                nc.vector.tensor_tensor(normed[:, t, :], rs_win[t][:].indirect(lists), diff[:, i, :], ALU.mult)
+
+        def activate(u, normed):
+            z[u] = keep.tile([P, UNIT, PACK], BF16, name=f"z{u}", tag=f"z{u}", align_bytes=64)
+            nc.scalar.activation(out=z[u][:], in_=normed.rearrange("p t j -> p j t"), func=ACT.Gelu_apprx_tanh, scale=-1.0)
+
+        def second_product(u):
+            z_words = keep.tile([P, UNIT], U32, name=f"z_words{u}", align_bytes=64)
+            z_scales = keep.tile([P, UNIT], U8, name=f"z_scales{u}", align_bytes=64)
+            nc.vector.quantize_mx(out=z_words[:].bitcast(FP8X4), scales=z_scales[:], in_=z[u][:].rearrange("p j t -> p (j t)"))
+            o_ps = psum.tile([P, PACK, UNIT], F32, name=f"o_ps{u}")
+            for t in range(PACK):
+                nc.tensor.matmul_mx(
+                    out=o_ps[:, t, :],
+                    lhsT=w2w[:, 2 * t * P : 2 * (t + 1) * P].bitcast(FP4X4),
+                    lhsT_scale=w2s[:, t * P : (t + 1) * P],
+                    rhs=z_words[:].bitcast(FP8X4),
+                    rhs_scale=z_scales[:],
+                    start=True,
+                    stop=True,
+                )
+            o_bf[u] = keep.tile([P, UNIT, PACK], BF16, name=f"o_bf{u}", tag=f"o_bf{u}", align_bytes=64)
+            nc.scalar.copy(out=o_bf[u][:], in_=o_ps[:].rearrange("p t j -> p j t"))
+            o_sb = keep.tile([P, PACK, UNIT], F32, name=f"o_sb{u}")
+            nc.scalar.copy(out=o_sb[:], in_=o_ps[:])
+            nc.sync.dma_start(out=out_rows[:, :, cols(u)], in_=o_sb[:])
+
+        def hand_on(u):
+            o_words = keep.tile([P, UNIT], I32, name=f"o_words{u}", align_bytes=64)
+            nc.vector.quantize_mx(
+                out=o_words[:].bitcast(FP8X4), scales=o_scales[:, cols(u)], in_=o_bf[u][:].rearrange("p j t -> p (j t)")
+            )
+            nc.sync.dma_start(out=out_words[:, cols(u)], in_=o_words[:])
+
+        for c in range(len(CHUNKS) + 2):
+            if c >= 2:
+                for u in CHUNKS[c - 2]:
+                    hand_on(u)
+            if c < len(CHUNKS):
+                chunk = CHUNKS[c]
+                slot = f"o_bf{CHUNKS[c - 2][0]}" if c >= 2 else f"normed{c}"
+                normed = keep.tile([P, PACK, len(chunk) * UNIT], F32, name=f"normed{c}", tag=slot, align_bytes=64)
+                normalise_pair(chunk, 0, normed, f"diff{c}")
+            if 1 <= c <= len(CHUNKS):
+                for u in CHUNKS[c - 1]:
+                    second_product(u)
+            if c < len(CHUNKS):
+                normalise_pair(chunk, 1, normed, f"z{chunk[0] - 1}")
+                for i, u in enumerate(chunk):
+                    activate(u, normed[:, :, cols(i)])
+
+        for q in range(QUADS):
+            nc.scalar.dma_start(
+                out=out_2[0, 4 * q : 4 * q + 4, :].bitcast(I32), in_=o_scales[32 * q : 32 * q + 4, :].bitcast(I32)
+            )

@@ -35,7 +35,7 @@ def tile_picked_clnorm_gelu_po_kernel(
         offs_sb = keep.tile([P, S // 16], U16, name="offs_sb")
         cl_sb = keep.tile([P, S // 16], U16, name="cl_sb")
         w1s_raw = keep.tile([P, PASSES * H], U8, name="w1s_raw", align_bytes=64)
-        w2s_raw = keep.tile([P, N], U8, name="w2s_raw", align_bytes=64)
+        w1w_raw = keep.tile([P, PASSES * 2 * H], U8, name="w1w_raw", align_bytes=64)
         xs_second = keep.tile([P, S], U8, name="xs_second", align_bytes=64)
         xs_picked = keep.tile([P, S], U8, name="xs_picked", align_bytes=64)
         w1w = keep.tile([P, PASSES * 2 * H], U8, name="w1w", align_bytes=64)
@@ -43,54 +43,59 @@ def tile_picked_clnorm_gelu_po_kernel(
 
         with tc.tile_pool(name="head", bufs=1) as head:
             xs_win = head.tile([P, T], U8, name="xs_win", align_bytes=64)
-            w1w_raw = head.tile([P, PASSES * 2 * H], U8, name="w1w_raw", align_bytes=64)
-            for plane in (xs_win, w1s_raw, w2s_raw, xs_second):
+            for plane in (xs_win, w1s_raw, xs_second):
                 nc.vector.memset(plane[:].bitcast(I32), 0)
 
+            def load_x(g):
+                nc.sync.dma_start(out=x_win[g][:], in_=x_words[g].rearrange("p n t -> p (n t)").bitcast(I32))
+
             nc.sync.dma_start(offs_sb[:], offs)
-            nc.sync.dma_start(cl_sb[:], cl)
-            for g in range(PASSES):
-                nc.sync.dma_start(out=w1w_raw[:, g * 2 * H : (g + 1) * 2 * H].bitcast(I32), in_=w1_words[g].bitcast(I32))
+            nc.sync.dma_start(
+                out=w1w_raw[:].bitcast(I32).rearrange("p (g c) -> p g c", g=PASSES),
+                in_=w1_words.bitcast(I32).rearrange("g p c -> p g c"),
+            )
             for q in range(QUADS):
-                nc.scalar.dma_start(
+                nc.sync.dma_start(
                     out=xs_win[32 * q : 32 * q + 4 * PASSES, :].bitcast(I32),
                     in_=x_scales[:, 4 * q : 4 * q + 4, :].bitcast(I32),
                 )
-            for g in range(PASSES):
-                nc.sync.dma_start(out=x_win[g][:], in_=x_words[g].rearrange("p n t -> p (n t)").bitcast(I32))
+            load_x(0)
             for q in range(QUADS):
-                nc.gpsimd.dma_start(
+                nc.sync.dma_start(
                     out=w1s_raw[32 * q : 32 * q + 4, :].bitcast(I32).rearrange("r (g c) -> r g c", g=PASSES),
                     in_=w1_scales[:, 4 * q : 4 * q + 4, :].bitcast(I32).rearrange("g r c -> r g c"),
                 )
-            for q in range(QUADS):
-                nc.gpsimd.dma_start(
-                    out=w2s_raw[32 * q : 32 * q + 4, :].bitcast(I32),
-                    in_=w2_scales[0, 4 * q : 4 * q + 4, :].bitcast(I32),
-                )
-
-            nc.vector.tensor_copy(
-                out=w1w[:].rearrange("p (g t m b) -> p g t m b", g=PASSES, t=PACK, b=2),
-                in_=w1w_raw[:].rearrange("p (g m t b) -> p g t m b", g=PASSES, t=PACK, b=2),
-            )
+            load_x(1)
+            nc.sync.dma_start(cl_sb[:], cl)
             nc.vector.tensor_copy(out=xs_picked[:], in_=xs_win[:].indirect(offs_sb[:]))
 
         last = 32 * (QUADS - 1) + 4
         nc.scalar.dma_start(out=xs_second[0:last, :].bitcast(I32), in_=xs_picked[4 : 4 + last, :].bitcast(I32))
 
         tables = ctx.enter_context(tc.tile_pool(name="tables", bufs=1))
-        w2w_raw = tables.tile([P, 2 * N], U8, name="w2w_raw", tag="w2w_raw", align_bytes=64)
+        w2s_raw = tables.tile([P, N], U8, name="w2s_raw", align_bytes=64)
+        nc.vector.memset(w2s_raw[:].bitcast(I32), 0)
         mu_rows = mu.rearrange("(p t) u -> p t u", t=PACK)
         rs_rows = rs.rearrange("(p t) u -> p t u", t=PACK)
         mu_win = [tables.tile([P, U], F32, name=f"mu_win{t}", align_bytes=64) for t in range(PACK)]
         rs_win = [tables.tile([P, U], F32, name=f"rs_win{t}", align_bytes=64) for t in range(PACK)]
+        w2w_raw = tables.tile([P, 2 * N], U8, name="w2w_raw", align_bytes=64)
         nc.sync.dma_start(out=w2w_raw[:].bitcast(I32), in_=w2_words[0].bitcast(I32))
         for pair in range(PACK // 2):
             for win, rows in ((mu_win, mu_rows), (rs_win, rs_rows)):
                 for t in (2 * pair, 2 * pair + 1):
                     nc.sync.dma_start(out=win[t][:], in_=rows[:, t, :])
+        for q in range(QUADS):
+            nc.sync.dma_start(
+                out=w2s_raw[32 * q : 32 * q + 4, :].bitcast(I32),
+                in_=w2_scales[0, 4 * q : 4 * q + 4, :].bitcast(I32),
+            )
 
         x_picked = [keep.tile([P, S], U32, name=f"x_picked{g}", align_bytes=64) for g in range(PASSES)]
+        nc.vector.tensor_copy(
+            out=w1w[:].rearrange("p (g t m b) -> p g t m b", g=PASSES, t=PACK, b=2),
+            in_=w1w_raw[:].rearrange("p (g m t b) -> p g t m b", g=PASSES, t=PACK, b=2),
+        )
         nc.vector.tensor_copy(out=x_picked[0][:], in_=x_win[0][:].bitcast(U32).indirect(offs_sb[:]))
         w1s = keep.tile([P, PASSES * H], U8, name="w1s", align_bytes=64)
         nc.vector.tensor_copy(
@@ -100,7 +105,7 @@ def tile_picked_clnorm_gelu_po_kernel(
         nc.vector.tensor_copy(out=x_picked[1][:], in_=x_win[1][:].bitcast(U32).indirect(offs_sb[:]))
 
         x_planes = (xs_picked, xs_second)
-        y_ps = [psum.tile([P, S], F32, name=f"y_ps{t}") for t in range(PACK)]
+        y_ps = [psum.tile([P, S], F32, name=f"y_ps{t}", tag=f"y_ps{t}") for t in range(PACK)]
         for g in range(PASSES):
             for t in range(PACK):
                 c0 = g * H + t * P
@@ -119,13 +124,8 @@ def tile_picked_clnorm_gelu_po_kernel(
             out=w2w[:].rearrange("p (t m b) -> p t m b", t=PACK, b=2),
             in_=w2w_raw[:].rearrange("p (m t b) -> p t m b", t=PACK, b=2),
         )
-        w2s = tables.tile([P, N], U8, name="w2s", tag="w2w_raw", align_bytes=64)
-        nc.vector.tensor_copy(
-            out=w2s[:].rearrange("p (t m) -> p t m", t=PACK),
-            in_=w2s_raw[:].rearrange("p (m t) -> p t m", t=PACK),
-        )
 
-        first = len(CHUNKS[0]) * UNIT
+        first = 2 * UNIT
         y_sb = [keep.tile([P, S], F32, name=f"y_sb{t}") for t in range(PACK)]
         for lo, hi in ((0, first), (first, S)):
             for t in range(PACK):
@@ -135,7 +135,7 @@ def tile_picked_clnorm_gelu_po_kernel(
         out_words = out_1[0].rearrange("p n t -> p (n t)").bitcast(I32)
         o_scales = keep.tile([P, S], U8, name="o_scales", align_bytes=64)
         z = {}
-        o_bf = {}
+        o_ps = {}
 
         def cols(u):
             return slice(u * UNIT, (u + 1) * UNIT)
@@ -155,14 +155,10 @@ def tile_picked_clnorm_gelu_po_kernel(
             z[u] = keep.tile([P, UNIT, PACK], BF16, name=f"z{u}", tag=f"z{u}", align_bytes=64)
             nc.scalar.activation(out=z[u][:], in_=normed.rearrange("p t j -> p j t"), func=ACT.Gelu_apprx_tanh, scale=-1.0)
 
-        def second_product(u):
-            z_words = keep.tile([P, UNIT], U32, name=f"z_words{u}", align_bytes=64)
-            z_scales = keep.tile([P, UNIT], U8, name=f"z_scales{u}", align_bytes=64)
-            nc.vector.quantize_mx(out=z_words[:].bitcast(FP8X4), scales=z_scales[:], in_=z[u][:].rearrange("p j t -> p (j t)"))
-            o_ps = psum.tile([P, PACK, UNIT], F32, name=f"o_ps{u}")
-            for t in range(PACK):
+        def multiply(bank, slots, w2s, z_words, z_scales):
+            for i, t in enumerate(slots):
                 nc.tensor.matmul_mx(
-                    out=o_ps[:, t, :],
+                    out=bank[:, i, :],
                     lhsT=w2w[:, 2 * t * P : 2 * (t + 1) * P].bitcast(FP4X4),
                     lhsT_scale=w2s[:, t * P : (t + 1) * P],
                     rhs=z_words[:].bitcast(FP8X4),
@@ -170,37 +166,60 @@ def tile_picked_clnorm_gelu_po_kernel(
                     start=True,
                     stop=True,
                 )
-            o_bf[u] = keep.tile([P, UNIT, PACK], BF16, name=f"o_bf{u}", tag=f"o_bf{u}", align_bytes=64)
-            nc.scalar.copy(out=o_bf[u][:], in_=o_ps[:].rearrange("p t j -> p j t"))
-            o_sb = keep.tile([P, PACK, UNIT], F32, name=f"o_sb{u}")
-            nc.scalar.copy(out=o_sb[:], in_=o_ps[:])
-            nc.sync.dma_start(out=out_rows[:, :, cols(u)], in_=o_sb[:])
 
-        def hand_on(u):
+        def second_product(u, w2s):
+            z_words = keep.tile([P, UNIT], U32, name=f"z_words{u}", align_bytes=64)
+            z_scales = keep.tile([P, UNIT], U8, name=f"z_scales{u}", align_bytes=64)
+            nc.vector.quantize_mx(out=z_words[:].bitcast(FP8X4), scales=z_scales[:], in_=z[u][:].rearrange("p j t -> p (j t)"))
+            o_bf = keep.tile([P, UNIT, PACK], BF16, name=f"o_bf{u}", align_bytes=64)
+            if u < S // UNIT - 1:
+                o_ps[u] = psum.tile([P, PACK, UNIT], F32, name=f"o_ps{u}")
+                multiply(o_ps[u], range(PACK), w2s, z_words, z_scales)
+                nc.scalar.copy(out=o_bf[:], in_=o_ps[u][:].rearrange("p t j -> p j t"))
+            else:
+                o_sb = keep.tile([P, PACK, UNIT], F32, name=f"o_sb{u}")
+                for half in range(2):
+                    bank = psum.tile([P, 2, UNIT], F32, name=f"o_last{half}", tag=f"y_ps{half}")
+                    multiply(bank, (2 * half, 2 * half + 1), w2s, z_words, z_scales)
+                    nc.scalar.copy(out=o_sb[:, 2 * half : 2 * half + 2, :], in_=bank[:])
+                nc.sync.dma_start(out=out_rows[:, :, cols(u)], in_=o_sb[:])
+                nc.vector.tensor_copy(out=o_bf[:], in_=o_sb[:].rearrange("p t j -> p j t"))
             o_words = keep.tile([P, UNIT], I32, name=f"o_words{u}", align_bytes=64)
             nc.vector.quantize_mx(
-                out=o_words[:].bitcast(FP8X4), scales=o_scales[:, cols(u)], in_=o_bf[u][:].rearrange("p j t -> p (j t)")
+                out=o_words[:].bitcast(FP8X4), scales=o_scales[:, cols(u)], in_=o_bf[:].rearrange("p j t -> p (j t)")
             )
             nc.sync.dma_start(out=out_words[:, cols(u)], in_=o_words[:])
 
-        for c in range(len(CHUNKS) + 2):
-            if c >= 2:
-                for u in CHUNKS[c - 2]:
-                    hand_on(u)
+        def store_result(u):
+            o_sb = keep.tile([P, PACK, UNIT], F32, name=f"o_sb{u}")
+            nc.scalar.copy(out=o_sb[:], in_=o_ps[u][:])
+            nc.sync.dma_start(out=out_rows[:, :, cols(u)], in_=o_sb[:])
+
+        held = "diff_b"
+        for c in range(len(CHUNKS) + 1):
+            before = CHUNKS[c - 1] if c > 0 else ()
             if c < len(CHUNKS):
                 chunk = CHUNKS[c]
-                slot = f"o_bf{CHUNKS[c - 2][0]}" if c >= 2 else f"normed{c}"
-                normed = keep.tile([P, PACK, len(chunk) * UNIT], F32, name=f"normed{c}", tag=slot, align_bytes=64)
-                normalise_pair(chunk, 0, normed, f"diff{c}")
-            if 1 <= c <= len(CHUNKS):
-                for u in CHUNKS[c - 1]:
-                    second_product(u)
+                normed = keep.tile([P, PACK, len(chunk) * UNIT], F32, name=f"normed{c}")
+                normalise_pair(chunk, 0, normed, "diff_a")
+            if c == 1:
+                w2s = keep.tile([P, N], U8, name="w2s", tag="diff_b", align_bytes=64)
+                nc.vector.tensor_copy(
+                    out=w2s[:].rearrange("p (t m) -> p t m", t=PACK),
+                    in_=w2s_raw[:].rearrange("p (m t) -> p t m", t=PACK),
+                )
+            for u in before:
+                second_product(u, w2s)
+                held = f"z{u}"
             if c < len(CHUNKS):
-                normalise_pair(chunk, 1, normed, f"z{chunk[0] - 1}")
+                normalise_pair(chunk, 1, normed, held)
                 for i, u in enumerate(chunk):
                     activate(u, normed[:, :, cols(i)])
+            for u in before:
+                if u in o_ps:
+                    store_result(u)
 
         for q in range(QUADS):
-            nc.scalar.dma_start(
+            (nc.scalar if q % 2 else nc.sync).dma_start(
                 out=out_2[0, 4 * q : 4 * q + 4, :].bitcast(I32), in_=o_scales[32 * q : 32 * q + 4, :].bitcast(I32)
             )

@@ -35,67 +35,60 @@ def tile_picked_clnorm_gelu_po_kernel(
         offs_sb = keep.tile([P, S // 16], U16, name="offs_sb")
         cl_sb = keep.tile([P, S // 16], U16, name="cl_sb")
         w1s_raw = keep.tile([P, PASSES * H], U8, name="w1s_raw", align_bytes=64)
-        w1w_raw = keep.tile([P, PASSES * 2 * H], U8, name="w1w_raw", align_bytes=64)
-        xs_second = keep.tile([P, S], U8, name="xs_second", align_bytes=64)
-        xs_picked = keep.tile([P, S], U8, name="xs_picked", align_bytes=64)
-        w1w = keep.tile([P, PASSES * 2 * H], U8, name="w1w", align_bytes=64)
+        w1w_raw = keep.tile([P, PASSES * 2 * H], U8, name="w1w_raw", tag="w1w_raw", align_bytes=64)
+        w2s_raw = keep.tile([P, N], U8, name="w2s_raw", align_bytes=64)
+        xs_win = keep.tile([P, PASSES * T], U8, name="xs_win", align_bytes=64)
         x_win = [keep.tile([P, T], I32, name=f"x_win{g}", tag=f"x_win{g}", align_bytes=64) for g in range(PASSES)]
 
-        with tc.tile_pool(name="head", bufs=1) as head:
-            xs_win = head.tile([P, T], U8, name="xs_win", align_bytes=64)
-            for plane in (xs_win, w1s_raw, xs_second):
-                nc.vector.memset(plane[:].bitcast(I32), 0)
+        for plane in (xs_win, w1s_raw, w2s_raw):
+            nc.vector.memset(plane[:].bitcast(I32), 0)
 
-            def load_x(g):
-                nc.sync.dma_start(out=x_win[g][:], in_=x_words[g].rearrange("p n t -> p (n t)").bitcast(I32))
+        def load_x(g):
+            nc.sync.dma_start(out=x_win[g][:], in_=x_words[g].rearrange("p n t -> p (n t)").bitcast(I32))
 
-            nc.sync.dma_start(offs_sb[:], offs)
-            nc.sync.dma_start(
-                out=w1w_raw[:].bitcast(I32).rearrange("p (g c) -> p g c", g=PASSES),
-                in_=w1_words.bitcast(I32).rearrange("g p c -> p g c"),
-            )
+        def load_scale_rows(plane, scales):
             for q in range(QUADS):
                 nc.sync.dma_start(
-                    out=xs_win[32 * q : 32 * q + 4 * PASSES, :].bitcast(I32),
-                    in_=x_scales[:, 4 * q : 4 * q + 4, :].bitcast(I32),
+                    out=plane[32 * q : 32 * q + 4, :].bitcast(I32).rearrange("r (g c) -> r g c", g=scales.shape[0]),
+                    in_=scales[:, 4 * q : 4 * q + 4, :].bitcast(I32).rearrange("g r c -> r g c"),
                 )
-            load_x(0)
-            for q in range(QUADS):
-                nc.sync.dma_start(
-                    out=w1s_raw[32 * q : 32 * q + 4, :].bitcast(I32).rearrange("r (g c) -> r g c", g=PASSES),
-                    in_=w1_scales[:, 4 * q : 4 * q + 4, :].bitcast(I32).rearrange("g r c -> r g c"),
-                )
-            load_x(1)
-            nc.sync.dma_start(cl_sb[:], cl)
-            nc.vector.tensor_copy(out=xs_picked[:], in_=xs_win[:].indirect(offs_sb[:]))
 
-        last = 32 * (QUADS - 1) + 4
-        nc.scalar.dma_start(out=xs_second[0:last, :].bitcast(I32), in_=xs_picked[4 : 4 + last, :].bitcast(I32))
-
-        tables = ctx.enter_context(tc.tile_pool(name="tables", bufs=1))
-        w2s_raw = tables.tile([P, N], U8, name="w2s_raw", align_bytes=64)
-        nc.vector.memset(w2s_raw[:].bitcast(I32), 0)
+        nc.sync.dma_start(offs_sb[:], offs)
+        nc.sync.dma_start(cl_sb[:], cl)
+        nc.sync.dma_start(
+            out=w1w_raw[:].bitcast(I32).rearrange("p (g c) -> p g c", g=PASSES),
+            in_=w1_words.bitcast(I32).rearrange("g p c -> p g c"),
+        )
+        load_scale_rows(xs_win, x_scales)
+        load_x(0)
+        load_scale_rows(w1s_raw, w1_scales)
+        load_x(1)
         mu_rows = mu.rearrange("(p t) u -> p t u", t=PACK)
         rs_rows = rs.rearrange("(p t) u -> p t u", t=PACK)
-        mu_win = [tables.tile([P, U], F32, name=f"mu_win{t}", align_bytes=64) for t in range(PACK)]
-        rs_win = [tables.tile([P, U], F32, name=f"rs_win{t}", align_bytes=64) for t in range(PACK)]
-        w2w_raw = tables.tile([P, 2 * N], U8, name="w2w_raw", align_bytes=64)
+        mu_win = [keep.tile([P, U], F32, name=f"mu_win{t}", align_bytes=64) for t in range(PACK)]
+        rs_win = [keep.tile([P, U], F32, name=f"rs_win{t}", align_bytes=64) for t in range(PACK)]
+        w2w_raw = keep.tile([P, 2 * N], U8, name="w2w_raw", align_bytes=64)
         nc.sync.dma_start(out=w2w_raw[:].bitcast(I32), in_=w2_words[0].bitcast(I32))
         for pair in range(PACK // 2):
             for win, rows in ((mu_win, mu_rows), (rs_win, rs_rows)):
                 for t in (2 * pair, 2 * pair + 1):
                     nc.sync.dma_start(out=win[t][:], in_=rows[:, t, :])
-        for q in range(QUADS):
-            nc.sync.dma_start(
-                out=w2s_raw[32 * q : 32 * q + 4, :].bitcast(I32),
-                in_=w2_scales[0, 4 * q : 4 * q + 4, :].bitcast(I32),
-            )
+        load_scale_rows(w2s_raw, w2_scales)
 
         x_picked = [keep.tile([P, S], U32, name=f"x_picked{g}", align_bytes=64) for g in range(PASSES)]
-        nc.vector.tensor_copy(
-            out=w1w[:].rearrange("p (g t m b) -> p g t m b", g=PASSES, t=PACK, b=2),
-            in_=w1w_raw[:].rearrange("p (g m t b) -> p g t m b", g=PASSES, t=PACK, b=2),
-        )
+        w1w = []
+
+        def deal_w1_words(pair, tag):
+            w1w.append(keep.tile([P, PASSES * H], U8, name=f"w1w{pair}", tag=tag, align_bytes=64))
+            nc.vector.tensor_copy(
+                out=w1w[pair][:].rearrange("p (g t m b) -> p g t m b", g=PASSES, t=2, b=2),
+                in_=w1w_raw[:].rearrange("p (g m t b) -> p g t m b", g=PASSES, t=PACK, b=2)[:, :, 2 * pair : 2 * pair + 2],
+            )
+
+        deal_w1_words(0, "w1w0")
+        x_planes = [keep.tile([P, S], U8, name=f"x_plane{g}", align_bytes=64) for g in range(PASSES)]
+        for g in range(PASSES):
+            nc.vector.tensor_copy(out=x_planes[g][:], in_=xs_win[:, g * T : (g + 1) * T].indirect(offs_sb[:]))
         nc.vector.tensor_copy(out=x_picked[0][:], in_=x_win[0][:].bitcast(U32).indirect(offs_sb[:]))
         w1s = keep.tile([P, PASSES * H], U8, name="w1s", align_bytes=64)
         nc.vector.tensor_copy(
@@ -104,22 +97,22 @@ def tile_picked_clnorm_gelu_po_kernel(
         )
         nc.vector.tensor_copy(out=x_picked[1][:], in_=x_win[1][:].bitcast(U32).indirect(offs_sb[:]))
 
-        x_planes = (xs_picked, xs_second)
-        y_ps = [psum.tile([P, S], F32, name=f"y_ps{t}", tag=f"y_ps{t}") for t in range(PACK)]
-        for g in range(PASSES):
-            for t in range(PACK):
-                c0 = g * H + t * P
-                nc.tensor.matmul_mx(
-                    out=y_ps[t][:],
-                    lhsT=w1w[:, 2 * c0 : 2 * (c0 + P)].bitcast(FP4X4),
-                    lhsT_scale=w1s[:, c0 : c0 + P],
-                    rhs=x_picked[g][:].bitcast(FP8X4),
-                    rhs_scale=x_planes[g][:],
-                    start=(g == 0),
-                    stop=(g == PASSES - 1),
-                )
+        deal_w1_words(1, f"x_win{PASSES - 1}")
 
-        w2w = keep.tile([P, 2 * N], U8, name="w2w", tag=f"x_win{PASSES - 1}", align_bytes=64)
+        y_ps = [psum.tile([P, S], F32, name=f"y_ps{t}", tag=f"y_ps{t}") for t in range(PACK)]
+        for g, t in [(g, t) for pair in ((0, 1), (2, 3)) for g in range(PASSES) for t in pair]:
+            c0 = g * H + t * P
+            nc.tensor.matmul_mx(
+                out=y_ps[t][:],
+                lhsT=w1w[t // 2][:, 2 * P * (2 * g + t % 2) : 2 * P * (2 * g + t % 2 + 1)].bitcast(FP4X4),
+                lhsT_scale=w1s[:, c0 : c0 + P],
+                rhs=x_picked[g][:].bitcast(FP8X4),
+                rhs_scale=x_planes[g][:],
+                start=(g == 0),
+                stop=(g == PASSES - 1),
+            )
+
+        w2w = keep.tile([P, 2 * N], U8, name="w2w", tag="w1w_raw", align_bytes=64)
         nc.vector.tensor_copy(
             out=w2w[:].rearrange("p (t m b) -> p t m b", t=PACK, b=2),
             in_=w2w_raw[:].rearrange("p (m t b) -> p t m b", t=PACK, b=2),

@@ -20,6 +20,7 @@ P = 128
 PACK = 4
 PASSES = K // (P * PACK)
 QUADS = 4
+LIST_ROWS = 16
 UNIT = 128
 CHUNKS = ((0, 1), (2,), (3,))
 
@@ -32,8 +33,8 @@ def tile_picked_clnorm_gelu_po_kernel(
         keep = ctx.enter_context(tc.tile_pool(name="keep", bufs=1))
         psum = ctx.enter_context(tc.psum_pool(name="psum", bufs=1))
 
-        offs_sb = keep.tile([P, S // 16], U16, name="offs_sb")
-        cl_sb = keep.tile([P, S // 16], U16, name="cl_sb")
+        offs_sb = keep.tile([P, S // LIST_ROWS], U16, name="offs_sb")
+        cl_sb = keep.tile([P, S // LIST_ROWS], U16, name="cl_sb")
         w1s_raw = keep.tile([P, PASSES * H], U8, name="w1s_raw", align_bytes=64)
         w1w_raw = keep.tile([P, PASSES * 2 * H], U8, name="w1w_raw", tag="w1w_raw", align_bytes=64)
         w2s_raw = keep.tile([P, N], U8, name="w2s_raw", align_bytes=64)
@@ -96,16 +97,16 @@ def tile_picked_clnorm_gelu_po_kernel(
             in_=w1s_raw[:].rearrange("p (g m t) -> p g t m", g=PASSES, t=PACK),
         )
         nc.vector.tensor_copy(out=x_picked[1][:], in_=x_win[1][:].bitcast(U32).indirect(offs_sb[:]))
-
         deal_w1_words(1, f"x_win{PASSES - 1}")
 
         y_ps = [psum.tile([P, S], F32, name=f"y_ps{t}", tag=f"y_ps{t}") for t in range(PACK)]
         for g, t in [(g, t) for pair in ((0, 1), (2, 3)) for g in range(PASSES) for t in pair]:
-            c0 = g * H + t * P
+            scale0 = g * H + t * P
+            word0 = 2 * P * (2 * g + t % 2)
             nc.tensor.matmul_mx(
                 out=y_ps[t][:],
-                lhsT=w1w[t // 2][:, 2 * P * (2 * g + t % 2) : 2 * P * (2 * g + t % 2 + 1)].bitcast(FP4X4),
-                lhsT_scale=w1s[:, c0 : c0 + P],
+                lhsT=w1w[t // 2][:, word0 : word0 + 2 * P].bitcast(FP4X4),
+                lhsT_scale=w1s[:, scale0 : scale0 + P],
                 rhs=x_picked[g][:].bitcast(FP8X4),
                 rhs_scale=x_planes[g][:],
                 start=(g == 0),
@@ -118,7 +119,7 @@ def tile_picked_clnorm_gelu_po_kernel(
             in_=w2w_raw[:].rearrange("p (m t b) -> p t m b", t=PACK, b=2),
         )
 
-        first = 2 * UNIT
+        first = len(CHUNKS[0]) * UNIT
         y_sb = [keep.tile([P, S], F32, name=f"y_sb{t}") for t in range(PACK)]
         for lo, hi in ((0, first), (first, S)):
             for t in range(PACK):
@@ -127,29 +128,30 @@ def tile_picked_clnorm_gelu_po_kernel(
         out_rows = out_0.rearrange("(p t) j -> p t j", t=PACK)
         out_words = out_1[0].rearrange("p n t -> p (n t)").bitcast(I32)
         o_scales = keep.tile([P, S], U8, name="o_scales", align_bytes=64)
+        last_unit = S // UNIT - 1
         z = {}
         o_ps = {}
 
         def cols(u):
             return slice(u * UNIT, (u + 1) * UNIT)
 
-        def normalise_pair(chunk, pair, normed, tag):
+        def normalise_pair(chunk, pair, normed, slots):
             lo, hi = chunk[0] * UNIT, (chunk[-1] + 1) * UNIT
-            lists = cl_sb[:, lo // 16 : hi // 16]
-            diff = keep.tile([P, 2, hi - lo], F32, name=f"diff{chunk[0]}_{pair}", tag=tag, align_bytes=64)
+            lists = cl_sb[:, lo // LIST_ROWS : hi // LIST_ROWS]
+            diff = [keep.tile([P, hi - lo], F32, name=f"diff{chunk[0]}_{pair}_{i}", tag=slots[i], align_bytes=64) for i in range(2)]
             for i in range(2):
                 t = 2 * pair + i
-                nc.vector.tensor_tensor(diff[:, i, :], mu_win[t][:].indirect(lists), y_sb[t][:, lo:hi], ALU.subtract)
+                nc.vector.tensor_tensor(diff[i][:], mu_win[t][:].indirect(lists), y_sb[t][:, lo:hi], ALU.subtract)
             for i in range(2):
                 t = 2 * pair + i
-                nc.vector.tensor_tensor(normed[:, t, :], rs_win[t][:].indirect(lists), diff[:, i, :], ALU.mult)
+                nc.vector.tensor_tensor(normed[:, t, :], rs_win[t][:].indirect(lists), diff[i][:], ALU.mult)
 
-        def activate(u, normed):
+        def activate(u, normed_unit):
             z[u] = keep.tile([P, UNIT, PACK], BF16, name=f"z{u}", tag=f"z{u}", align_bytes=64)
-            nc.scalar.activation(out=z[u][:], in_=normed.rearrange("p t j -> p j t"), func=ACT.Gelu_apprx_tanh, scale=-1.0)
+            nc.scalar.activation(out=z[u][:], in_=normed_unit.rearrange("p t j -> p j t"), func=ACT.Gelu_apprx_tanh, scale=-1.0)
 
-        def multiply(bank, slots, w2s, z_words, z_scales):
-            for i, t in enumerate(slots):
+        def multiply(bank, result_tiles, w2s, z_words, z_scales):
+            for i, t in enumerate(result_tiles):
                 nc.tensor.matmul_mx(
                     out=bank[:, i, :],
                     lhsT=w2w[:, 2 * t * P : 2 * (t + 1) * P].bitcast(FP4X4),
@@ -165,16 +167,16 @@ def tile_picked_clnorm_gelu_po_kernel(
             z_scales = keep.tile([P, UNIT], U8, name=f"z_scales{u}", align_bytes=64)
             nc.vector.quantize_mx(out=z_words[:].bitcast(FP8X4), scales=z_scales[:], in_=z[u][:].rearrange("p j t -> p (j t)"))
             o_bf = keep.tile([P, UNIT, PACK], BF16, name=f"o_bf{u}", align_bytes=64)
-            if u < S // UNIT - 1:
+            if u < last_unit:
                 o_ps[u] = psum.tile([P, PACK, UNIT], F32, name=f"o_ps{u}")
                 multiply(o_ps[u], range(PACK), w2s, z_words, z_scales)
                 nc.scalar.copy(out=o_bf[:], in_=o_ps[u][:].rearrange("p t j -> p j t"))
             else:
                 o_sb = keep.tile([P, PACK, UNIT], F32, name=f"o_sb{u}")
-                for half in range(2):
-                    bank = psum.tile([P, 2, UNIT], F32, name=f"o_last{half}", tag=f"y_ps{half}")
-                    multiply(bank, (2 * half, 2 * half + 1), w2s, z_words, z_scales)
-                    nc.scalar.copy(out=o_sb[:, 2 * half : 2 * half + 2, :], in_=bank[:])
+                for pair in range(PACK // 2):
+                    bank = psum.tile([P, 2, UNIT], F32, name=f"o_last{pair}", tag=f"y_ps{pair}")
+                    multiply(bank, (2 * pair, 2 * pair + 1), w2s, z_words, z_scales)
+                    nc.scalar.copy(out=o_sb[:, 2 * pair : 2 * pair + 2, :], in_=bank[:])
                 nc.sync.dma_start(out=out_rows[:, :, cols(u)], in_=o_sb[:])
                 nc.vector.tensor_copy(out=o_bf[:], in_=o_sb[:].rearrange("p t j -> p j t"))
             o_words = keep.tile([P, UNIT], I32, name=f"o_words{u}", align_bytes=64)
@@ -188,28 +190,28 @@ def tile_picked_clnorm_gelu_po_kernel(
             nc.scalar.copy(out=o_sb[:], in_=o_ps[u][:])
             nc.sync.dma_start(out=out_rows[:, :, cols(u)], in_=o_sb[:])
 
-        held = "diff_b"
+        slots = ["diff_even", "diff_odd"]
         for c in range(len(CHUNKS) + 1):
             before = CHUNKS[c - 1] if c > 0 else ()
             if c < len(CHUNKS):
                 chunk = CHUNKS[c]
                 normed = keep.tile([P, PACK, len(chunk) * UNIT], F32, name=f"normed{c}")
-                normalise_pair(chunk, 0, normed, "diff_a")
-            if c == 1:
-                w2s = keep.tile([P, N], U8, name="w2s", tag="diff_b", align_bytes=64)
+                normalise_pair(chunk, 0, normed, slots)
+            if before == CHUNKS[0]:
+                w2s = keep.tile([P, N], U8, name="w2s", tag="diff_even", align_bytes=64)
                 nc.vector.tensor_copy(
                     out=w2s[:].rearrange("p (t m) -> p t m", t=PACK),
                     in_=w2s_raw[:].rearrange("p (m t) -> p t m", t=PACK),
                 )
             for u in before:
                 second_product(u, w2s)
-                held = f"z{u}"
+                slots[before[-1] - u] = f"z{u}"
             if c < len(CHUNKS):
-                normalise_pair(chunk, 1, normed, held)
+                normalise_pair(chunk, 1, normed, slots)
                 for i, u in enumerate(chunk):
                     activate(u, normed[:, :, cols(i)])
             for u in before:
-                if u in o_ps:
+                if u < last_unit:
                     store_result(u)
 
         for q in range(QUADS):

@@ -1,6 +1,7 @@
 from contextlib import ExitStack
 
 import concourse.mybir as mybir
+from concourse.masks import make_identity
 
 F32 = mybir.dt.float32
 BF16 = mybir.dt.bfloat16
@@ -22,7 +23,6 @@ PASSES = K // (P * PACK)
 QUADS = 4
 LIST_ROWS = 16
 UNIT = 128
-CHUNKS = ((0, 1), (2,), (3,))
 
 
 def tile_picked_clnorm_gelu_po_kernel(
@@ -35,14 +35,21 @@ def tile_picked_clnorm_gelu_po_kernel(
 
         offs_sb = keep.tile([P, S // LIST_ROWS], U16, name="offs_sb")
         cl_sb = keep.tile([P, S // LIST_ROWS], U16, name="cl_sb")
+        xs_win = keep.tile([P, T], U8, name="xs_win", align_bytes=64)
         w1s_raw = keep.tile([P, PASSES * H], U8, name="w1s_raw", align_bytes=64)
-        w1w_raw = keep.tile([P, PASSES * 2 * H], U8, name="w1w_raw", tag="w1w_raw", align_bytes=64)
         w2s_raw = keep.tile([P, N], U8, name="w2s_raw", align_bytes=64)
-        xs_win = keep.tile([P, PASSES * T], U8, name="xs_win", align_bytes=64)
-        x_win = [keep.tile([P, T], I32, name=f"x_win{g}", tag=f"x_win{g}", align_bytes=64) for g in range(PASSES)]
+        x_planes = [keep.tile([P, S], U8, name=f"x_plane{g}", align_bytes=64) for g in range(PASSES)]
+        w1w_raw = keep.tile([P, PASSES * 2 * H], U8, name="w1w_raw", align_bytes=64)
+        w2w_raw = keep.tile([P, 2 * N], U8, name="w2w_raw", align_bytes=64)
+        x_win = [keep.tile([P, T], I32, name=f"x_win{g}", align_bytes=64) for g in range(PASSES)]
+        mu_win = [keep.tile([P, 2 * U], F32, name=f"mu_win{t}", align_bytes=64) for t in range(PACK)]
+        rs_win = [keep.tile([P, U], F32, name=f"rs_win{t}", align_bytes=64) for t in range(PACK)]
 
-        for plane in (xs_win, w1s_raw, w2s_raw):
+        for plane in (xs_win, w1s_raw, w2s_raw, x_planes[1]):
             nc.vector.memset(plane[:].bitcast(I32), 0)
+
+        for t in range(PACK):
+            nc.gpsimd.memset(mu_win[t][:, U:], 0.0)
 
         def load_x(g):
             nc.sync.dma_start(out=x_win[g][:], in_=x_words[g].rearrange("p n t -> p (n t)").bitcast(I32))
@@ -54,103 +61,105 @@ def tile_picked_clnorm_gelu_po_kernel(
                     in_=scales[:, 4 * q : 4 * q + 4, :].bitcast(I32).rearrange("g r c -> r g c"),
                 )
 
-        nc.sync.dma_start(offs_sb[:], offs)
+        mu_rows = mu.rearrange("(p t) u -> p t u", t=PACK)
+        rs_rows = rs.rearrange("(p t) u -> p t u", t=PACK)
+
+        def load_table(win, rows, t):
+            nc.sync.dma_start(out=win[t][:, :U], in_=rows[:, t, :])
+
         nc.sync.dma_start(cl_sb[:], cl)
+        load_table(mu_win, mu_rows, 0)
+        load_table(mu_win, mu_rows, 1)
+        nc.sync.dma_start(offs_sb[:], offs)
+        for r in range(4):
+            nc.sync.dma_start(
+                out=xs_win[r:P:16, :].bitcast(I32),
+                in_=x_scales[:, r:16:4, :].bitcast(I32).rearrange("g q c -> q g c"),
+            )
+        load_x(0)
+        load_x(1)
         nc.sync.dma_start(
             out=w1w_raw[:].bitcast(I32).rearrange("p (g c) -> p g c", g=PASSES),
             in_=w1_words.bitcast(I32).rearrange("g p c -> p g c"),
         )
-        load_scale_rows(xs_win, x_scales)
-        load_x(0)
         load_scale_rows(w1s_raw, w1_scales)
-        load_x(1)
-        mu_rows = mu.rearrange("(p t) u -> p t u", t=PACK)
-        rs_rows = rs.rearrange("(p t) u -> p t u", t=PACK)
-        mu_win = [keep.tile([P, U], F32, name=f"mu_win{t}", align_bytes=64) for t in range(PACK)]
-        rs_win = [keep.tile([P, U], F32, name=f"rs_win{t}", align_bytes=64) for t in range(PACK)]
-        w2w_raw = keep.tile([P, 2 * N], U8, name="w2w_raw", align_bytes=64)
+        load_table(mu_win, mu_rows, 2)
+        load_table(mu_win, mu_rows, 3)
         nc.sync.dma_start(out=w2w_raw[:].bitcast(I32), in_=w2_words[0].bitcast(I32))
-        for pair in range(PACK // 2):
-            for win, rows in ((mu_win, mu_rows), (rs_win, rs_rows)):
-                for t in (2 * pair, 2 * pair + 1):
-                    nc.sync.dma_start(out=win[t][:], in_=rows[:, t, :])
+        for t in range(PACK):
+            load_table(rs_win, rs_rows, t)
         load_scale_rows(w2s_raw, w2_scales)
 
+        mu_picked = keep.tile([P, PACK, S], F32, name="mu_picked", align_bytes=64)
+
+        def pick_mu(t):
+            nc.vector.tensor_copy(out=mu_picked[:, t, :], in_=mu_win[t][:].indirect(cl_sb[:]))
+
         x_picked = [keep.tile([P, S], U32, name=f"x_picked{g}", align_bytes=64) for g in range(PASSES)]
-        w1w = []
 
-        def deal_w1_words(pair, tag):
-            w1w.append(keep.tile([P, PASSES * H], U8, name=f"w1w{pair}", tag=tag, align_bytes=64))
-            nc.vector.tensor_copy(
-                out=w1w[pair][:].rearrange("p (g t m b) -> p g t m b", g=PASSES, t=2, b=2),
-                in_=w1w_raw[:].rearrange("p (g m t b) -> p g t m b", g=PASSES, t=PACK, b=2)[:, :, 2 * pair : 2 * pair + 2],
-            )
+        def pick_x(g):
+            nc.vector.tensor_copy(out=x_picked[g][:], in_=x_win[g][:].bitcast(U32).indirect(offs_sb[:]))
 
-        deal_w1_words(0, "w1w0")
-        x_planes = [keep.tile([P, S], U8, name=f"x_plane{g}", align_bytes=64) for g in range(PASSES)]
-        for g in range(PASSES):
-            nc.vector.tensor_copy(out=x_planes[g][:], in_=xs_win[:, g * T : (g + 1) * T].indirect(offs_sb[:]))
-        nc.vector.tensor_copy(out=x_picked[0][:], in_=x_win[0][:].bitcast(U32).indirect(offs_sb[:]))
-        w1s = keep.tile([P, PASSES * H], U8, name="w1s", align_bytes=64)
-        nc.vector.tensor_copy(
-            out=w1s[:].rearrange("p (g t m) -> p g t m", g=PASSES, t=PACK),
-            in_=w1s_raw[:].rearrange("p (g m t) -> p g t m", g=PASSES, t=PACK),
-        )
-        nc.vector.tensor_copy(out=x_picked[1][:], in_=x_win[1][:].bitcast(U32).indirect(offs_sb[:]))
-        deal_w1_words(1, f"x_win{PASSES - 1}")
-
-        y_ps = [psum.tile([P, S], F32, name=f"y_ps{t}", tag=f"y_ps{t}") for t in range(PACK)]
-        for g, t in [(g, t) for pair in ((0, 1), (2, 3)) for g in range(PASSES) for t in pair]:
-            scale0 = g * H + t * P
-            word0 = 2 * P * (2 * g + t % 2)
-            nc.tensor.matmul_mx(
-                out=y_ps[t][:],
-                lhsT=w1w[t // 2][:, word0 : word0 + 2 * P].bitcast(FP4X4),
-                lhsT_scale=w1s[:, scale0 : scale0 + P],
-                rhs=x_picked[g][:].bitcast(FP8X4),
-                rhs_scale=x_planes[g][:],
-                start=(g == 0),
-                stop=(g == PASSES - 1),
-            )
-
-        w2w = keep.tile([P, 2 * N], U8, name="w2w", tag="w1w_raw", align_bytes=64)
+        pick_mu(0)
+        pick_mu(1)
+        nc.vector.tensor_copy(out=x_planes[0][:], in_=xs_win[:].indirect(offs_sb[:]))
+        nc.scalar.dma_start(out=x_planes[1][0 : P - 16, :].bitcast(I32), in_=x_planes[0][16:P, :].bitcast(I32))
+        pick_x(0)
+        pick_x(1)
+        pick_mu(2)
+        pick_mu(3)
+        w2w = keep.tile([P, 2 * N], U8, name="w2w", align_bytes=64)
         nc.vector.tensor_copy(
             out=w2w[:].rearrange("p (t m b) -> p t m b", t=PACK, b=2),
             in_=w2w_raw[:].rearrange("p (m t b) -> p t m b", t=PACK, b=2),
         )
-
-        first = len(CHUNKS[0]) * UNIT
-        y_sb = [keep.tile([P, S], F32, name=f"y_sb{t}") for t in range(PACK)]
-        for lo, hi in ((0, first), (first, S)):
-            for t in range(PACK):
-                nc.scalar.copy(out=y_sb[t][:, lo:hi], in_=y_ps[t][:, lo:hi])
-
-        out_rows = out_0.rearrange("(p t) j -> p t j", t=PACK)
-        out_words = out_1[0].rearrange("p n t -> p (n t)").bitcast(I32)
-        o_scales = keep.tile([P, S], U8, name="o_scales", align_bytes=64)
-        last_unit = S // UNIT - 1
-        z = {}
-        o_ps = {}
+        w2s = keep.tile([P, N], U8, name="w2s", align_bytes=64)
 
         def cols(u):
             return slice(u * UNIT, (u + 1) * UNIT)
 
-        def normalise_pair(chunk, pair, normed, slots):
-            lo, hi = chunk[0] * UNIT, (chunk[-1] + 1) * UNIT
-            lists = cl_sb[:, lo // LIST_ROWS : hi // LIST_ROWS]
-            diff = [keep.tile([P, hi - lo], F32, name=f"diff{chunk[0]}_{pair}_{i}", tag=slots[i], align_bytes=64) for i in range(2)]
-            for i in range(2):
-                t = 2 * pair + i
-                nc.vector.tensor_tensor(diff[i][:], mu_win[t][:].indirect(lists), y_sb[t][:, lo:hi], ALU.subtract)
-            for i in range(2):
-                t = 2 * pair + i
-                nc.vector.tensor_tensor(normed[:, t, :], rs_win[t][:].indirect(lists), diff[i][:], ALU.mult)
+        units = S // UNIT
+        ident = keep.tile([P, P], F32, name="ident", align_bytes=64)
+        make_identity(nc, ident[:])
+        y_ps = []
+        for u in range(units):
+            turned = psum.tile([P, H], F32, name=f"turned{u}", tag=f"y_ps{u}")
+            for g in range(PASSES):
+                nc.tensor.matmul_mx(
+                    out=turned[:],
+                    lhsT=x_picked[g][:, cols(u)].bitcast(FP8X4),
+                    lhsT_scale=x_planes[g][:, cols(u)],
+                    rhs=w1w_raw[:, 2 * g * H : 2 * (g + 1) * H].bitcast(FP4X4),
+                    rhs_scale=w1s_raw[:, g * H : (g + 1) * H],
+                    start=(g == 0),
+                    stop=(g == PASSES - 1),
+                )
+            dealt = keep.tile([P, PACK, P], F32, name=f"dealt{u}", align_bytes=64)
+            nc.scalar.copy(out=dealt[:], in_=turned[:].rearrange("j (m t) -> j t m", t=PACK))
+            y_ps.append(psum.tile([P, PACK, UNIT], F32, name=f"y_ps{u}", tag=f"y_ps{u}"))
+            for t in range(PACK):
+                nc.tensor.transpose(y_ps[u][:, t, :], dealt[:, t, :], ident[:])
 
-        def activate(u, normed_unit):
-            z[u] = keep.tile([P, UNIT, PACK], BF16, name=f"z{u}", tag=f"z{u}", align_bytes=64)
-            nc.scalar.activation(out=z[u][:], in_=normed_unit.rearrange("p t j -> p j t"), func=ACT.Gelu_apprx_tanh, scale=-1.0)
+        out_rows = out_0.rearrange("(p t) j -> p t j", t=PACK)
+        out_words = out_1[0].rearrange("p n t -> p (n t)").bitcast(I32)
+        o_scales = keep.tile([P, S], U8, name="o_scales", align_bytes=64)
+        last_unit = units - 1
+        z = {}
+        o_ps = {}
 
-        def multiply(bank, result_tiles, w2s, z_words, z_scales):
+        def normalise(u):
+            diff = keep.tile([P, PACK, UNIT], F32, name=f"diff{u}", tag="diff" if u < 2 else f"normed{u - 2}", align_bytes=64)
+            for pair in range(PACK // 2):
+                ts = slice(2 * pair, 2 * pair + 2)
+                nc.vector.tensor_tensor(diff[:, ts, :], mu_picked[:, ts, cols(u)], y_ps[u][:, ts, :], ALU.subtract)
+            normed = keep.tile([P, PACK, UNIT], F32, name=f"normed{u}", tag=f"normed{u}", align_bytes=64)
+            lists = cl_sb[:, u * UNIT // LIST_ROWS : (u + 1) * UNIT // LIST_ROWS]
+            for t in range(PACK):
+                nc.vector.tensor_tensor(normed[:, t, :], rs_win[t][:].indirect(lists), diff[:, t, :], ALU.mult)
+            z[u] = keep.tile([P, UNIT, PACK], BF16, name=f"z{u}", align_bytes=64)
+            nc.scalar.activation(out=z[u][:], in_=normed[:].rearrange("p t j -> p j t"), func=ACT.Gelu_apprx_tanh, scale=-1.0)
+
+        def multiply(bank, result_tiles, z_words, z_scales):
             for i, t in enumerate(result_tiles):
                 nc.tensor.matmul_mx(
                     out=bank[:, i, :],
@@ -162,20 +171,20 @@ def tile_picked_clnorm_gelu_po_kernel(
                     stop=True,
                 )
 
-        def second_product(u, w2s):
+        def second_product(u):
             z_words = keep.tile([P, UNIT], U32, name=f"z_words{u}", align_bytes=64)
             z_scales = keep.tile([P, UNIT], U8, name=f"z_scales{u}", align_bytes=64)
             nc.vector.quantize_mx(out=z_words[:].bitcast(FP8X4), scales=z_scales[:], in_=z[u][:].rearrange("p j t -> p (j t)"))
             o_bf = keep.tile([P, UNIT, PACK], BF16, name=f"o_bf{u}", align_bytes=64)
             if u < last_unit:
                 o_ps[u] = psum.tile([P, PACK, UNIT], F32, name=f"o_ps{u}")
-                multiply(o_ps[u], range(PACK), w2s, z_words, z_scales)
+                multiply(o_ps[u], range(PACK), z_words, z_scales)
                 nc.scalar.copy(out=o_bf[:], in_=o_ps[u][:].rearrange("p t j -> p j t"))
             else:
                 o_sb = keep.tile([P, PACK, UNIT], F32, name=f"o_sb{u}")
                 for pair in range(PACK // 2):
                     bank = psum.tile([P, 2, UNIT], F32, name=f"o_last{pair}", tag=f"y_ps{pair}")
-                    multiply(bank, (2 * pair, 2 * pair + 1), w2s, z_words, z_scales)
+                    multiply(bank, (2 * pair, 2 * pair + 1), z_words, z_scales)
                     nc.scalar.copy(out=o_sb[:, 2 * pair : 2 * pair + 2, :], in_=bank[:])
                 nc.sync.dma_start(out=out_rows[:, :, cols(u)], in_=o_sb[:])
                 nc.vector.tensor_copy(out=o_bf[:], in_=o_sb[:].rearrange("p t j -> p j t"))
@@ -187,32 +196,24 @@ def tile_picked_clnorm_gelu_po_kernel(
 
         def store_result(u):
             o_sb = keep.tile([P, PACK, UNIT], F32, name=f"o_sb{u}")
-            nc.scalar.copy(out=o_sb[:], in_=o_ps[u][:])
+            if u == last_unit - 1:
+                nc.vector.tensor_copy(out=o_sb[:], in_=o_ps[u][:])
+            else:
+                nc.scalar.copy(out=o_sb[:], in_=o_ps[u][:])
             nc.sync.dma_start(out=out_rows[:, :, cols(u)], in_=o_sb[:])
 
-        slots = ["diff_even", "diff_odd"]
-        for c in range(len(CHUNKS) + 1):
-            before = CHUNKS[c - 1] if c > 0 else ()
-            if c < len(CHUNKS):
-                chunk = CHUNKS[c]
-                normed = keep.tile([P, PACK, len(chunk) * UNIT], F32, name=f"normed{c}")
-                normalise_pair(chunk, 0, normed, slots)
-            if before == CHUNKS[0]:
-                w2s = keep.tile([P, N], U8, name="w2s", tag="diff_even", align_bytes=64)
+        for u in range(units + 1):
+            if u < units:
+                normalise(u)
+            if u == 0:
                 nc.vector.tensor_copy(
                     out=w2s[:].rearrange("p (t m) -> p t m", t=PACK),
                     in_=w2s_raw[:].rearrange("p (m t) -> p t m", t=PACK),
                 )
-            for u in before:
-                second_product(u, w2s)
-                slots[before[-1] - u] = f"z{u}"
-            if c < len(CHUNKS):
-                normalise_pair(chunk, 1, normed, slots)
-                for i, u in enumerate(chunk):
-                    activate(u, normed[:, :, cols(i)])
-            for u in before:
-                if u < last_unit:
-                    store_result(u)
+            else:
+                second_product(u - 1)
+                if u - 1 < last_unit:
+                    store_result(u - 1)
 
         for q in range(QUADS):
             (nc.scalar if q % 2 else nc.sync).dma_start(

@@ -23,6 +23,7 @@ PASSES = K // (P * PACK)
 QUADS = 4
 LIST_ROWS = 16
 UNIT = 128
+HALF = S // 2
 
 
 def tile_picked_clnorm_gelu_po_kernel(
@@ -35,21 +36,19 @@ def tile_picked_clnorm_gelu_po_kernel(
 
         offs_sb = keep.tile([P, S // LIST_ROWS], U16, name="offs_sb")
         cl_sb = keep.tile([P, S // LIST_ROWS], U16, name="cl_sb")
-        xs_win = keep.tile([P, T], U8, name="xs_win", align_bytes=64)
+        xs_win = keep.tile([P, PASSES * T], U8, name="xs_win", align_bytes=64)
         w1s_raw = keep.tile([P, PASSES * H], U8, name="w1s_raw", align_bytes=64)
         w2s_raw = keep.tile([P, N], U8, name="w2s_raw", align_bytes=64)
         x_planes = [keep.tile([P, S], U8, name=f"x_plane{g}", align_bytes=64) for g in range(PASSES)]
         w1w_raw = keep.tile([P, PASSES * 2 * H], U8, name="w1w_raw", align_bytes=64)
         w2w_raw = keep.tile([P, 2 * N], U8, name="w2w_raw", align_bytes=64)
         x_win = [keep.tile([P, T], I32, name=f"x_win{g}", align_bytes=64) for g in range(PASSES)]
-        mu_win = [keep.tile([P, 2 * U], F32, name=f"mu_win{t}", align_bytes=64) for t in range(PACK)]
+        mu_win = [keep.tile([P, U], F32, name=f"mu_win{t}", align_bytes=64) for t in range(PACK)]
         rs_win = [keep.tile([P, U], F32, name=f"rs_win{t}", align_bytes=64) for t in range(PACK)]
 
-        for plane in (xs_win, w1s_raw, w2s_raw, x_planes[1]):
+        nc.vector.memset(xs_win[:].bitcast(I32), 0)
+        for plane in (w1s_raw, w2s_raw):
             nc.vector.memset(plane[:].bitcast(I32), 0)
-
-        for t in range(PACK):
-            nc.gpsimd.memset(mu_win[t][:, U:], 0.0)
 
         def load_x(g):
             nc.sync.dma_start(out=x_win[g][:], in_=x_words[g].rearrange("p n t -> p (n t)").bitcast(I32))
@@ -65,17 +64,13 @@ def tile_picked_clnorm_gelu_po_kernel(
         rs_rows = rs.rearrange("(p t) u -> p t u", t=PACK)
 
         def load_table(win, rows, t):
-            nc.sync.dma_start(out=win[t][:, :U], in_=rows[:, t, :])
+            nc.sync.dma_start(out=win[t][:], in_=rows[:, t, :])
 
         nc.sync.dma_start(cl_sb[:], cl)
         load_table(mu_win, mu_rows, 0)
         load_table(mu_win, mu_rows, 1)
         nc.sync.dma_start(offs_sb[:], offs)
-        for r in range(4):
-            nc.sync.dma_start(
-                out=xs_win[r:P:16, :].bitcast(I32),
-                in_=x_scales[:, r:16:4, :].bitcast(I32).rearrange("g q c -> q g c"),
-            )
+        load_scale_rows(xs_win, x_scales)
         load_x(0)
         load_x(1)
         nc.sync.dma_start(
@@ -93,7 +88,9 @@ def tile_picked_clnorm_gelu_po_kernel(
         mu_picked = keep.tile([P, PACK, S], F32, name="mu_picked", align_bytes=64)
 
         def pick_mu(t):
-            nc.vector.tensor_copy(out=mu_picked[:, t, :], in_=mu_win[t][:].indirect(cl_sb[:]))
+            for lo in range(0, S, HALF):
+                lists = cl_sb[:, lo // LIST_ROWS : (lo + HALF) // LIST_ROWS]
+                nc.vector.tensor_copy(out=mu_picked[:, t, lo : lo + HALF], in_=mu_win[t][:].indirect(lists))
 
         x_picked = [keep.tile([P, S], U32, name=f"x_picked{g}", align_bytes=64) for g in range(PASSES)]
 
@@ -102,8 +99,8 @@ def tile_picked_clnorm_gelu_po_kernel(
 
         pick_mu(0)
         pick_mu(1)
-        nc.vector.tensor_copy(out=x_planes[0][:], in_=xs_win[:].indirect(offs_sb[:]))
-        nc.scalar.dma_start(out=x_planes[1][0 : P - 16, :].bitcast(I32), in_=x_planes[0][16:P, :].bitcast(I32))
+        for g in range(PASSES):
+            nc.vector.tensor_copy(out=x_planes[g][:], in_=xs_win[:, g * T : (g + 1) * T].indirect(offs_sb[:]))
         pick_x(0)
         pick_x(1)
         pick_mu(2)

@@ -44,7 +44,7 @@ def tile_picked_clnorm_gelu_po_kernel(
         w2w_raw = keep.tile([P, 2 * N], U8, name="w2w_raw", align_bytes=64)
         x_win = [keep.tile([P, T], I32, name=f"x_win{g}", align_bytes=64) for g in range(PASSES)]
         mu_win = [keep.tile([P, U], F32, name=f"mu_win{t}", align_bytes=64) for t in range(PACK)]
-        rs_win = [keep.tile([P, U], F32, name=f"rs_win{t}", align_bytes=64) for t in range(PACK)]
+        rs_win = [keep.tile([P, U], F32, name=f"rs_win{t}", tag=f"rs_win{t}", align_bytes=64) for t in range(PACK)]
 
         nc.vector.memset(xs_win[:].bitcast(I32), 0)
         for plane in (w1s_raw, w2s_raw):
@@ -80,9 +80,9 @@ def tile_picked_clnorm_gelu_po_kernel(
         load_scale_rows(w1s_raw, w1_scales)
         load_table(mu_win, mu_rows, 2)
         load_table(mu_win, mu_rows, 3)
-        nc.sync.dma_start(out=w2w_raw[:].bitcast(I32), in_=w2_words[0].bitcast(I32))
         for t in range(PACK):
             load_table(rs_win, rs_rows, t)
+        nc.sync.dma_start(out=w2w_raw[:].bitcast(I32), in_=w2_words[0].bitcast(I32))
         load_scale_rows(w2s_raw, w2_scales)
 
         mu_picked = keep.tile([P, PACK, S], F32, name="mu_picked", align_bytes=64)
@@ -95,7 +95,10 @@ def tile_picked_clnorm_gelu_po_kernel(
         x_picked = [keep.tile([P, S], U32, name=f"x_picked{g}", align_bytes=64) for g in range(PASSES)]
 
         def pick_x(g):
-            nc.vector.tensor_copy(out=x_picked[g][:], in_=x_win[g][:].bitcast(U32).indirect(offs_sb[:]))
+            step = HALF if g == PASSES - 1 else S
+            for lo in range(0, S, step):
+                lists = offs_sb[:, lo // LIST_ROWS : (lo + step) // LIST_ROWS]
+                nc.vector.tensor_copy(out=x_picked[g][:, lo : lo + step], in_=x_win[g][:].bitcast(U32).indirect(lists))
 
         pick_mu(0)
         pick_mu(1)
@@ -106,10 +109,6 @@ def tile_picked_clnorm_gelu_po_kernel(
         pick_mu(2)
         pick_mu(3)
         w2w = keep.tile([P, 2 * N], U8, name="w2w", align_bytes=64)
-        nc.vector.tensor_copy(
-            out=w2w[:].rearrange("p (t m b) -> p t m b", t=PACK, b=2),
-            in_=w2w_raw[:].rearrange("p (m t b) -> p t m b", t=PACK, b=2),
-        )
         w2s = keep.tile([P, N], U8, name="w2s", align_bytes=64)
 
         def cols(u):
@@ -120,7 +119,7 @@ def tile_picked_clnorm_gelu_po_kernel(
         make_identity(nc, ident[:])
         y_ps = []
         for u in range(units):
-            turned = psum.tile([P, H], F32, name=f"turned{u}", tag=f"y_ps{u}")
+            turned = psum.tile([P, H], F32, name=f"turned{u}", tag=f"turned{u % 2}")
             for g in range(PASSES):
                 nc.tensor.matmul_mx(
                     out=turned[:],
@@ -174,18 +173,18 @@ def tile_picked_clnorm_gelu_po_kernel(
             nc.vector.quantize_mx(out=z_words[:].bitcast(FP8X4), scales=z_scales[:], in_=z[u][:].rearrange("p j t -> p (j t)"))
             o_bf = keep.tile([P, UNIT, PACK], BF16, name=f"o_bf{u}", align_bytes=64)
             if u < last_unit:
-                o_ps[u] = psum.tile([P, PACK, UNIT], F32, name=f"o_ps{u}")
+                o_ps[u] = psum.tile([P, PACK, UNIT], F32, name=f"o_ps{u}", tag=f"y_ps{u}")
                 multiply(o_ps[u], range(PACK), z_words, z_scales)
                 nc.scalar.copy(out=o_bf[:], in_=o_ps[u][:].rearrange("p t j -> p j t"))
             else:
                 o_sb = keep.tile([P, PACK, UNIT], F32, name=f"o_sb{u}")
                 for pair in range(PACK // 2):
-                    bank = psum.tile([P, 2, UNIT], F32, name=f"o_last{pair}", tag=f"y_ps{pair}")
+                    bank = psum.tile([P, 2, UNIT], F32, name=f"o_last{pair}", tag=f"turned{pair}")
                     multiply(bank, (2 * pair, 2 * pair + 1), z_words, z_scales)
                     nc.scalar.copy(out=o_sb[:, 2 * pair : 2 * pair + 2, :], in_=bank[:])
-                nc.sync.dma_start(out=out_rows[:, :, cols(u)], in_=o_sb[:])
+                    nc.sync.dma_start(out=out_rows[:, 2 * pair : 2 * pair + 2, cols(u)], in_=o_sb[:, 2 * pair : 2 * pair + 2, :])
                 nc.vector.tensor_copy(out=o_bf[:], in_=o_sb[:].rearrange("p t j -> p j t"))
-            o_words = keep.tile([P, UNIT], I32, name=f"o_words{u}", align_bytes=64)
+            o_words = keep.tile([P, UNIT], I32, name=f"o_words{u}", tag=f"rs_win{u + 2}" if u < 2 else f"o_words{u}", align_bytes=64)
             nc.vector.quantize_mx(
                 out=o_words[:].bitcast(FP8X4), scales=o_scales[:, cols(u)], in_=o_bf[:].rearrange("p j t -> p (j t)")
             )
@@ -203,6 +202,10 @@ def tile_picked_clnorm_gelu_po_kernel(
             if u < units:
                 normalise(u)
             if u == 0:
+                nc.vector.tensor_copy(
+                    out=w2w[:].bitcast(U16).rearrange("p (t m) -> p t m", t=PACK),
+                    in_=w2w_raw[:].bitcast(U16).rearrange("p (m t) -> p t m", t=PACK),
+                )
                 nc.vector.tensor_copy(
                     out=w2s[:].rearrange("p (t m) -> p t m", t=PACK),
                     in_=w2s_raw[:].rearrange("p (m t) -> p t m", t=PACK),

@@ -38,7 +38,7 @@ def tile_picked_clnorm_gelu_po_kernel(
         cl_sb = keep.tile([P, S // LIST_ROWS], U16, name="cl_sb")
         xs_win = keep.tile([P, PASSES * T], U8, name="xs_win", align_bytes=64)
         w1s_raw = keep.tile([P, PASSES * H], U8, name="w1s_raw", align_bytes=64)
-        w2s_raw = keep.tile([P, N], U8, name="w2s_raw", align_bytes=64)
+        w2s_raw = keep.tile([P, N], U8, name="w2s_raw", tag="w2s_raw", align_bytes=64)
         x_planes = [keep.tile([P, S], U8, name=f"x_plane{g}", align_bytes=64) for g in range(PASSES)]
         w1w_raw = keep.tile([P, PASSES * 2 * H], U8, name="w1w_raw", align_bytes=64)
         w2w_raw = keep.tile([P, 2 * N], U8, name="w2w_raw", align_bytes=64)
@@ -49,6 +49,12 @@ def tile_picked_clnorm_gelu_po_kernel(
         nc.vector.memset(xs_win[:].bitcast(I32), 0)
         for plane in (w1s_raw, w2s_raw):
             nc.vector.memset(plane[:].bitcast(I32), 0)
+
+        ident = keep.tile([P, P], F32, name="ident", align_bytes=64)
+        make_identity(nc, ident[:])
+        warm = keep.tile([P, 2], F32, name="warm")
+        nc.vector.memset(warm[:, 0:1], 0.0)
+        nc.scalar.activation(out=warm[:, 1:2], in_=warm[:, 0:1], func=ACT.Gelu_apprx_tanh)
 
         def load_x(g):
             nc.sync.dma_start(out=x_win[g][:], in_=x_words[g].rearrange("p n t -> p (n t)").bitcast(I32))
@@ -80,10 +86,10 @@ def tile_picked_clnorm_gelu_po_kernel(
         load_scale_rows(w1s_raw, w1_scales)
         load_table(mu_win, mu_rows, 2)
         load_table(mu_win, mu_rows, 3)
-        for t in range(PACK):
-            load_table(rs_win, rs_rows, t)
         nc.sync.dma_start(out=w2w_raw[:].bitcast(I32), in_=w2_words[0].bitcast(I32))
         load_scale_rows(w2s_raw, w2_scales)
+        for t in range(PACK):
+            load_table(rs_win, rs_rows, t)
 
         mu_picked = keep.tile([P, PACK, S], F32, name="mu_picked", align_bytes=64)
 
@@ -109,14 +115,20 @@ def tile_picked_clnorm_gelu_po_kernel(
         pick_mu(2)
         pick_mu(3)
         w2w = keep.tile([P, 2 * N], U8, name="w2w", align_bytes=64)
+        nc.vector.tensor_copy(
+            out=w2w[:].bitcast(U16).rearrange("p (t m) -> p t m", t=PACK),
+            in_=w2w_raw[:].bitcast(U16).rearrange("p (m t) -> p t m", t=PACK),
+        )
         w2s = keep.tile([P, N], U8, name="w2s", align_bytes=64)
+        nc.vector.tensor_copy(
+            out=w2s[:].rearrange("p (t m) -> p t m", t=PACK),
+            in_=w2s_raw[:].rearrange("p (m t) -> p t m", t=PACK),
+        )
 
         def cols(u):
             return slice(u * UNIT, (u + 1) * UNIT)
 
         units = S // UNIT
-        ident = keep.tile([P, P], F32, name="ident", align_bytes=64)
-        make_identity(nc, ident[:])
         y_ps = []
         for u in range(units):
             turned = psum.tile([P, H], F32, name=f"turned{u}", tag=f"turned{u % 2}")
@@ -130,7 +142,7 @@ def tile_picked_clnorm_gelu_po_kernel(
                     start=(g == 0),
                     stop=(g == PASSES - 1),
                 )
-            dealt = keep.tile([P, PACK, P], F32, name=f"dealt{u}", align_bytes=64)
+            dealt = keep.tile([P, PACK, P], F32, name=f"dealt{u}", tag=f"dealt{u}", align_bytes=64)
             nc.scalar.copy(out=dealt[:], in_=turned[:].rearrange("j (m t) -> j t m", t=PACK))
             y_ps.append(psum.tile([P, PACK, UNIT], F32, name=f"y_ps{u}", tag=f"y_ps{u}"))
             for t in range(PACK):
@@ -144,7 +156,7 @@ def tile_picked_clnorm_gelu_po_kernel(
         o_ps = {}
 
         def normalise(u):
-            diff = keep.tile([P, PACK, UNIT], F32, name=f"diff{u}", tag="diff" if u < 2 else f"normed{u - 2}", align_bytes=64)
+            diff = keep.tile([P, PACK, UNIT], F32, name=f"diff{u}", tag=("diff", "diff", "dealt2", "o_bf0")[u], align_bytes=64)
             for pair in range(PACK // 2):
                 ts = slice(2 * pair, 2 * pair + 2)
                 nc.vector.tensor_tensor(diff[:, ts, :], mu_picked[:, ts, cols(u)], y_ps[u][:, ts, :], ALU.subtract)
@@ -152,7 +164,7 @@ def tile_picked_clnorm_gelu_po_kernel(
             lists = cl_sb[:, u * UNIT // LIST_ROWS : (u + 1) * UNIT // LIST_ROWS]
             for t in range(PACK):
                 nc.vector.tensor_tensor(normed[:, t, :], rs_win[t][:].indirect(lists), diff[:, t, :], ALU.mult)
-            z[u] = keep.tile([P, UNIT, PACK], BF16, name=f"z{u}", align_bytes=64)
+            z[u] = keep.tile([P, UNIT, PACK], BF16, name=f"z{u}", tag=("dealt2", "z1", "dealt3", "z_words1")[u], align_bytes=64)
             nc.scalar.activation(out=z[u][:], in_=normed[:].rearrange("p t j -> p j t"), func=ACT.Gelu_apprx_tanh, scale=-1.0)
 
         def multiply(bank, result_tiles, z_words, z_scales):
@@ -168,10 +180,10 @@ def tile_picked_clnorm_gelu_po_kernel(
                 )
 
         def second_product(u):
-            z_words = keep.tile([P, UNIT], U32, name=f"z_words{u}", align_bytes=64)
+            z_words = keep.tile([P, UNIT], U32, name=f"z_words{u}", tag=f"z_words{u}" if u else "dealt3", align_bytes=64)
             z_scales = keep.tile([P, UNIT], U8, name=f"z_scales{u}", align_bytes=64)
             nc.vector.quantize_mx(out=z_words[:].bitcast(FP8X4), scales=z_scales[:], in_=z[u][:].rearrange("p j t -> p (j t)"))
-            o_bf = keep.tile([P, UNIT, PACK], BF16, name=f"o_bf{u}", align_bytes=64)
+            o_bf = keep.tile([P, UNIT, PACK], BF16, name=f"o_bf{u}", tag=f"o_bf{u}", align_bytes=64)
             if u < last_unit:
                 o_ps[u] = psum.tile([P, PACK, UNIT], F32, name=f"o_ps{u}", tag=f"y_ps{u}")
                 multiply(o_ps[u], range(PACK), z_words, z_scales)
@@ -184,7 +196,7 @@ def tile_picked_clnorm_gelu_po_kernel(
                     nc.scalar.copy(out=o_sb[:, 2 * pair : 2 * pair + 2, :], in_=bank[:])
                     nc.sync.dma_start(out=out_rows[:, 2 * pair : 2 * pair + 2, cols(u)], in_=o_sb[:, 2 * pair : 2 * pair + 2, :])
                 nc.vector.tensor_copy(out=o_bf[:], in_=o_sb[:].rearrange("p t j -> p j t"))
-            o_words = keep.tile([P, UNIT], I32, name=f"o_words{u}", tag=f"rs_win{u + 2}" if u < 2 else f"o_words{u}", align_bytes=64)
+            o_words = keep.tile([P, UNIT], I32, name=f"o_words{u}", align_bytes=64)
             nc.vector.quantize_mx(
                 out=o_words[:].bitcast(FP8X4), scales=o_scales[:, cols(u)], in_=o_bf[:].rearrange("p j t -> p (j t)")
             )
@@ -201,16 +213,7 @@ def tile_picked_clnorm_gelu_po_kernel(
         for u in range(units + 1):
             if u < units:
                 normalise(u)
-            if u == 0:
-                nc.vector.tensor_copy(
-                    out=w2w[:].bitcast(U16).rearrange("p (t m) -> p t m", t=PACK),
-                    in_=w2w_raw[:].bitcast(U16).rearrange("p (m t) -> p t m", t=PACK),
-                )
-                nc.vector.tensor_copy(
-                    out=w2s[:].rearrange("p (t m) -> p t m", t=PACK),
-                    in_=w2s_raw[:].rearrange("p (m t) -> p t m", t=PACK),
-                )
-            else:
+            if u > 0:
                 second_product(u - 1)
                 if u - 1 < last_unit:
                     store_result(u - 1)

@@ -36,19 +36,20 @@ def tile_picked_clnorm_gelu_po_kernel(
 
         offs_sb = keep.tile([P, S // LIST_ROWS], U16, name="offs_sb")
         cl_sb = keep.tile([P, S // LIST_ROWS], U16, name="cl_sb")
-        xs_win = keep.tile([P, PASSES * T], U8, name="xs_win", align_bytes=64)
+        late = ctx.enter_context(tc.tile_pool(name="late", bufs=1))
+        xs_tile = late.tile([P, 5 * T], U8, name="xs_tile", offset=0, align_bytes=64)
+        xs_win = xs_tile[:, 0:T]
+        xs_picked = keep.tile([P, S], U8, name="xs_picked", align_bytes=64)
         w1s_raw = keep.tile([P, PASSES * H], U8, name="w1s_raw", align_bytes=64)
-        w2s_raw = keep.tile([P, N], U8, name="w2s_raw", tag="w2s_raw", align_bytes=64)
-        x_planes = [keep.tile([P, S], U8, name=f"x_plane{g}", align_bytes=64) for g in range(PASSES)]
+        x_planes = keep.tile([P, PASSES * S], U8, name="x_planes", align_bytes=64)
         w1w_raw = keep.tile([P, PASSES * 2 * H], U8, name="w1w_raw", align_bytes=64)
-        w2w_raw = keep.tile([P, 2 * N], U8, name="w2w_raw", align_bytes=64)
         x_win = [keep.tile([P, T], I32, name=f"x_win{g}", align_bytes=64) for g in range(PASSES)]
         mu_win = [keep.tile([P, U], F32, name=f"mu_win{t}", align_bytes=64) for t in range(PACK)]
-        rs_win = [keep.tile([P, U], F32, name=f"rs_win{t}", tag=f"rs_win{t}", align_bytes=64) for t in range(PACK)]
 
-        nc.vector.memset(xs_win[:].bitcast(I32), 0)
-        for plane in (w1s_raw, w2s_raw):
-            nc.vector.memset(plane[:].bitcast(I32), 0)
+        nc.gpsimd.memset(w1s_raw[:].bitcast(I32), 0)
+        nc.vector.memset(xs_tile[32:64, 0:T].bitcast(I32), 0)
+        nc.vector.memset(xs_tile[64:128, 0:T].bitcast(I32), 0)
+        nc.vector.memset(x_planes[:].bitcast(I32), 0)
 
         ident = keep.tile([P, P], F32, name="ident", align_bytes=64)
         make_identity(nc, ident[:])
@@ -72,31 +73,52 @@ def tile_picked_clnorm_gelu_po_kernel(
         def load_table(win, rows, t):
             nc.sync.dma_start(out=win[t][:], in_=rows[:, t, :])
 
-        nc.sync.dma_start(cl_sb[:], cl)
-        load_table(mu_win, mu_rows, 0)
-        load_table(mu_win, mu_rows, 1)
         nc.sync.dma_start(offs_sb[:], offs)
-        load_scale_rows(xs_win, x_scales)
+        nc.sync.dma_start(out=xs_tile[0:32, 0:T].bitcast(I32), in_=x_scales.bitcast(I32).rearrange("g a c -> a g c"))
+        nc.sync.dma_start(cl_sb[:], cl)
+        for t in range(PACK):
+            load_table(mu_win, mu_rows, t)
+        load_scale_rows(w1s_raw, w1_scales)
         load_x(0)
         load_x(1)
         nc.sync.dma_start(
             out=w1w_raw[:].bitcast(I32).rearrange("p (g c) -> p g c", g=PASSES),
             in_=w1_words.bitcast(I32).rearrange("g p c -> p g c"),
         )
-        load_scale_rows(w1s_raw, w1_scales)
-        load_table(mu_win, mu_rows, 2)
-        load_table(mu_win, mu_rows, 3)
-        nc.sync.dma_start(out=w2w_raw[:].bitcast(I32), in_=w2_words[0].bitcast(I32))
-        load_scale_rows(w2s_raw, w2_scales)
+        nc.vector.tensor_copy(out=xs_picked[:], in_=xs_win.indirect(offs_sb[:]))
+        for q in range(QUADS):
+            nc.sync.dma_start(
+                out=x_planes[32 * q : 32 * q + 4, :].bitcast(I32).rearrange("r (g c) -> r g c", g=PASSES),
+                in_=xs_picked[8 * q : 8 * q + 8, :].bitcast(I32),
+            )
+        rs_win = [late.tile([P, U], F32, name=f"rs_win{t}", offset=t * T) for t in range(PACK)]
+        w2w_raw = late.tile([P, 2 * N], U8, name="w2w_raw", offset=PACK * T)
+        w2s_raw = late.tile([P, N], U8, name="w2s_raw", offset=PACK * T + 2 * N)
+        nc.gpsimd.memset(w2s_raw[:].bitcast(I32), 0)
         for t in range(PACK):
             load_table(rs_win, rs_rows, t)
+        nc.sync.dma_start(out=w2w_raw[:].bitcast(I32), in_=w2_words[0].bitcast(I32))
+        load_scale_rows(w2s_raw, w2_scales)
 
-        mu_picked = keep.tile([P, PACK, S], F32, name="mu_picked", align_bytes=64)
+        def cols(u):
+            return slice(u * UNIT, (u + 1) * UNIT)
+
+        units = S // UNIT
+        neg_mu = []
+        y_ps = [psum.tile([P, PACK, UNIT], F32, name=f"y_ps{u}", tag=f"y_ps{u}") for u in range(units)]
 
         def pick_mu(t):
+            picked = keep.tile([P, S], F32, name=f"mu_picked{t}", align_bytes=64)
             for lo in range(0, S, HALF):
                 lists = cl_sb[:, lo // LIST_ROWS : (lo + HALF) // LIST_ROWS]
-                nc.vector.tensor_copy(out=mu_picked[:, t, lo : lo + HALF], in_=mu_win[t][:].indirect(lists))
+                nc.vector.tensor_copy(out=picked[:, lo : lo + HALF], in_=mu_win[t][:].indirect(lists))
+            bank = psum.tile([P, units, P], F32, name=f"mu_ps{t}", tag=f"turned{t % 2}")
+            for u in range(units):
+                nc.tensor.transpose(bank[:, u, :], picked[:, cols(u)], ident[:])
+            neg_mu.append(keep.tile([P, units, P], F32, name=f"neg_mu{t}", align_bytes=64))
+            nc.scalar.activation(out=neg_mu[t][:], in_=bank[:], func=ACT.Copy, scale=-1.0)
+            for u in range(units):
+                nc.tensor.matmul(y_ps[u][:, t, :], lhsT=neg_mu[t][:, u, :], rhs=ident[:], is_transpose=True, start=(t == 0), stop=False)
 
         x_picked = [keep.tile([P, S], U32, name=f"x_picked{g}", align_bytes=64) for g in range(PASSES)]
 
@@ -106,66 +128,62 @@ def tile_picked_clnorm_gelu_po_kernel(
                 lists = offs_sb[:, lo // LIST_ROWS : (lo + step) // LIST_ROWS]
                 nc.vector.tensor_copy(out=x_picked[g][:, lo : lo + step], in_=x_win[g][:].bitcast(U32).indirect(lists))
 
-        pick_mu(0)
-        pick_mu(1)
-        for g in range(PASSES):
-            nc.vector.tensor_copy(out=x_planes[g][:], in_=xs_win[:, g * T : (g + 1) * T].indirect(offs_sb[:]))
+        for t in range(PACK):
+            pick_mu(t)
         pick_x(0)
         pick_x(1)
-        pick_mu(2)
-        pick_mu(3)
-        w2w = keep.tile([P, 2 * N], U8, name="w2w", align_bytes=64)
-        nc.vector.tensor_copy(
-            out=w2w[:].bitcast(U16).rearrange("p (t m) -> p t m", t=PACK),
-            in_=w2w_raw[:].bitcast(U16).rearrange("p (m t) -> p t m", t=PACK),
-        )
-        w2s = keep.tile([P, N], U8, name="w2s", align_bytes=64)
-        nc.vector.tensor_copy(
-            out=w2s[:].rearrange("p (t m) -> p t m", t=PACK),
-            in_=w2s_raw[:].rearrange("p (m t) -> p t m", t=PACK),
-        )
 
-        def cols(u):
-            return slice(u * UNIT, (u + 1) * UNIT)
-
-        units = S // UNIT
-        y_ps = []
+        turned = [psum.tile([P, H], F32, name=f"turned{u}", tag=f"turned{u}") for u in range(units)]
         for u in range(units):
-            turned = psum.tile([P, H], F32, name=f"turned{u}", tag=f"turned{u % 2}")
             for g in range(PASSES):
                 nc.tensor.matmul_mx(
-                    out=turned[:],
+                    out=turned[u][:],
                     lhsT=x_picked[g][:, cols(u)].bitcast(FP8X4),
-                    lhsT_scale=x_planes[g][:, cols(u)],
+                    lhsT_scale=x_planes[:, g * S + u * UNIT : g * S + (u + 1) * UNIT],
                     rhs=w1w_raw[:, 2 * g * H : 2 * (g + 1) * H].bitcast(FP4X4),
                     rhs_scale=w1s_raw[:, g * H : (g + 1) * H],
                     start=(g == 0),
                     stop=(g == PASSES - 1),
                 )
+        for u in range(units):
             dealt = keep.tile([P, PACK, P], F32, name=f"dealt{u}", tag=f"dealt{u}", align_bytes=64)
-            nc.scalar.copy(out=dealt[:], in_=turned[:].rearrange("j (m t) -> j t m", t=PACK))
-            y_ps.append(psum.tile([P, PACK, UNIT], F32, name=f"y_ps{u}", tag=f"y_ps{u}"))
+            nc.scalar.copy(out=dealt[:], in_=turned[u][:].rearrange("j (m t) -> j t m", t=PACK))
             for t in range(PACK):
-                nc.tensor.transpose(y_ps[u][:, t, :], dealt[:, t, :], ident[:])
+                nc.tensor.matmul(y_ps[u][:, t, :], lhsT=dealt[:, t, :], rhs=ident[:], is_transpose=True, start=False, stop=(t == PACK - 1))
 
         out_rows = out_0.rearrange("(p t) j -> p t j", t=PACK)
         out_words = out_1[0].rearrange("p n t -> p (n t)").bitcast(I32)
         o_scales = keep.tile([P, S], U8, name="o_scales", align_bytes=64)
         last_unit = units - 1
         z = {}
+        normed = {}
         o_ps = {}
 
-        def normalise(u):
-            diff = keep.tile([P, PACK, UNIT], F32, name=f"diff{u}", tag=("diff", "diff", "dealt2", "o_bf0")[u], align_bytes=64)
-            for pair in range(PACK // 2):
-                ts = slice(2 * pair, 2 * pair + 2)
-                nc.vector.tensor_tensor(diff[:, ts, :], mu_picked[:, ts, cols(u)], y_ps[u][:, ts, :], ALU.subtract)
-            normed = keep.tile([P, PACK, UNIT], F32, name=f"normed{u}", tag=f"normed{u}", align_bytes=64)
-            lists = cl_sb[:, u * UNIT // LIST_ROWS : (u + 1) * UNIT // LIST_ROWS]
+        def pick_rs(first, picked):
+            lists = cl_sb[:, first * UNIT // LIST_ROWS : (first * UNIT + HALF) // LIST_ROWS]
             for t in range(PACK):
-                nc.vector.tensor_tensor(normed[:, t, :], rs_win[t][:].indirect(lists), diff[:, t, :], ALU.mult)
-            z[u] = keep.tile([P, UNIT, PACK], BF16, name=f"z{u}", tag=("dealt2", "z1", "dealt3", "z_words1")[u], align_bytes=64)
-            nc.scalar.activation(out=z[u][:], in_=normed[:].rearrange("p t j -> p j t"), func=ACT.Gelu_apprx_tanh, scale=-1.0)
+                nc.vector.tensor_copy(out=picked[:, t, :], in_=rs_win[t][:].indirect(lists))
+            for i in range(HALF // UNIT):
+                u = first + i
+                normed[u] = keep.tile([P, PACK, UNIT], F32, name=f"normed{u}", align_bytes=64)
+                nc.vector.tensor_tensor(normed[u][:], picked[:, :, cols(i)], y_ps[u][:], ALU.mult)
+
+        def activate(u, tag):
+            z[u] = keep.tile([P, UNIT, PACK], BF16, name=f"z{u}", tag=tag, align_bytes=64)
+            nc.scalar.activation(out=z[u][:], in_=normed[u][:].rearrange("p t j -> p j t"), func=ACT.Gelu_apprx_tanh)
+
+        w2w = keep.tile([P, 2 * N], U8, name="w2w", align_bytes=64)
+        w2s = keep.tile([P, N], U8, name="w2s", align_bytes=64)
+
+        def deal_w2():
+            nc.gpsimd.tensor_copy(
+                out=w2w[:].bitcast(U16).rearrange("p (t m) -> p t m", t=PACK),
+                in_=w2w_raw[:].bitcast(U16).rearrange("p (m t) -> p t m", t=PACK),
+            )
+            nc.gpsimd.tensor_copy(
+                out=w2s[:].rearrange("p (t m) -> p t m", t=PACK),
+                in_=w2s_raw[:].rearrange("p (m t) -> p t m", t=PACK),
+            )
 
         def multiply(bank, result_tiles, z_words, z_scales):
             for i, t in enumerate(result_tiles):
@@ -179,44 +197,69 @@ def tile_picked_clnorm_gelu_po_kernel(
                     stop=True,
                 )
 
+        quantised = {}
+
         def second_product(u):
-            z_words = keep.tile([P, UNIT], U32, name=f"z_words{u}", tag=f"z_words{u}" if u else "dealt3", align_bytes=64)
+            z_words = keep.tile([P, UNIT], U32, name=f"z_words{u}", tag=f"z_words{u}", align_bytes=64)
             z_scales = keep.tile([P, UNIT], U8, name=f"z_scales{u}", align_bytes=64)
             nc.vector.quantize_mx(out=z_words[:].bitcast(FP8X4), scales=z_scales[:], in_=z[u][:].rearrange("p j t -> p (j t)"))
-            o_bf = keep.tile([P, UNIT, PACK], BF16, name=f"o_bf{u}", tag=f"o_bf{u}", align_bytes=64)
+            quantised[u] = (z_words, z_scales)
             if u < last_unit:
                 o_ps[u] = psum.tile([P, PACK, UNIT], F32, name=f"o_ps{u}", tag=f"y_ps{u}")
                 multiply(o_ps[u], range(PACK), z_words, z_scales)
-                nc.scalar.copy(out=o_bf[:], in_=o_ps[u][:].rearrange("p t j -> p j t"))
-            else:
-                o_sb = keep.tile([P, PACK, UNIT], F32, name=f"o_sb{u}")
-                for pair in range(PACK // 2):
-                    bank = psum.tile([P, 2, UNIT], F32, name=f"o_last{pair}", tag=f"turned{pair}")
-                    multiply(bank, (2 * pair, 2 * pair + 1), z_words, z_scales)
-                    nc.scalar.copy(out=o_sb[:, 2 * pair : 2 * pair + 2, :], in_=bank[:])
-                    nc.sync.dma_start(out=out_rows[:, 2 * pair : 2 * pair + 2, cols(u)], in_=o_sb[:, 2 * pair : 2 * pair + 2, :])
-                nc.vector.tensor_copy(out=o_bf[:], in_=o_sb[:].rearrange("p t j -> p j t"))
-            o_words = keep.tile([P, UNIT], I32, name=f"o_words{u}", align_bytes=64)
-            nc.vector.quantize_mx(
-                out=o_words[:].bitcast(FP8X4), scales=o_scales[:, cols(u)], in_=o_bf[:].rearrange("p j t -> p (j t)")
-            )
-            nc.sync.dma_start(out=out_words[:, cols(u)], in_=o_words[:])
 
         def store_result(u):
             o_sb = keep.tile([P, PACK, UNIT], F32, name=f"o_sb{u}")
-            if u == last_unit - 1:
-                nc.vector.tensor_copy(out=o_sb[:], in_=o_ps[u][:])
-            else:
-                nc.scalar.copy(out=o_sb[:], in_=o_ps[u][:])
+            nc.scalar.copy(out=o_sb[:], in_=o_ps[u][:])
             nc.sync.dma_start(out=out_rows[:, :, cols(u)], in_=o_sb[:])
+            return o_sb
 
-        for u in range(units + 1):
-            if u < units:
-                normalise(u)
-            if u > 0:
-                second_product(u - 1)
-                if u - 1 < last_unit:
-                    store_result(u - 1)
+        o_bf = {}
+
+        def round_result(u, tag):
+            o_bf[u] = keep.tile([P, UNIT, PACK], BF16, name=f"o_bf{u}", tag=tag, align_bytes=64)
+            nc.scalar.copy(out=o_bf[u][:], in_=o_ps[u][:].rearrange("p t j -> p j t"))
+
+        def quantise_results(first, count, o_words):
+            for i in range(count):
+                nc.vector.quantize_mx(
+                    out=o_words[:, cols(i)].bitcast(FP8X4),
+                    scales=o_scales[:, cols(first + i)],
+                    in_=o_bf[first + i][:].rearrange("p j t -> p (j t)"),
+                )
+            nc.sync.dma_start(out=out_words[:, first * UNIT : (first + count) * UNIT], in_=o_words[:])
+
+        def finish_last(u):
+            o_sb = keep.tile([P, PACK, UNIT], F32, name=f"o_sb{u}")
+            for pair in range(PACK // 2):
+                bank = psum.tile([P, 2, UNIT], F32, name=f"o_last{pair}", tag=f"turned{pair}")
+                multiply(bank, (2 * pair, 2 * pair + 1), *quantised[u])
+                nc.scalar.copy(out=o_sb[:, 2 * pair : 2 * pair + 2, :], in_=bank[:])
+                nc.sync.dma_start(out=out_rows[:, 2 * pair : 2 * pair + 2, cols(u)], in_=o_sb[:, 2 * pair : 2 * pair + 2, :])
+            o_bf[u] = keep.tile([P, UNIT, PACK], BF16, name=f"o_bf{u}", align_bytes=64)
+            nc.vector.tensor_copy(out=o_bf[u][:], in_=o_sb[:].rearrange("p t j -> p j t"))
+            quantise_results(u, 1, keep.tile([P, UNIT], I32, name="o_words3", align_bytes=64))
+
+        pick_rs(0, keep.tile([P, PACK, HALF], F32, name="rs_picked0", align_bytes=64))
+        activate(0, "z0")
+        activate(1, "z1")
+        deal_w2()
+        second_product(0)
+        store_result(0)
+        round_result(0, "o_bf0")
+        second_product(1)
+        store_result(1)
+        round_result(1, "o_bf1")
+        pick_rs(2, keep.tile([P, PACK, HALF], F32, name="rs_picked2", tag="z0", align_bytes=64))
+        activate(2, "z_words1")
+        activate(3, "z3")
+        second_product(2)
+        second_product(3)
+        o_sb2 = store_result(2)
+        o_bf[2] = keep.tile([P, UNIT, PACK], BF16, name="o_bf2", align_bytes=64)
+        nc.vector.tensor_copy(out=o_bf[2][:], in_=o_sb2[:].rearrange("p t j -> p j t"))
+        quantise_results(0, 3, keep.tile([P, 3 * UNIT], I32, name="o_words0", tag="z0", align_bytes=64))
+        finish_last(3)
 
         for q in range(QUADS):
             (nc.scalar if q % 2 else nc.sync).dma_start(

@@ -37,13 +37,12 @@ def tile_picked_clnorm_gelu_po_kernel(
         offs_sb = keep.tile([P, S // LIST_ROWS], U16, name="offs_sb")
         cl_sb = keep.tile([P, S // LIST_ROWS], U16, name="cl_sb")
         late = ctx.enter_context(tc.tile_pool(name="late", bufs=1))
-        xs_tile = late.tile([P, 5 * T], U8, name="xs_tile", offset=0, align_bytes=64)
+        xs_tile = late.tile([P, 10 * T], U8, name="xs_tile", offset=0, align_bytes=64)
         xs_win = xs_tile[:, 0:T]
         xs_picked = keep.tile([P, S], U8, name="xs_picked", align_bytes=64)
         w1s_raw = keep.tile([P, PASSES * H], U8, name="w1s_raw", align_bytes=64)
         x_planes = keep.tile([P, PASSES * S], U8, name="x_planes", align_bytes=64)
-        w1w_raw = keep.tile([P, PASSES * 2 * H], U8, name="w1w_raw", align_bytes=64)
-        x_win = [keep.tile([P, T], I32, name=f"x_win{g}", align_bytes=64) for g in range(PASSES)]
+        x_win = [keep.tile([P, T], I32, name="x_win0", align_bytes=64)]
         mu_win = [keep.tile([P, U], F32, name=f"mu_win{t}", align_bytes=64) for t in range(PACK)]
 
         nc.gpsimd.memset(w1s_raw[:].bitcast(I32), 0)
@@ -80,17 +79,19 @@ def tile_picked_clnorm_gelu_po_kernel(
             load_table(mu_win, mu_rows, t)
         load_scale_rows(w1s_raw, w1_scales)
         load_x(0)
-        load_x(1)
-        nc.sync.dma_start(
-            out=w1w_raw[:].bitcast(I32).rearrange("p (g c) -> p g c", g=PASSES),
-            in_=w1_words.bitcast(I32).rearrange("g p c -> p g c"),
-        )
         nc.vector.tensor_copy(out=xs_picked[:], in_=xs_win.indirect(offs_sb[:]))
         for q in range(QUADS):
             nc.sync.dma_start(
                 out=x_planes[32 * q : 32 * q + 4, :].bitcast(I32).rearrange("r (g c) -> r g c", g=PASSES),
                 in_=xs_picked[8 * q : 8 * q + 8, :].bitcast(I32),
             )
+        x_win.append(late.tile([P, T], I32, name="x_win1", offset=6 * T))
+        w1w_raw = late.tile([P, PASSES * 2 * H], U8, name="w1w_raw", offset=5 * T)
+        load_x(1)
+        nc.sync.dma_start(
+            out=w1w_raw[:].bitcast(I32).rearrange("p (g c) -> p g c", g=PASSES),
+            in_=w1_words.bitcast(I32).rearrange("g p c -> p g c"),
+        )
         rs_win = [late.tile([P, U], F32, name=f"rs_win{t}", offset=t * T) for t in range(PACK)]
         w2w_raw = late.tile([P, 2 * N], U8, name="w2w_raw", offset=PACK * T)
         w2s_raw = late.tile([P, N], U8, name="w2s_raw", offset=PACK * T + 2 * N)
@@ -156,21 +157,22 @@ def tile_picked_clnorm_gelu_po_kernel(
         o_scales = keep.tile([P, S], U8, name="o_scales", align_bytes=64)
         last_unit = units - 1
         z = {}
-        normed = {}
         o_ps = {}
 
-        def pick_rs(first, picked):
-            lists = cl_sb[:, first * UNIT // LIST_ROWS : (first * UNIT + HALF) // LIST_ROWS]
-            for t in range(PACK):
-                nc.vector.tensor_copy(out=picked[:, t, :], in_=rs_win[t][:].indirect(lists))
-            for i in range(HALF // UNIT):
-                u = first + i
-                normed[u] = keep.tile([P, PACK, UNIT], F32, name=f"normed{u}", align_bytes=64)
-                nc.vector.tensor_tensor(normed[u][:], picked[:, :, cols(i)], y_ps[u][:], ALU.mult)
+        rs_picked = [keep.tile([P, PACK, HALF], F32, name=f"rs_picked{h}", align_bytes=64) for h in range(S // HALF)]
 
-        def activate(u, tag):
-            z[u] = keep.tile([P, UNIT, PACK], BF16, name=f"z{u}", tag=tag, align_bytes=64)
-            nc.scalar.activation(out=z[u][:], in_=normed[u][:].rearrange("p t j -> p j t"), func=ACT.Gelu_apprx_tanh)
+        def pick_rs(t, h):
+            lists = cl_sb[:, h * HALF // LIST_ROWS : (h + 1) * HALF // LIST_ROWS]
+            nc.vector.tensor_copy(out=rs_picked[h][:, t, :], in_=rs_win[t][:].indirect(lists))
+
+        def normalise(u, z_place):
+            h, i = divmod(u, HALF // UNIT)
+            normed = keep.tile([P, PACK, UNIT], F32, name=f"normed{u}", tag=f"normed{u}", align_bytes=64)
+            nc.vector.tensor_tensor(normed[:], rs_picked[h][:, :, cols(i)], y_ps[u][:], ALU.mult)
+            z[u] = z_place
+            nc.scalar.activation(
+                out=z_place.rearrange("p (j t) -> p j t", t=PACK), in_=normed[:].rearrange("p t j -> p j t"), func=ACT.Gelu_apprx_tanh
+            )
 
         w2w = keep.tile([P, 2 * N], U8, name="w2w", align_bytes=64)
         w2s = keep.tile([P, N], U8, name="w2s", align_bytes=64)
@@ -202,23 +204,23 @@ def tile_picked_clnorm_gelu_po_kernel(
         def second_product(u):
             z_words = keep.tile([P, UNIT], U32, name=f"z_words{u}", tag=f"z_words{u}", align_bytes=64)
             z_scales = keep.tile([P, UNIT], U8, name=f"z_scales{u}", align_bytes=64)
-            nc.vector.quantize_mx(out=z_words[:].bitcast(FP8X4), scales=z_scales[:], in_=z[u][:].rearrange("p j t -> p (j t)"))
+            nc.vector.quantize_mx(out=z_words[:].bitcast(FP8X4), scales=z_scales[:], in_=z[u])
             quantised[u] = (z_words, z_scales)
             if u < last_unit:
                 o_ps[u] = psum.tile([P, PACK, UNIT], F32, name=f"o_ps{u}", tag=f"y_ps{u}")
                 multiply(o_ps[u], range(PACK), z_words, z_scales)
 
+        o_bf = {}
+
+        def round_result(u, o_sb):
+            o_bf[u] = keep.tile([P, UNIT, PACK], BF16, name=f"o_bf{u}", align_bytes=64)
+            nc.vector.tensor_copy(out=o_bf[u][:], in_=o_sb[:].rearrange("p t j -> p j t"))
+
         def store_result(u):
             o_sb = keep.tile([P, PACK, UNIT], F32, name=f"o_sb{u}")
             nc.scalar.copy(out=o_sb[:], in_=o_ps[u][:])
             nc.sync.dma_start(out=out_rows[:, :, cols(u)], in_=o_sb[:])
-            return o_sb
-
-        o_bf = {}
-
-        def round_result(u, tag):
-            o_bf[u] = keep.tile([P, UNIT, PACK], BF16, name=f"o_bf{u}", tag=tag, align_bytes=64)
-            nc.scalar.copy(out=o_bf[u][:], in_=o_ps[u][:].rearrange("p t j -> p j t"))
+            round_result(u, o_sb)
 
         def quantise_results(first, count, o_words):
             for i in range(count):
@@ -236,29 +238,27 @@ def tile_picked_clnorm_gelu_po_kernel(
                 multiply(bank, (2 * pair, 2 * pair + 1), *quantised[u])
                 nc.scalar.copy(out=o_sb[:, 2 * pair : 2 * pair + 2, :], in_=bank[:])
                 nc.sync.dma_start(out=out_rows[:, 2 * pair : 2 * pair + 2, cols(u)], in_=o_sb[:, 2 * pair : 2 * pair + 2, :])
-            o_bf[u] = keep.tile([P, UNIT, PACK], BF16, name=f"o_bf{u}", align_bytes=64)
-            nc.vector.tensor_copy(out=o_bf[u][:], in_=o_sb[:].rearrange("p t j -> p j t"))
+            round_result(u, o_sb)
             quantise_results(u, 1, keep.tile([P, UNIT], I32, name="o_words3", align_bytes=64))
 
-        pick_rs(0, keep.tile([P, PACK, HALF], F32, name="rs_picked0", align_bytes=64))
-        activate(0, "z0")
-        activate(1, "z1")
+        for t in range(PACK - 1):
+            pick_rs(t, 0)
+            pick_rs(t, 1)
+        pick_rs(PACK - 1, 0)
+        normalise(0, rs_picked[1][:, PACK - 1, :].bitcast(BF16))
+        normalise(1, keep.tile([P, UNIT * PACK], BF16, name="z1", align_bytes=64)[:])
         deal_w2()
         second_product(0)
-        store_result(0)
-        round_result(0, "o_bf0")
+        pick_rs(PACK - 1, 1)
         second_product(1)
-        store_result(1)
-        round_result(1, "o_bf1")
-        pick_rs(2, keep.tile([P, PACK, HALF], F32, name="rs_picked2", tag="z0", align_bytes=64))
-        activate(2, "z_words1")
-        activate(3, "z3")
+        store_result(0)
+        normalise(2, keep.tile([P, UNIT * PACK], BF16, name="z2", tag="z_words0", align_bytes=64)[:])
+        normalise(3, keep.tile([P, UNIT * PACK], BF16, name="z3", tag="normed2", align_bytes=64)[:])
         second_product(2)
         second_product(3)
-        o_sb2 = store_result(2)
-        o_bf[2] = keep.tile([P, UNIT, PACK], BF16, name="o_bf2", align_bytes=64)
-        nc.vector.tensor_copy(out=o_bf[2][:], in_=o_sb2[:].rearrange("p t j -> p j t"))
-        quantise_results(0, 3, keep.tile([P, 3 * UNIT], I32, name="o_words0", tag="z0", align_bytes=64))
+        store_result(1)
+        store_result(2)
+        quantise_results(0, 3, keep.tile([P, 3 * UNIT], I32, name="o_words0", align_bytes=64))
         finish_last(3)
 
         for q in range(QUADS):

@@ -23,6 +23,7 @@ PASSES = K // (P * PACK)
 QUADS = 4
 LIST_ROWS = 16
 UNIT = 128
+LAST = PACK - 1
 HALF = S // 2
 
 
@@ -146,11 +147,14 @@ def tile_picked_clnorm_gelu_po_kernel(
                     start=(g == 0),
                     stop=(g == PASSES - 1),
                 )
+        centred = []
         for u in range(units):
             dealt = keep.tile([P, PACK, P], F32, name=f"dealt{u}", tag=f"dealt{u}", align_bytes=64)
             nc.scalar.copy(out=dealt[:], in_=turned[u][:].rearrange("j (m t) -> j t m", t=PACK))
             for t in range(PACK):
                 nc.tensor.matmul(y_ps[u][:, t, :], lhsT=dealt[:, t, :], rhs=ident[:], is_transpose=True, start=False, stop=(t == PACK - 1))
+            centred.append(keep.tile([P, UNIT], F32, name=f"centred{u}", align_bytes=64))
+            nc.scalar.copy(out=centred[u][:], in_=y_ps[u][:, LAST, :])
 
         out_rows = out_0.rearrange("(p t) j -> p t j", t=PACK)
         out_words = out_1[0].rearrange("p n t -> p (n t)").bitcast(I32)
@@ -159,20 +163,19 @@ def tile_picked_clnorm_gelu_po_kernel(
         z = {}
         o_ps = {}
 
-        rs_picked = [keep.tile([P, PACK, HALF], F32, name=f"rs_picked{h}", align_bytes=64) for h in range(S // HALF)]
+        rs_picked = keep.tile([P, LAST, S], F32, name="rs_picked", align_bytes=64)
 
         def pick_rs(t, h):
             lists = cl_sb[:, h * HALF // LIST_ROWS : (h + 1) * HALF // LIST_ROWS]
-            nc.vector.tensor_copy(out=rs_picked[h][:, t, :], in_=rs_win[t][:].indirect(lists))
+            nc.vector.tensor_copy(out=rs_picked[:, t, h * HALF : (h + 1) * HALF], in_=rs_win[t][:].indirect(lists))
 
-        def normalise(u, z_place):
-            h, i = divmod(u, HALF // UNIT)
-            normed = keep.tile([P, PACK, UNIT], F32, name=f"normed{u}", tag=f"normed{u}", align_bytes=64)
-            nc.vector.tensor_tensor(normed[:], rs_picked[h][:, :, cols(i)], y_ps[u][:], ALU.mult)
-            z[u] = z_place
-            nc.scalar.activation(
-                out=z_place.rearrange("p (j t) -> p j t", t=PACK), in_=normed[:].rearrange("p t j -> p j t"), func=ACT.Gelu_apprx_tanh
-            )
+        def normalise(u, normed_tag, z_tag):
+            normed = keep.tile([P, PACK, UNIT], F32, name=f"normed{u}", tag=normed_tag, align_bytes=64)
+            nc.vector.tensor_tensor(normed[:, :LAST, :], rs_picked[:, :, cols(u)], y_ps[u][:, :LAST, :], ALU.mult)
+            lists = cl_sb[:, u * UNIT // LIST_ROWS : (u + 1) * UNIT // LIST_ROWS]
+            nc.vector.tensor_tensor(normed[:, LAST, :], rs_win[LAST][:].indirect(lists), centred[u][:], ALU.mult)
+            z[u] = keep.tile([P, UNIT, PACK], BF16, name=f"z{u}", tag=z_tag, align_bytes=64)
+            nc.scalar.activation(out=z[u][:], in_=normed[:].rearrange("p t j -> p j t"), func=ACT.Gelu_apprx_tanh)
 
         w2w = keep.tile([P, 2 * N], U8, name="w2w", align_bytes=64)
         w2s = keep.tile([P, N], U8, name="w2s", align_bytes=64)
@@ -204,7 +207,7 @@ def tile_picked_clnorm_gelu_po_kernel(
         def second_product(u):
             z_words = keep.tile([P, UNIT], U32, name=f"z_words{u}", tag=f"z_words{u}", align_bytes=64)
             z_scales = keep.tile([P, UNIT], U8, name=f"z_scales{u}", align_bytes=64)
-            nc.vector.quantize_mx(out=z_words[:].bitcast(FP8X4), scales=z_scales[:], in_=z[u])
+            nc.vector.quantize_mx(out=z_words[:].bitcast(FP8X4), scales=z_scales[:], in_=z[u][:].rearrange("p j t -> p (j t)"))
             quantised[u] = (z_words, z_scales)
             if u < last_unit:
                 o_ps[u] = psum.tile([P, PACK, UNIT], F32, name=f"o_ps{u}", tag=f"y_ps{u}")
@@ -241,19 +244,17 @@ def tile_picked_clnorm_gelu_po_kernel(
             round_result(u, o_sb)
             quantise_results(u, 1, keep.tile([P, UNIT], I32, name="o_words3", align_bytes=64))
 
-        for t in range(PACK - 1):
-            pick_rs(t, 0)
-            pick_rs(t, 1)
-        pick_rs(PACK - 1, 0)
-        normalise(0, rs_picked[1][:, PACK - 1, :].bitcast(BF16))
-        normalise(1, keep.tile([P, UNIT * PACK], BF16, name="z1", align_bytes=64)[:])
+        for t in range(LAST):
+            for h in range(S // HALF):
+                pick_rs(t, h)
+        normalise(0, "normed0", "z0")
+        normalise(1, "normed1", "z1")
         deal_w2()
         second_product(0)
-        pick_rs(PACK - 1, 1)
-        second_product(1)
+        normalise(2, "z0", "z2")
         store_result(0)
-        normalise(2, keep.tile([P, UNIT * PACK], BF16, name="z2", tag="z_words0", align_bytes=64)[:])
-        normalise(3, keep.tile([P, UNIT * PACK], BF16, name="z3", tag="normed2", align_bytes=64)[:])
+        second_product(1)
+        normalise(3, "z1", "z_words1")
         second_product(2)
         second_product(3)
         store_result(1)

@@ -44,6 +44,7 @@ def tile_picked_clnorm_gelu_po_kernel(
         w1s_raw = keep.tile([P, PASSES * H], U8, name="w1s_raw", align_bytes=64)
         x_planes = keep.tile([P, PASSES * S], U8, name="x_planes", align_bytes=64)
         x_win = [keep.tile([P, T], I32, name="x_win0", align_bytes=64)]
+        w1w_raw = keep.tile([P, PASSES * 2 * H], U8, name="w1w_raw", align_bytes=64)
         mu_win = [keep.tile([P, U], F32, name=f"mu_win{t}", align_bytes=64) for t in range(PACK)]
 
         nc.gpsimd.memset(w1s_raw[:].bitcast(I32), 0)
@@ -60,8 +61,8 @@ def tile_picked_clnorm_gelu_po_kernel(
         def load_x(g):
             nc.sync.dma_start(out=x_win[g][:], in_=x_words[g].rearrange("p n t -> p (n t)").bitcast(I32))
 
-        def load_scale_rows(plane, scales):
-            for q in range(QUADS):
+        def load_scale_rows(plane, scales, quads=range(QUADS)):
+            for q in quads:
                 nc.sync.dma_start(
                     out=plane[32 * q : 32 * q + 4, :].bitcast(I32).rearrange("r (g c) -> r g c", g=scales.shape[0]),
                     in_=scales[:, 4 * q : 4 * q + 4, :].bitcast(I32).rearrange("g r c -> r g c"),
@@ -78,8 +79,13 @@ def tile_picked_clnorm_gelu_po_kernel(
         nc.sync.dma_start(cl_sb[:], cl)
         for t in range(PACK):
             load_table(mu_win, mu_rows, t)
-        load_scale_rows(w1s_raw, w1_scales)
+        nc.sync.dma_start(
+            out=w1w_raw[:].bitcast(I32).rearrange("p (g c) -> p g c", g=PASSES),
+            in_=w1_words.bitcast(I32).rearrange("g p c -> p g c"),
+        )
+        load_scale_rows(w1s_raw, w1_scales, range(QUADS // 2))
         load_x(0)
+        load_scale_rows(w1s_raw, w1_scales, range(QUADS // 2, QUADS))
         nc.vector.tensor_copy(out=xs_picked[:], in_=xs_win.indirect(offs_sb[:]))
         for q in range(QUADS):
             nc.sync.dma_start(
@@ -87,20 +93,15 @@ def tile_picked_clnorm_gelu_po_kernel(
                 in_=xs_picked[8 * q : 8 * q + 8, :].bitcast(I32),
             )
         x_win.append(late.tile([P, T], I32, name="x_win1", offset=6 * T))
-        w1w_raw = late.tile([P, PASSES * 2 * H], U8, name="w1w_raw", offset=5 * T)
         load_x(1)
-        nc.sync.dma_start(
-            out=w1w_raw[:].bitcast(I32).rearrange("p (g c) -> p g c", g=PASSES),
-            in_=w1_words.bitcast(I32).rearrange("g p c -> p g c"),
-        )
         rs_win = [late.tile([P, U], F32, name=f"rs_win{t}", offset=t * T) for t in range(PACK)]
         w2w_raw = late.tile([P, 2 * N], U8, name="w2w_raw", offset=PACK * T)
         w2s_raw = late.tile([P, N], U8, name="w2s_raw", offset=PACK * T + 2 * N)
         nc.gpsimd.memset(w2s_raw[:].bitcast(I32), 0)
-        for t in range(PACK):
-            load_table(rs_win, rs_rows, t)
         nc.sync.dma_start(out=w2w_raw[:].bitcast(I32), in_=w2_words[0].bitcast(I32))
         load_scale_rows(w2s_raw, w2_scales)
+        for t in range(PACK):
+            load_table(rs_win, rs_rows, t)
 
         def cols(u):
             return slice(u * UNIT, (u + 1) * UNIT)
@@ -136,8 +137,8 @@ def tile_picked_clnorm_gelu_po_kernel(
         pick_x(1)
 
         turned = [psum.tile([P, H], F32, name=f"turned{u}", tag=f"turned{u}") for u in range(units)]
-        for u in range(units):
-            for g in range(PASSES):
+        for g in range(PASSES):
+            for u in range(units):
                 nc.tensor.matmul_mx(
                     out=turned[u][:],
                     lhsT=x_picked[g][:, cols(u)].bitcast(FP8X4),
@@ -153,7 +154,7 @@ def tile_picked_clnorm_gelu_po_kernel(
             nc.scalar.copy(out=dealt[:], in_=turned[u][:].rearrange("j (m t) -> j t m", t=PACK))
             for t in range(PACK):
                 nc.tensor.matmul(y_ps[u][:, t, :], lhsT=dealt[:, t, :], rhs=ident[:], is_transpose=True, start=False, stop=(t == PACK - 1))
-            centred.append(keep.tile([P, UNIT], F32, name=f"centred{u}", align_bytes=64))
+            centred.append(keep.tile([P, UNIT], F32, name=f"centred{u}", tag=f"centred{u}", align_bytes=64))
             nc.scalar.copy(out=centred[u][:], in_=y_ps[u][:, LAST, :])
 
         out_rows = out_0.rearrange("(p t) j -> p t j", t=PACK)
@@ -213,26 +214,27 @@ def tile_picked_clnorm_gelu_po_kernel(
                 o_ps[u] = psum.tile([P, PACK, UNIT], F32, name=f"o_ps{u}", tag=f"y_ps{u}")
                 multiply(o_ps[u], range(PACK), z_words, z_scales)
 
-        o_bf = {}
-
         def round_result(u, o_sb):
-            o_bf[u] = keep.tile([P, UNIT, PACK], BF16, name=f"o_bf{u}", align_bytes=64)
-            nc.vector.tensor_copy(out=o_bf[u][:], in_=o_sb[:].rearrange("p t j -> p j t"))
+            nc.vector.tensor_copy(out=o_bf[:, cols(u), :], in_=o_sb[:].rearrange("p t j -> p j t"))
 
         def store_result(u):
             o_sb = keep.tile([P, PACK, UNIT], F32, name=f"o_sb{u}")
-            nc.scalar.copy(out=o_sb[:], in_=o_ps[u][:])
+            if u == 1:
+                nc.vector.tensor_copy(out=o_sb[:], in_=o_ps[u][:])
+            else:
+                nc.scalar.copy(out=o_sb[:], in_=o_ps[u][:])
             nc.sync.dma_start(out=out_rows[:, :, cols(u)], in_=o_sb[:])
-            round_result(u, o_sb)
+            return o_sb
 
-        def quantise_results(first, count, o_words):
-            for i in range(count):
-                nc.vector.quantize_mx(
-                    out=o_words[:, cols(i)].bitcast(FP8X4),
-                    scales=o_scales[:, cols(first + i)],
-                    in_=o_bf[first + i][:].rearrange("p j t -> p (j t)"),
-                )
-            nc.sync.dma_start(out=out_words[:, first * UNIT : (first + count) * UNIT], in_=o_words[:])
+        o_words = keep.tile([P, S], I32, name="o_words", align_bytes=64)
+
+        def quantise_results(tokens):
+            nc.vector.quantize_mx(
+                out=o_words[:, tokens].bitcast(FP8X4), scales=o_scales[:, tokens], in_=o_bf[:, tokens, :].rearrange("p j t -> p (j t)")
+            )
+
+        def store_words(tokens):
+            nc.sync.dma_start(out=out_words[:, tokens], in_=o_words[:, tokens])
 
         def finish_last(u):
             o_sb = keep.tile([P, PACK, UNIT], F32, name=f"o_sb{u}")
@@ -242,7 +244,8 @@ def tile_picked_clnorm_gelu_po_kernel(
                 nc.scalar.copy(out=o_sb[:, 2 * pair : 2 * pair + 2, :], in_=bank[:])
                 nc.sync.dma_start(out=out_rows[:, 2 * pair : 2 * pair + 2, cols(u)], in_=o_sb[:, 2 * pair : 2 * pair + 2, :])
             round_result(u, o_sb)
-            quantise_results(u, 1, keep.tile([P, UNIT], I32, name="o_words3", align_bytes=64))
+            quantise_results(cols(u))
+            store_words(slice(HALF, S))
 
         for t in range(LAST):
             for h in range(S // HALF):
@@ -252,14 +255,18 @@ def tile_picked_clnorm_gelu_po_kernel(
         deal_w2()
         second_product(0)
         normalise(2, "z0", "z2")
-        store_result(0)
+        first_result = store_result(0)
         second_product(1)
         normalise(3, "z1", "z_words1")
+        o_bf = keep.tile([P, S, PACK], BF16, name="o_bf", tag="centred3", align_bytes=64)
         second_product(2)
         second_product(3)
-        store_result(1)
-        store_result(2)
-        quantise_results(0, 3, keep.tile([P, 3 * UNIT], I32, name="o_words0", align_bytes=64))
+        round_result(0, first_result)
+        round_result(1, store_result(1))
+        quantise_results(slice(0, HALF))
+        store_words(slice(0, HALF))
+        round_result(2, store_result(2))
+        quantise_results(cols(2))
         finish_last(3)
 
         for q in range(QUADS):

@@ -24,6 +24,7 @@ QUADS = 4
 LIST_ROWS = 16
 UNIT = 128
 LAST = PACK - 1
+LINE = 4
 HALF = S // 2
 
 
@@ -164,6 +165,12 @@ def tile_picked_clnorm_gelu_po_kernel(
         z = {}
         o_ps = {}
 
+        def by_tile(ap):
+            return ap.rearrange("p t (c i) -> p c t i", i=LINE)
+
+        def by_token(ap):
+            return ap.rearrange("p (c i) t -> p c t i", i=LINE)
+
         rs_picked = keep.tile([P, LAST, S], F32, name="rs_picked", align_bytes=64)
 
         def pick_rs(t, h):
@@ -176,7 +183,7 @@ def tile_picked_clnorm_gelu_po_kernel(
             lists = cl_sb[:, u * UNIT // LIST_ROWS : (u + 1) * UNIT // LIST_ROWS]
             nc.vector.tensor_tensor(normed[:, LAST, :], rs_win[LAST][:].indirect(lists), centred[u][:], ALU.mult)
             z[u] = keep.tile([P, UNIT, PACK], BF16, name=f"z{u}", tag=z_tag, align_bytes=64)
-            nc.scalar.activation(out=z[u][:], in_=normed[:].rearrange("p t j -> p j t"), func=ACT.Gelu_apprx_tanh)
+            nc.scalar.activation(out=by_token(z[u][:]), in_=by_tile(normed[:]), func=ACT.Gelu_apprx_tanh)
 
         w2w = keep.tile([P, 2 * N], U8, name="w2w", align_bytes=64)
         w2s = keep.tile([P, N], U8, name="w2s", align_bytes=64)
@@ -215,7 +222,7 @@ def tile_picked_clnorm_gelu_po_kernel(
                 multiply(o_ps[u], range(PACK), z_words, z_scales)
 
         def round_result(u, o_sb):
-            nc.vector.tensor_copy(out=o_bf[:, cols(u), :], in_=o_sb[:].rearrange("p t j -> p j t"))
+            nc.vector.tensor_copy(out=by_token(o_bf[:, cols(u), :]), in_=by_tile(o_sb[:]))
 
         def store_result(u):
             o_sb = keep.tile([P, PACK, UNIT], F32, name=f"o_sb{u}")

@@ -35,26 +35,24 @@ def tile_picked_clnorm_gelu_po_kernel(
     with ExitStack() as ctx:
         keep = ctx.enter_context(tc.tile_pool(name="keep", bufs=1))
         psum = ctx.enter_context(tc.psum_pool(name="psum", bufs=1))
+        late = ctx.enter_context(tc.tile_pool(name="late", bufs=1))
 
         offs_sb = keep.tile([P, S // LIST_ROWS], U16, name="offs_sb")
         cl_sb = keep.tile([P, S // LIST_ROWS], U16, name="cl_sb")
-        late = ctx.enter_context(tc.tile_pool(name="late", bufs=1))
-        xs_tile = late.tile([P, 10 * T], U8, name="xs_tile", offset=0, align_bytes=64)
-        xs_win = xs_tile[:, 0:T]
+        late_small = 8 * T + 8 * U
+        xs_tile = late.tile([P, late_small + 3 * N + PASSES * H], U8, name="xs_tile", offset=0, align_bytes=64)
         xs_picked = keep.tile([P, S], U8, name="xs_picked", align_bytes=64)
-        w1s_raw = keep.tile([P, PASSES * H], U8, name="w1s_raw", align_bytes=64)
+        w1w = keep.tile([P, PASSES * 2 * H], U8, name="w1w", align_bytes=64)
         x_planes = keep.tile([P, PASSES * S], U8, name="x_planes", align_bytes=64)
-        x_win = [keep.tile([P, T], I32, name="x_win0", align_bytes=64)]
-        w1w_raw = keep.tile([P, PASSES * 2 * H], U8, name="w1w_raw", align_bytes=64)
         mu_win = [keep.tile([P, U], F32, name=f"mu_win{t}", align_bytes=64) for t in range(PACK)]
+        rs_win = [keep.tile([P, U], F32, name=f"rs_win{t}", align_bytes=64) for t in range(2)]
 
-        nc.gpsimd.memset(w1s_raw[:].bitcast(I32), 0)
         nc.vector.memset(xs_tile[32:64, 0:T].bitcast(I32), 0)
         nc.vector.memset(xs_tile[64:128, 0:T].bitcast(I32), 0)
-        nc.vector.memset(x_planes[:].bitcast(I32), 0)
-
         ident = keep.tile([P, P], F32, name="ident", align_bytes=64)
         make_identity(nc, ident[:])
+        nc.gpsimd.memset(x_planes[:].bitcast(I32), 0)
+
         warm = keep.tile([P, 2], F32, name="warm")
         nc.vector.memset(warm[:, 0:1], 0.0)
         nc.scalar.activation(out=warm[:, 1:2], in_=warm[:, 0:1], func=ACT.Gelu_apprx_tanh)
@@ -80,62 +78,85 @@ def tile_picked_clnorm_gelu_po_kernel(
         nc.sync.dma_start(cl_sb[:], cl)
         for t in range(PACK):
             load_table(mu_win, mu_rows, t)
+        load_table(rs_win, rs_rows, 0)
         nc.sync.dma_start(
-            out=w1w_raw[:].bitcast(I32).rearrange("p (g c) -> p g c", g=PASSES),
+            out=w1w[:].bitcast(I32).rearrange("p (g c) -> p g c", g=PASSES),
             in_=w1_words.bitcast(I32).rearrange("g p c -> p g c"),
         )
-        load_scale_rows(w1s_raw, w1_scales, range(QUADS // 2))
-        load_x(0)
-        load_scale_rows(w1s_raw, w1_scales, range(QUADS // 2, QUADS))
-        nc.vector.tensor_copy(out=xs_picked[:], in_=xs_win.indirect(offs_sb[:]))
+        load_table(rs_win, rs_rows, 1)
+        nc.vector.tensor_copy(out=xs_picked[:], in_=xs_tile[:, 0:T].indirect(offs_sb[:]))
         for q in range(QUADS):
             nc.sync.dma_start(
                 out=x_planes[32 * q : 32 * q + 4, :].bitcast(I32).rearrange("r (g c) -> r g c", g=PASSES),
                 in_=xs_picked[8 * q : 8 * q + 8, :].bitcast(I32),
             )
-        x_win.append(late.tile([P, T], I32, name="x_win1", offset=6 * T))
+        x_win = [late.tile([P, T], I32, name=f"x_win{g}", offset=4 * T * g) for g in range(PASSES)]
+        w1s = late.tile([P, PASSES * H], U8, name="w1s", offset=late_small + 3 * N, align_bytes=64)
+        nc.gpsimd.memset(w1s[:].bitcast(I32), 0)
+        rs_win.extend([late.tile([P, U], F32, name=f"rs_win{t}", offset=8 * T + 4 * U * (t - 2)) for t in (2, 3)])
+        load_x(0)
+        load_scale_rows(w1s, w1_scales)
+        load_table(rs_win, rs_rows, 2)
         load_x(1)
-        rs_win = [late.tile([P, U], F32, name=f"rs_win{t}", offset=t * T) for t in range(PACK)]
-        w2w_raw = late.tile([P, 2 * N], U8, name="w2w_raw", offset=PACK * T)
-        w2s_raw = late.tile([P, N], U8, name="w2s_raw", offset=PACK * T + 2 * N)
+        load_table(rs_win, rs_rows, LAST)
+        w2w_raw = late.tile([P, 2 * N], U8, name="w2w_raw", offset=late_small)
+        w2s_raw = late.tile([P, N], U8, name="w2s_raw", offset=late_small + 2 * N)
         nc.gpsimd.memset(w2s_raw[:].bitcast(I32), 0)
         nc.sync.dma_start(out=w2w_raw[:].bitcast(I32), in_=w2_words[0].bitcast(I32))
         load_scale_rows(w2s_raw, w2_scales)
-        for t in range(PACK):
-            load_table(rs_win, rs_rows, t)
 
         def cols(u):
             return slice(u * UNIT, (u + 1) * UNIT)
 
+        def half(h):
+            return slice(h * HALF, (h + 1) * HALF)
+
+        def entries(lists, tokens):
+            return lists[:, tokens.start // LIST_ROWS : tokens.stop // LIST_ROWS]
+
         units = S // UNIT
-        neg_mu = []
+        halves = S // HALF
         y_ps = [psum.tile([P, PACK, UNIT], F32, name=f"y_ps{u}", tag=f"y_ps{u}") for u in range(units)]
+
+        def pick(win, out, h, on_scalar):
+            looked_up = win[:].indirect(entries(cl_sb, half(h)))
+            if on_scalar:
+                nc.scalar.activation(out=out, in_=looked_up, func=ACT.Copy)
+            else:
+                nc.vector.tensor_copy(out=out, in_=looked_up)
 
         def pick_mu(t):
             picked = keep.tile([P, S], F32, name=f"mu_picked{t}", align_bytes=64)
-            for lo in range(0, S, HALF):
-                lists = cl_sb[:, lo // LIST_ROWS : (lo + HALF) // LIST_ROWS]
-                nc.vector.tensor_copy(out=picked[:, lo : lo + HALF], in_=mu_win[t][:].indirect(lists))
-            bank = psum.tile([P, units, P], F32, name=f"mu_ps{t}", tag=f"turned{t % 2}")
+            for h in range(halves):
+                pick(mu_win[t], picked[:, half(h)], h, t % 2 == 0)
+            bank = psum.tile([P, units, P], F32, name=f"mu_ps{t}", tag=f"turned{t}")
             for u in range(units):
                 nc.tensor.transpose(bank[:, u, :], picked[:, cols(u)], ident[:])
-            neg_mu.append(keep.tile([P, units, P], F32, name=f"neg_mu{t}", align_bytes=64))
-            nc.scalar.activation(out=neg_mu[t][:], in_=bank[:], func=ACT.Copy, scale=-1.0)
+            neg_mu = keep.tile([P, units, P], F32, name=f"neg_mu{t}", align_bytes=64)
+            nc.scalar.activation(out=neg_mu[:], in_=bank[:], func=ACT.Copy, scale=-1.0)
             for u in range(units):
-                nc.tensor.matmul(y_ps[u][:, t, :], lhsT=neg_mu[t][:, u, :], rhs=ident[:], is_transpose=True, start=(t == 0), stop=False)
+                nc.tensor.matmul(y_ps[u][:, t, :], lhsT=neg_mu[:, u, :], rhs=ident[:], is_transpose=True, start=(t == 0), stop=False)
+
+        rs_picked = keep.tile([P, PACK, S], F32, name="rs_picked", align_bytes=64)
+
+        def pick_rs(t):
+            for h in range(halves):
+                pick(rs_win[t], rs_picked[:, t, half(h)], h, t == 0 or (t, h) == (LAST, 0))
 
         x_picked = [keep.tile([P, S], U32, name=f"x_picked{g}", align_bytes=64) for g in range(PASSES)]
 
-        def pick_x(g):
-            step = HALF if g == PASSES - 1 else S
+        def pick_x(g, step):
             for lo in range(0, S, step):
-                lists = offs_sb[:, lo // LIST_ROWS : (lo + step) // LIST_ROWS]
-                nc.vector.tensor_copy(out=x_picked[g][:, lo : lo + step], in_=x_win[g][:].bitcast(U32).indirect(lists))
+                tokens = slice(lo, lo + step)
+                nc.vector.tensor_copy(out=x_picked[g][:, tokens], in_=x_win[g][:].bitcast(U32).indirect(entries(offs_sb, tokens)))
 
         for t in range(PACK):
             pick_mu(t)
-        pick_x(0)
-        pick_x(1)
+        for t in range(LAST):
+            pick_rs(t)
+        pick_x(0, S)
+        pick_x(1, UNIT)
+        pick_rs(LAST)
 
         turned = [psum.tile([P, H], F32, name=f"turned{u}", tag=f"turned{u}") for u in range(units)]
         for g in range(PASSES):
@@ -144,26 +165,33 @@ def tile_picked_clnorm_gelu_po_kernel(
                     out=turned[u][:],
                     lhsT=x_picked[g][:, cols(u)].bitcast(FP8X4),
                     lhsT_scale=x_planes[:, g * S + u * UNIT : g * S + (u + 1) * UNIT],
-                    rhs=w1w_raw[:, 2 * g * H : 2 * (g + 1) * H].bitcast(FP4X4),
-                    rhs_scale=w1s_raw[:, g * H : (g + 1) * H],
+                    rhs=w1w[:, 2 * g * H : 2 * (g + 1) * H].bitcast(FP4X4),
+                    rhs_scale=w1s[:, g * H : (g + 1) * H],
                     start=(g == 0),
                     stop=(g == PASSES - 1),
                 )
-        centred = []
         for u in range(units):
-            dealt = keep.tile([P, PACK, P], F32, name=f"dealt{u}", tag=f"dealt{u}", align_bytes=64)
+            dealt = keep.tile([P, PACK, P], F32, name=f"dealt{u}", align_bytes=64)
             nc.scalar.copy(out=dealt[:], in_=turned[u][:].rearrange("j (m t) -> j t m", t=PACK))
             for t in range(PACK):
                 nc.tensor.matmul(y_ps[u][:, t, :], lhsT=dealt[:, t, :], rhs=ident[:], is_transpose=True, start=False, stop=(t == PACK - 1))
-            centred.append(keep.tile([P, UNIT], F32, name=f"centred{u}", tag=f"centred{u}", align_bytes=64))
-            nc.scalar.copy(out=centred[u][:], in_=y_ps[u][:, LAST, :])
+
+        w2w = keep.tile([P, 2 * N], U8, name="w2w", align_bytes=64)
+        w2s = keep.tile([P, N], U8, name="w2s", align_bytes=64)
+        nc.gpsimd.tensor_copy(
+            out=w2w[:].bitcast(U16).rearrange("p (t m) -> p t m", t=PACK),
+            in_=w2w_raw[:].bitcast(U16).rearrange("p (m t) -> p t m", t=PACK),
+        )
+        nc.gpsimd.tensor_copy(
+            out=w2s[:].rearrange("p (t m) -> p t m", t=PACK),
+            in_=w2s_raw[:].rearrange("p (m t) -> p t m", t=PACK),
+        )
 
         out_rows = out_0.rearrange("(p t) j -> p t j", t=PACK)
         out_words = out_1[0].rearrange("p n t -> p (n t)").bitcast(I32)
         o_scales = keep.tile([P, S], U8, name="o_scales", align_bytes=64)
-        last_unit = units - 1
-        z = {}
-        o_ps = {}
+        o_words = keep.tile([P, S], I32, name="o_words", align_bytes=64)
+        o_bf = keep.tile([P, S, PACK], BF16, name="o_bf", align_bytes=64)
 
         def by_tile(ap):
             return ap.rearrange("p t (c i) -> p c t i", i=LINE)
@@ -171,37 +199,27 @@ def tile_picked_clnorm_gelu_po_kernel(
         def by_token(ap):
             return ap.rearrange("p (c i) t -> p c t i", i=LINE)
 
-        rs_picked = keep.tile([P, LAST, S], F32, name="rs_picked", align_bytes=64)
+        normed = {}
+        z = {}
+        o_ps = {}
+        o_sb = {}
 
-        def pick_rs(t, h):
-            lists = cl_sb[:, h * HALF // LIST_ROWS : (h + 1) * HALF // LIST_ROWS]
-            nc.vector.tensor_copy(out=rs_picked[:, t, h * HALF : (h + 1) * HALF], in_=rs_win[t][:].indirect(lists))
+        def normalise(u, tag=None):
+            normed[u] = keep.tile([P, PACK, UNIT], F32, name=f"normed{u}", tag=tag or f"normed{u}", align_bytes=64)
+            nc.vector.tensor_tensor(normed[u][:], rs_picked[:, :, cols(u)], y_ps[u][:], ALU.mult)
 
-        def normalise(u, normed_tag, z_tag):
-            normed = keep.tile([P, PACK, UNIT], F32, name=f"normed{u}", tag=normed_tag, align_bytes=64)
-            nc.vector.tensor_tensor(normed[:, :LAST, :], rs_picked[:, :, cols(u)], y_ps[u][:, :LAST, :], ALU.mult)
-            lists = cl_sb[:, u * UNIT // LIST_ROWS : (u + 1) * UNIT // LIST_ROWS]
-            nc.vector.tensor_tensor(normed[:, LAST, :], rs_win[LAST][:].indirect(lists), centred[u][:], ALU.mult)
-            z[u] = keep.tile([P, UNIT, PACK], BF16, name=f"z{u}", tag=z_tag, align_bytes=64)
-            nc.scalar.activation(out=by_token(z[u][:]), in_=by_tile(normed[:]), func=ACT.Gelu_apprx_tanh)
+        def activate(u, tag=None):
+            z[u] = keep.tile([P, UNIT, PACK], BF16, name=f"z{u}", tag=tag or f"z{u}", align_bytes=64)
+            nc.scalar.activation(out=by_token(z[u][:]), in_=by_tile(normed[u][:]), func=ACT.Gelu_apprx_tanh)
 
-        w2w = keep.tile([P, 2 * N], U8, name="w2w", align_bytes=64)
-        w2s = keep.tile([P, N], U8, name="w2s", align_bytes=64)
-
-        def deal_w2():
-            nc.gpsimd.tensor_copy(
-                out=w2w[:].bitcast(U16).rearrange("p (t m) -> p t m", t=PACK),
-                in_=w2w_raw[:].bitcast(U16).rearrange("p (m t) -> p t m", t=PACK),
-            )
-            nc.gpsimd.tensor_copy(
-                out=w2s[:].rearrange("p (t m) -> p t m", t=PACK),
-                in_=w2s_raw[:].rearrange("p (m t) -> p t m", t=PACK),
-            )
-
-        def multiply(bank, result_tiles, z_words, z_scales):
-            for i, t in enumerate(result_tiles):
+        def second_product(u):
+            z_words = keep.tile([P, UNIT], U32, name=f"z_words{u}", tag=f"z_words{u}", align_bytes=64)
+            z_scales = keep.tile([P, UNIT], U8, name=f"z_scales{u}", align_bytes=64)
+            nc.vector.quantize_mx(out=z_words[:].bitcast(FP8X4), scales=z_scales[:], in_=z[u][:].rearrange("p j t -> p (j t)"))
+            o_ps[u] = psum.tile([P, PACK, UNIT], F32, name=f"o_ps{u}", tag=f"turned{u}")
+            for t in range(PACK):
                 nc.tensor.matmul_mx(
-                    out=bank[:, i, :],
+                    out=o_ps[u][:, t, :],
                     lhsT=w2w[:, 2 * t * P : 2 * (t + 1) * P].bitcast(FP4X4),
                     lhsT_scale=w2s[:, t * P : (t + 1) * P],
                     rhs=z_words[:].bitcast(FP8X4),
@@ -210,71 +228,32 @@ def tile_picked_clnorm_gelu_po_kernel(
                     stop=True,
                 )
 
-        quantised = {}
-
-        def second_product(u):
-            z_words = keep.tile([P, UNIT], U32, name=f"z_words{u}", tag=f"z_words{u}", align_bytes=64)
-            z_scales = keep.tile([P, UNIT], U8, name=f"z_scales{u}", align_bytes=64)
-            nc.vector.quantize_mx(out=z_words[:].bitcast(FP8X4), scales=z_scales[:], in_=z[u][:].rearrange("p j t -> p (j t)"))
-            quantised[u] = (z_words, z_scales)
-            if u < last_unit:
-                o_ps[u] = psum.tile([P, PACK, UNIT], F32, name=f"o_ps{u}", tag=f"y_ps{u}")
-                multiply(o_ps[u], range(PACK), z_words, z_scales)
-
-        def round_result(u, o_sb):
-            nc.vector.tensor_copy(out=by_token(o_bf[:, cols(u), :]), in_=by_tile(o_sb[:]))
-
-        def store_result(u):
-            o_sb = keep.tile([P, PACK, UNIT], F32, name=f"o_sb{u}")
-            if u == 1:
-                nc.vector.tensor_copy(out=o_sb[:], in_=o_ps[u][:])
+        def store_result(u, on_scalar):
+            o_sb[u] = keep.tile([P, PACK, UNIT], F32, name=f"o_sb{u}")
+            if on_scalar:
+                nc.scalar.copy(out=o_sb[u][:], in_=o_ps[u][:])
             else:
-                nc.scalar.copy(out=o_sb[:], in_=o_ps[u][:])
-            nc.sync.dma_start(out=out_rows[:, :, cols(u)], in_=o_sb[:])
-            return o_sb
+                nc.vector.tensor_copy(out=o_sb[u][:], in_=o_ps[u][:])
+            nc.sync.dma_start(out=out_rows[:, :, cols(u)], in_=o_sb[u][:])
 
-        o_words = keep.tile([P, S], I32, name="o_words", align_bytes=64)
+        def round_result(u):
+            nc.vector.tensor_copy(out=by_token(o_bf[:, cols(u), :]), in_=by_tile(o_sb[u][:]))
 
         def quantise_results(tokens):
             nc.vector.quantize_mx(
                 out=o_words[:, tokens].bitcast(FP8X4), scales=o_scales[:, tokens], in_=o_bf[:, tokens, :].rearrange("p j t -> p (j t)")
             )
-
-        def store_words(tokens):
             nc.sync.dma_start(out=out_words[:, tokens], in_=o_words[:, tokens])
 
-        def finish_last(u):
-            o_sb = keep.tile([P, PACK, UNIT], F32, name=f"o_sb{u}")
-            for pair in range(PACK // 2):
-                bank = psum.tile([P, 2, UNIT], F32, name=f"o_last{pair}", tag=f"turned{pair}")
-                multiply(bank, (2 * pair, 2 * pair + 1), *quantised[u])
-                nc.scalar.copy(out=o_sb[:, 2 * pair : 2 * pair + 2, :], in_=bank[:])
-                nc.sync.dma_start(out=out_rows[:, 2 * pair : 2 * pair + 2, cols(u)], in_=o_sb[:, 2 * pair : 2 * pair + 2, :])
-            round_result(u, o_sb)
-            quantise_results(cols(u))
-            store_words(slice(HALF, S))
-
-        for t in range(LAST):
-            for h in range(S // HALF):
-                pick_rs(t, h)
-        normalise(0, "normed0", "z0")
-        normalise(1, "normed1", "z1")
-        deal_w2()
-        second_product(0)
-        normalise(2, "z0", "z2")
-        first_result = store_result(0)
-        second_product(1)
-        normalise(3, "z1", "z_words1")
-        o_bf = keep.tile([P, S, PACK], BF16, name="o_bf", tag="centred3", align_bytes=64)
-        second_product(2)
-        second_product(3)
-        round_result(0, first_result)
-        round_result(1, store_result(1))
-        quantise_results(slice(0, HALF))
-        store_words(slice(0, HALF))
-        round_result(2, store_result(2))
-        quantise_results(cols(2))
-        finish_last(3)
+        for u in range(units):
+            normalise(u)
+            activate(u)
+            second_product(u)
+        for h in range(halves):
+            for u in (2 * h, 2 * h + 1):
+                store_result(u, u > 0)
+                round_result(u)
+            quantise_results(half(h))
 
         for q in range(QUADS):
             (nc.scalar if q % 2 else nc.sync).dma_start(

@@ -44,7 +44,7 @@ def tile_picked_clnorm_gelu_po_kernel(
         xs_picked = keep.tile([P, S], U8, name="xs_picked", align_bytes=64)
         w1w = keep.tile([P, PASSES * 2 * H], U8, name="w1w", align_bytes=64)
         x_planes = keep.tile([P, PASSES * S], U8, name="x_planes", align_bytes=64)
-        mu_win = [keep.tile([P, U], F32, name=f"mu_win{t}", align_bytes=64) for t in range(PACK)]
+        mu_win = [keep.tile([P, U], F32, name=f"mu_win{t}", tag=f"mu_win{t}", align_bytes=64) for t in range(PACK)]
         rs_win = [keep.tile([P, U], F32, name=f"rs_win{t}", align_bytes=64) for t in range(2)]
 
         nc.vector.memset(xs_tile[32:64, 0:T].bitcast(I32), 0)
@@ -132,7 +132,7 @@ def tile_picked_clnorm_gelu_po_kernel(
             bank = psum.tile([P, units, P], F32, name=f"mu_ps{t}", tag=f"turned{t}")
             for u in range(units):
                 nc.tensor.transpose(bank[:, u, :], picked[:, cols(u)], ident[:])
-            neg_mu = keep.tile([P, units, P], F32, name=f"neg_mu{t}", align_bytes=64)
+            neg_mu = keep.tile([P, units, P], F32, name=f"neg_mu{t}", tag=("mu_win2" if t == 0 else f"neg_mu{t}"), align_bytes=64)
             nc.scalar.activation(out=neg_mu[:], in_=bank[:], func=ACT.Copy, scale=-1.0)
             for u in range(units):
                 nc.tensor.matmul(y_ps[u][:, t, :], lhsT=neg_mu[:, u, :], rhs=ident[:], is_transpose=True, start=(t == 0), stop=False)
@@ -141,7 +141,7 @@ def tile_picked_clnorm_gelu_po_kernel(
 
         def pick_rs(t):
             for h in range(halves):
-                pick(rs_win[t], rs_picked[:, t, half(h)], h, t == 0 or (t, h) == (LAST, 0))
+                pick(rs_win[t], rs_picked[:, t, half(h)], h, (t, h) in ((1, 1), (2, 0), (2, 1), (LAST, 0), (LAST, 1)))
 
         x_picked = [keep.tile([P, S], U32, name=f"x_picked{g}", align_bytes=64) for g in range(PASSES)]
 
@@ -154,7 +154,7 @@ def tile_picked_clnorm_gelu_po_kernel(
             pick_mu(t)
         for t in range(LAST):
             pick_rs(t)
-        pick_x(0, S)
+        pick_x(0, HALF)
         pick_x(1, UNIT)
         pick_rs(LAST)
 
@@ -172,7 +172,10 @@ def tile_picked_clnorm_gelu_po_kernel(
                 )
         for u in range(units):
             dealt = keep.tile([P, PACK, P], F32, name=f"dealt{u}", align_bytes=64)
-            nc.scalar.copy(out=dealt[:], in_=turned[u][:].rearrange("j (m t) -> j t m", t=PACK))
+            if u == 0:
+                nc.vector.tensor_copy(out=dealt[:], in_=turned[u][:].rearrange("j (m t) -> j t m", t=PACK))
+            else:
+                nc.scalar.copy(out=dealt[:], in_=turned[u][:].rearrange("j (m t) -> j t m", t=PACK))
             for t in range(PACK):
                 nc.tensor.matmul(y_ps[u][:, t, :], lhsT=dealt[:, t, :], rhs=ident[:], is_transpose=True, start=False, stop=(t == PACK - 1))
 
@@ -204,18 +207,27 @@ def tile_picked_clnorm_gelu_po_kernel(
         o_ps = {}
         o_sb = {}
 
-        def normalise(u, tag=None):
-            normed[u] = keep.tile([P, PACK, UNIT], F32, name=f"normed{u}", tag=tag or f"normed{u}", align_bytes=64)
-            nc.vector.tensor_tensor(normed[u][:], rs_picked[:, :, cols(u)], y_ps[u][:], ALU.mult)
+        def buffer(name):
+            return keep.tile([P, PACK * UNIT], F32, name=name, align_bytes=64)
 
-        def activate(u, tag=None):
-            z[u] = keep.tile([P, UNIT, PACK], BF16, name=f"z{u}", tag=tag or f"z{u}", align_bytes=64)
-            nc.scalar.activation(out=by_token(z[u][:]), in_=by_tile(normed[u][:]), func=ACT.Gelu_apprx_tanh)
+        def as_tiles(buf):
+            return buf[:].rearrange("p (t j) -> p t j", t=PACK)
+
+        def as_tokens(buf):
+            return buf[:, 0 : PACK * UNIT // 2].bitcast(BF16).rearrange("p (j t) -> p j t", t=PACK)
+
+        def normalise(u, out):
+            normed[u] = out
+            nc.vector.tensor_tensor(out, rs_picked[:, :, cols(u)], y_ps[u][:], ALU.mult)
+
+        def activate(u, out):
+            z[u] = out
+            nc.scalar.activation(out=by_token(out), in_=by_tile(normed[u]), func=ACT.Gelu_apprx_tanh)
 
         def second_product(u):
             z_words = keep.tile([P, UNIT], U32, name=f"z_words{u}", tag=f"z_words{u}", align_bytes=64)
             z_scales = keep.tile([P, UNIT], U8, name=f"z_scales{u}", align_bytes=64)
-            nc.vector.quantize_mx(out=z_words[:].bitcast(FP8X4), scales=z_scales[:], in_=z[u][:].rearrange("p j t -> p (j t)"))
+            nc.vector.quantize_mx(out=z_words[:].bitcast(FP8X4), scales=z_scales[:], in_=z[u].rearrange("p j t -> p (j t)"))
             o_ps[u] = psum.tile([P, PACK, UNIT], F32, name=f"o_ps{u}", tag=f"turned{u}")
             for t in range(PACK):
                 nc.tensor.matmul_mx(
@@ -228,16 +240,15 @@ def tile_picked_clnorm_gelu_po_kernel(
                     stop=True,
                 )
 
-        def store_result(u, on_scalar):
-            o_sb[u] = keep.tile([P, PACK, UNIT], F32, name=f"o_sb{u}")
-            if on_scalar:
-                nc.scalar.copy(out=o_sb[u][:], in_=o_ps[u][:])
+        def copy_result(u, out):
+            o_sb[u] = out
+            if u == 0:
+                nc.vector.tensor_copy(out=out, in_=o_ps[u][:])
             else:
-                nc.vector.tensor_copy(out=o_sb[u][:], in_=o_ps[u][:])
-            nc.sync.dma_start(out=out_rows[:, :, cols(u)], in_=o_sb[u][:])
+                nc.scalar.copy(out=out, in_=o_ps[u][:])
 
         def round_result(u):
-            nc.vector.tensor_copy(out=by_token(o_bf[:, cols(u), :]), in_=by_tile(o_sb[u][:]))
+            nc.vector.tensor_copy(out=by_token(o_bf[:, cols(u), :]), in_=by_tile(o_sb[u]))
 
         def quantise_results(tokens):
             nc.vector.quantize_mx(
@@ -246,13 +257,15 @@ def tile_picked_clnorm_gelu_po_kernel(
             nc.sync.dma_start(out=out_words[:, tokens], in_=o_words[:, tokens])
 
         for u in range(units):
-            normalise(u)
-            activate(u)
+            normalise(u, as_tiles(buffer(f"normed{u}")))
+            activate(u, as_tokens(buffer(f"z{u}")))
             second_product(u)
         for h in range(halves):
-            for u in (2 * h, 2 * h + 1):
-                store_result(u, u > 0)
-                round_result(u)
+            o_half = keep.tile([P, PACK, HALF], F32, name=f"o_half{h}", align_bytes=64)
+            for i in range(2):
+                copy_result(2 * h + i, o_half[:, :, cols(i)])
+                round_result(2 * h + i)
+            nc.sync.dma_start(out=out_rows[:, :, half(h)], in_=o_half[:])
             quantise_results(half(h))
 
         for q in range(QUADS):

@@ -40,9 +40,9 @@ def tile_picked_clnorm_gelu_po_kernel(
         offs_sb = keep.tile([P, S // LIST_ROWS], U16, name="offs_sb")
         cl_sb = keep.tile([P, S // LIST_ROWS], U16, name="cl_sb")
         late_small = 8 * T + 8 * U
-        xs_tile = late.tile([P, late_small + 3 * N + PASSES * H], U8, name="xs_tile", offset=0, align_bytes=64)
+        xs_tile = late.tile([P, late_small + 3 * N + PASSES * H + 2 * H], U8, name="xs_tile", offset=0, align_bytes=64)
         xs_picked = keep.tile([P, S], U8, name="xs_picked", align_bytes=64)
-        w1w = keep.tile([P, PASSES * 2 * H], U8, name="w1w", align_bytes=64)
+        w1w = [keep.tile([P, 2 * H], U8, name="w1w0", align_bytes=64)]
         x_planes = keep.tile([P, PASSES * S], U8, name="x_planes", align_bytes=64)
         mu_win = [keep.tile([P, U], F32, name=f"mu_win{t}", tag=f"mu_win{t}", align_bytes=64) for t in range(PACK)]
         rs_win = [keep.tile([P, U], F32, name=f"rs_win{t}", align_bytes=64) for t in range(2)]
@@ -79,10 +79,7 @@ def tile_picked_clnorm_gelu_po_kernel(
         for t in range(PACK):
             load_table(mu_win, mu_rows, t)
         load_table(rs_win, rs_rows, 0)
-        nc.sync.dma_start(
-            out=w1w[:].bitcast(I32).rearrange("p (g c) -> p g c", g=PASSES),
-            in_=w1_words.bitcast(I32).rearrange("g p c -> p g c"),
-        )
+        nc.sync.dma_start(out=w1w[0][:].bitcast(I32), in_=w1_words[0].bitcast(I32))
         load_table(rs_win, rs_rows, 1)
         nc.vector.tensor_copy(out=xs_picked[:], in_=xs_tile[:, 0:T].indirect(offs_sb[:]))
         for q in range(QUADS):
@@ -98,6 +95,8 @@ def tile_picked_clnorm_gelu_po_kernel(
         load_scale_rows(w1s, w1_scales)
         load_table(rs_win, rs_rows, 2)
         load_x(1)
+        w1w.append(late.tile([P, 2 * H], U8, name="w1w1", offset=late_small + 3 * N + PASSES * H, align_bytes=64))
+        nc.sync.dma_start(out=w1w[1][:].bitcast(I32), in_=w1_words[1].bitcast(I32))
         load_table(rs_win, rs_rows, LAST)
         w2w_raw = late.tile([P, 2 * N], U8, name="w2w_raw", offset=late_small)
         w2s_raw = late.tile([P, N], U8, name="w2s_raw", offset=late_small + 2 * N)
@@ -141,7 +140,7 @@ def tile_picked_clnorm_gelu_po_kernel(
 
         def pick_rs(t):
             for h in range(halves):
-                pick(rs_win[t], rs_picked[:, t, half(h)], h, (t, h) in ((1, 1), (2, 0), (2, 1), (LAST, 0), (LAST, 1)))
+                pick(rs_win[t], rs_picked[:, t, half(h)], h, (t, h) == (1, 1))
 
         x_picked = [keep.tile([P, S], U32, name=f"x_picked{g}", align_bytes=64) for g in range(PASSES)]
 
@@ -156,7 +155,7 @@ def tile_picked_clnorm_gelu_po_kernel(
             pick_rs(t)
         pick_x(0, HALF)
         pick_x(1, UNIT)
-        pick_rs(LAST)
+        pick(rs_win[LAST], rs_picked[:, LAST, half(0)], 0, True)
 
         turned = [psum.tile([P, H], F32, name=f"turned{u}", tag=f"turned{u}") for u in range(units)]
         for g in range(PASSES):
@@ -165,7 +164,7 @@ def tile_picked_clnorm_gelu_po_kernel(
                     out=turned[u][:],
                     lhsT=x_picked[g][:, cols(u)].bitcast(FP8X4),
                     lhsT_scale=x_planes[:, g * S + u * UNIT : g * S + (u + 1) * UNIT],
-                    rhs=w1w[:, 2 * g * H : 2 * (g + 1) * H].bitcast(FP4X4),
+                    rhs=w1w[g][:].bitcast(FP4X4),
                     rhs_scale=w1s[:, g * H : (g + 1) * H],
                     start=(g == 0),
                     stop=(g == PASSES - 1),
@@ -174,6 +173,7 @@ def tile_picked_clnorm_gelu_po_kernel(
             dealt = keep.tile([P, PACK, P], F32, name=f"dealt{u}", align_bytes=64)
             if u == 0:
                 nc.vector.tensor_copy(out=dealt[:], in_=turned[u][:].rearrange("j (m t) -> j t m", t=PACK))
+                pick(rs_win[LAST], rs_picked[:, LAST, half(1)], 1, False)
             else:
                 nc.scalar.copy(out=dealt[:], in_=turned[u][:].rearrange("j (m t) -> j t m", t=PACK))
             for t in range(PACK):
@@ -261,11 +261,10 @@ def tile_picked_clnorm_gelu_po_kernel(
             activate(u, as_tokens(buffer(f"z{u}")))
             second_product(u)
         for h in range(halves):
-            o_half = keep.tile([P, PACK, HALF], F32, name=f"o_half{h}", align_bytes=64)
-            for i in range(2):
-                copy_result(2 * h + i, o_half[:, :, cols(i)])
-                round_result(2 * h + i)
-            nc.sync.dma_start(out=out_rows[:, :, half(h)], in_=o_half[:])
+            for u in (2 * h, 2 * h + 1):
+                copy_result(u, as_tiles(buffer(f"o_sb{u}")))
+                nc.sync.dma_start(out=out_rows[:, :, cols(u)], in_=o_sb[u])
+                round_result(u)
             quantise_results(half(h))
 
         for q in range(QUADS):

@@ -23,9 +23,21 @@ PASSES = K // (P * PACK)
 QUADS = 4
 LIST_ROWS = 16
 UNIT = 128
+UNITS = S // UNIT
+HALF = S // 2
+HALVES = S // HALF
 LAST = PACK - 1
 LINE = 4
-HALF = S // 2
+EARLY_RS = 2
+
+X_BYTES = 4 * T
+TABLE_BYTES = 4 * U
+AT_RS = PASSES * X_BYTES
+AT_W2_WORDS = AT_RS + (PACK - EARLY_RS) * TABLE_BYTES
+AT_W2_SCALES = AT_W2_WORDS + 2 * N
+AT_W1_SCALES = AT_W2_SCALES + N
+AT_W1_WORDS = AT_W1_SCALES + PASSES * H
+LATE_BYTES = AT_W1_WORDS + 2 * H
 
 
 def tile_picked_clnorm_gelu_po_kernel(
@@ -39,13 +51,12 @@ def tile_picked_clnorm_gelu_po_kernel(
 
         offs_sb = keep.tile([P, S // LIST_ROWS], U16, name="offs_sb")
         cl_sb = keep.tile([P, S // LIST_ROWS], U16, name="cl_sb")
-        late_small = 8 * T + 8 * U
-        xs_tile = late.tile([P, late_small + 3 * N + PASSES * H + 2 * H], U8, name="xs_tile", offset=0, align_bytes=64)
+        xs_tile = late.tile([P, LATE_BYTES], U8, name="xs_tile", offset=0, align_bytes=64)
         xs_picked = keep.tile([P, S], U8, name="xs_picked", align_bytes=64)
         w1w = [keep.tile([P, 2 * H], U8, name="w1w0", align_bytes=64)]
         x_planes = keep.tile([P, PASSES * S], U8, name="x_planes", align_bytes=64)
         mu_win = [keep.tile([P, U], F32, name=f"mu_win{t}", tag=f"mu_win{t}", align_bytes=64) for t in range(PACK)]
-        rs_win = [keep.tile([P, U], F32, name=f"rs_win{t}", align_bytes=64) for t in range(2)]
+        rs_win = [keep.tile([P, U], F32, name=f"rs_win{t}", align_bytes=64) for t in range(EARLY_RS)]
 
         nc.vector.memset(xs_tile[32:64, 0:T].bitcast(I32), 0)
         nc.vector.memset(xs_tile[64:128, 0:T].bitcast(I32), 0)
@@ -60,8 +71,11 @@ def tile_picked_clnorm_gelu_po_kernel(
         def load_x(g):
             nc.sync.dma_start(out=x_win[g][:], in_=x_words[g].rearrange("p n t -> p (n t)").bitcast(I32))
 
-        def load_scale_rows(plane, scales, quads=range(QUADS)):
-            for q in quads:
+        def load_w1_words(g):
+            nc.sync.dma_start(out=w1w[g][:].bitcast(I32), in_=w1_words[g].bitcast(I32))
+
+        def load_scale_rows(plane, scales):
+            for q in range(QUADS):
                 nc.sync.dma_start(
                     out=plane[32 * q : 32 * q + 4, :].bitcast(I32).rearrange("r (g c) -> r g c", g=scales.shape[0]),
                     in_=scales[:, 4 * q : 4 * q + 4, :].bitcast(I32).rearrange("g r c -> r g c"),
@@ -78,28 +92,30 @@ def tile_picked_clnorm_gelu_po_kernel(
         nc.sync.dma_start(cl_sb[:], cl)
         for t in range(PACK):
             load_table(mu_win, mu_rows, t)
-        load_table(rs_win, rs_rows, 0)
-        nc.sync.dma_start(out=w1w[0][:].bitcast(I32), in_=w1_words[0].bitcast(I32))
-        load_table(rs_win, rs_rows, 1)
+            if t == 1:
+                load_w1_words(0)
+        for t in range(EARLY_RS):
+            load_table(rs_win, rs_rows, t)
         nc.vector.tensor_copy(out=xs_picked[:], in_=xs_tile[:, 0:T].indirect(offs_sb[:]))
         for q in range(QUADS):
             nc.sync.dma_start(
                 out=x_planes[32 * q : 32 * q + 4, :].bitcast(I32).rearrange("r (g c) -> r g c", g=PASSES),
                 in_=xs_picked[8 * q : 8 * q + 8, :].bitcast(I32),
             )
-        x_win = [late.tile([P, T], I32, name=f"x_win{g}", offset=4 * T * g) for g in range(PASSES)]
-        w1s = late.tile([P, PASSES * H], U8, name="w1s", offset=late_small + 3 * N, align_bytes=64)
+        x_win = [late.tile([P, T], I32, name=f"x_win{g}", offset=X_BYTES * g) for g in range(PASSES)]
+        w1s = late.tile([P, PASSES * H], U8, name="w1s", offset=AT_W1_SCALES, align_bytes=64)
         nc.gpsimd.memset(w1s[:].bitcast(I32), 0)
-        rs_win.extend([late.tile([P, U], F32, name=f"rs_win{t}", offset=8 * T + 4 * U * (t - 2)) for t in (2, 3)])
+        for t in range(EARLY_RS, PACK):
+            rs_win.append(late.tile([P, U], F32, name=f"rs_win{t}", offset=AT_RS + TABLE_BYTES * (t - EARLY_RS)))
         load_x(0)
         load_scale_rows(w1s, w1_scales)
-        load_table(rs_win, rs_rows, 2)
+        load_table(rs_win, rs_rows, EARLY_RS)
         load_x(1)
-        w1w.append(late.tile([P, 2 * H], U8, name="w1w1", offset=late_small + 3 * N + PASSES * H, align_bytes=64))
-        nc.sync.dma_start(out=w1w[1][:].bitcast(I32), in_=w1_words[1].bitcast(I32))
+        w1w.append(late.tile([P, 2 * H], U8, name="w1w1", offset=AT_W1_WORDS, align_bytes=64))
+        load_w1_words(1)
         load_table(rs_win, rs_rows, LAST)
-        w2w_raw = late.tile([P, 2 * N], U8, name="w2w_raw", offset=late_small)
-        w2s_raw = late.tile([P, N], U8, name="w2s_raw", offset=late_small + 2 * N)
+        w2w_raw = late.tile([P, 2 * N], U8, name="w2w_raw", offset=AT_W2_WORDS)
+        w2s_raw = late.tile([P, N], U8, name="w2s_raw", offset=AT_W2_SCALES)
         nc.gpsimd.memset(w2s_raw[:].bitcast(I32), 0)
         nc.sync.dma_start(out=w2w_raw[:].bitcast(I32), in_=w2_words[0].bitcast(I32))
         load_scale_rows(w2s_raw, w2_scales)
@@ -113,9 +129,7 @@ def tile_picked_clnorm_gelu_po_kernel(
         def entries(lists, tokens):
             return lists[:, tokens.start // LIST_ROWS : tokens.stop // LIST_ROWS]
 
-        units = S // UNIT
-        halves = S // HALF
-        y_ps = [psum.tile([P, PACK, UNIT], F32, name=f"y_ps{u}", tag=f"y_ps{u}") for u in range(units)]
+        y_ps = [psum.tile([P, PACK, UNIT], F32, name=f"y_ps{u}", tag=f"y_ps{u}") for u in range(UNITS)]
 
         def pick(win, out, h, on_scalar):
             looked_up = win[:].indirect(entries(cl_sb, half(h)))
@@ -126,21 +140,20 @@ def tile_picked_clnorm_gelu_po_kernel(
 
         def pick_mu(t):
             picked = keep.tile([P, S], F32, name=f"mu_picked{t}", align_bytes=64)
-            for h in range(halves):
+            for h in range(HALVES):
                 pick(mu_win[t], picked[:, half(h)], h, t % 2 == 0)
-            bank = psum.tile([P, units, P], F32, name=f"mu_ps{t}", tag=f"turned{t}")
-            for u in range(units):
+            bank = psum.tile([P, UNITS, P], F32, name=f"mu_ps{t}", tag=f"turned{t}")
+            for u in range(UNITS):
                 nc.tensor.transpose(bank[:, u, :], picked[:, cols(u)], ident[:])
-            neg_mu = keep.tile([P, units, P], F32, name=f"neg_mu{t}", tag=("mu_win2" if t == 0 else f"neg_mu{t}"), align_bytes=64)
+            neg_mu = keep.tile([P, UNITS, P], F32, name=f"neg_mu{t}", tag=("mu_win2" if t == 0 else f"neg_mu{t}"), align_bytes=64)
             nc.scalar.activation(out=neg_mu[:], in_=bank[:], func=ACT.Copy, scale=-1.0)
-            for u in range(units):
+            for u in range(UNITS):
                 nc.tensor.matmul(y_ps[u][:, t, :], lhsT=neg_mu[:, u, :], rhs=ident[:], is_transpose=True, start=(t == 0), stop=False)
 
         rs_picked = keep.tile([P, PACK, S], F32, name="rs_picked", align_bytes=64)
 
-        def pick_rs(t):
-            for h in range(halves):
-                pick(rs_win[t], rs_picked[:, t, half(h)], h, (t, h) == (1, 1))
+        def pick_rs(t, h, on_scalar):
+            pick(rs_win[t], rs_picked[:, t, half(h)], h, on_scalar)
 
         x_picked = [keep.tile([P, S], U32, name=f"x_picked{g}", align_bytes=64) for g in range(PASSES)]
 
@@ -152,14 +165,15 @@ def tile_picked_clnorm_gelu_po_kernel(
         for t in range(PACK):
             pick_mu(t)
         for t in range(LAST):
-            pick_rs(t)
+            for h in range(HALVES):
+                pick_rs(t, h, (t, h) == (EARLY_RS - 1, HALVES - 1))
         pick_x(0, HALF)
         pick_x(1, UNIT)
-        pick(rs_win[LAST], rs_picked[:, LAST, half(0)], 0, True)
+        pick_rs(LAST, 0, True)
 
-        turned = [psum.tile([P, H], F32, name=f"turned{u}", tag=f"turned{u}") for u in range(units)]
+        turned = [psum.tile([P, H], F32, name=f"turned{u}", tag=f"turned{u}") for u in range(UNITS)]
         for g in range(PASSES):
-            for u in range(units):
+            for u in range(UNITS):
                 nc.tensor.matmul_mx(
                     out=turned[u][:],
                     lhsT=x_picked[g][:, cols(u)].bitcast(FP8X4),
@@ -169,15 +183,16 @@ def tile_picked_clnorm_gelu_po_kernel(
                     start=(g == 0),
                     stop=(g == PASSES - 1),
                 )
-        for u in range(units):
-            dealt = keep.tile([P, PACK, P], F32, name=f"dealt{u}", align_bytes=64)
+        for u in range(UNITS):
+            y_dealt = keep.tile([P, PACK, P], F32, name=f"y_dealt{u}", align_bytes=64)
+            y_columns = turned[u][:].rearrange("j (m t) -> j t m", t=PACK)
             if u == 0:
-                nc.vector.tensor_copy(out=dealt[:], in_=turned[u][:].rearrange("j (m t) -> j t m", t=PACK))
-                pick(rs_win[LAST], rs_picked[:, LAST, half(1)], 1, False)
+                nc.vector.tensor_copy(out=y_dealt[:], in_=y_columns)
+                pick_rs(LAST, 1, False)
             else:
-                nc.scalar.copy(out=dealt[:], in_=turned[u][:].rearrange("j (m t) -> j t m", t=PACK))
+                nc.scalar.copy(out=y_dealt[:], in_=y_columns)
             for t in range(PACK):
-                nc.tensor.matmul(y_ps[u][:, t, :], lhsT=dealt[:, t, :], rhs=ident[:], is_transpose=True, start=False, stop=(t == PACK - 1))
+                nc.tensor.matmul(y_ps[u][:, t, :], lhsT=y_dealt[:, t, :], rhs=ident[:], is_transpose=True, start=False, stop=(t == LAST))
 
         w2w = keep.tile([P, 2 * N], U8, name="w2w", align_bytes=64)
         w2s = keep.tile([P, N], U8, name="w2s", align_bytes=64)
@@ -202,36 +217,18 @@ def tile_picked_clnorm_gelu_po_kernel(
         def by_token(ap):
             return ap.rearrange("p (c i) t -> p c t i", i=LINE)
 
-        normed = {}
-        z = {}
-        o_ps = {}
-        o_sb = {}
-
-        def buffer(name):
-            return keep.tile([P, PACK * UNIT], F32, name=name, align_bytes=64)
-
-        def as_tiles(buf):
-            return buf[:].rearrange("p (t j) -> p t j", t=PACK)
-
-        def as_tokens(buf):
-            return buf[:, 0 : PACK * UNIT // 2].bitcast(BF16).rearrange("p (j t) -> p j t", t=PACK)
-
-        def normalise(u, out):
-            normed[u] = out
-            nc.vector.tensor_tensor(out, rs_picked[:, :, cols(u)], y_ps[u][:], ALU.mult)
-
-        def activate(u, out):
-            z[u] = out
-            nc.scalar.activation(out=by_token(out), in_=by_tile(normed[u]), func=ACT.Gelu_apprx_tanh)
-
-        def second_product(u):
-            z_words = keep.tile([P, UNIT], U32, name=f"z_words{u}", tag=f"z_words{u}", align_bytes=64)
+        def second_layer(u):
+            normed = keep.tile([P, PACK, UNIT], F32, name=f"normed{u}", align_bytes=64)
+            nc.vector.tensor_tensor(normed[:], rs_picked[:, :, cols(u)], y_ps[u][:], ALU.mult)
+            z = keep.tile([P, UNIT, PACK], BF16, name=f"z{u}", align_bytes=64)
+            nc.scalar.activation(out=by_token(z[:]), in_=by_tile(normed[:]), func=ACT.Gelu_apprx_tanh)
+            z_words = keep.tile([P, UNIT], U32, name=f"z_words{u}", align_bytes=64)
             z_scales = keep.tile([P, UNIT], U8, name=f"z_scales{u}", align_bytes=64)
-            nc.vector.quantize_mx(out=z_words[:].bitcast(FP8X4), scales=z_scales[:], in_=z[u].rearrange("p j t -> p (j t)"))
-            o_ps[u] = psum.tile([P, PACK, UNIT], F32, name=f"o_ps{u}", tag=f"turned{u}")
+            nc.vector.quantize_mx(out=z_words[:].bitcast(FP8X4), scales=z_scales[:], in_=z[:].rearrange("p j t -> p (j t)"))
+            o_ps = psum.tile([P, PACK, UNIT], F32, name=f"o_ps{u}", tag=f"turned{u}")
             for t in range(PACK):
                 nc.tensor.matmul_mx(
-                    out=o_ps[u][:, t, :],
+                    out=o_ps[:, t, :],
                     lhsT=w2w[:, 2 * t * P : 2 * (t + 1) * P].bitcast(FP4X4),
                     lhsT_scale=w2s[:, t * P : (t + 1) * P],
                     rhs=z_words[:].bitcast(FP8X4),
@@ -239,33 +236,34 @@ def tile_picked_clnorm_gelu_po_kernel(
                     start=True,
                     stop=True,
                 )
+            return o_ps
 
-        def copy_result(u, out):
-            o_sb[u] = out
+        def store_and_round(u, o_ps):
+            o_sb = keep.tile([P, PACK, UNIT], F32, name=f"o_sb{u}", align_bytes=64)
             if u == 0:
-                nc.vector.tensor_copy(out=out, in_=o_ps[u][:])
+                nc.vector.tensor_copy(out=o_sb[:], in_=o_ps[:])
             else:
-                nc.scalar.copy(out=out, in_=o_ps[u][:])
-
-        def round_result(u):
-            nc.vector.tensor_copy(out=by_token(o_bf[:, cols(u), :]), in_=by_tile(o_sb[u]))
+                nc.scalar.copy(out=o_sb[:], in_=o_ps[:])
+            nc.sync.dma_start(out=out_rows[:, :, cols(u)], in_=o_sb[:])
+            nc.vector.tensor_copy(out=by_token(o_bf[:, cols(u), :]), in_=by_tile(o_sb[:]))
 
         def quantise_results(tokens):
             nc.vector.quantize_mx(
                 out=o_words[:, tokens].bitcast(FP8X4), scales=o_scales[:, tokens], in_=o_bf[:, tokens, :].rearrange("p j t -> p (j t)")
             )
+
+        def store_words(tokens):
             nc.sync.dma_start(out=out_words[:, tokens], in_=o_words[:, tokens])
 
-        for u in range(units):
-            normalise(u, as_tiles(buffer(f"normed{u}")))
-            activate(u, as_tokens(buffer(f"z{u}")))
-            second_product(u)
-        for h in range(halves):
-            for u in (2 * h, 2 * h + 1):
-                copy_result(u, as_tiles(buffer(f"o_sb{u}")))
-                nc.sync.dma_start(out=out_rows[:, :, cols(u)], in_=o_sb[u])
-                round_result(u)
-            quantise_results(half(h))
+        results = [second_layer(u) for u in range(UNITS)]
+        for u in range(UNITS // 2):
+            store_and_round(u, results[u])
+        quantise_results(half(0))
+        store_words(half(0))
+        for u in range(UNITS // 2, UNITS):
+            store_and_round(u, results[u])
+            quantise_results(cols(u))
+        store_words(half(1))
 
         for q in range(QUADS):
             (nc.scalar if q % 2 else nc.sync).dma_start(

@@ -28,16 +28,15 @@ HALF = S // 2
 HALVES = S // HALF
 LAST = PACK - 1
 LINE = 4
-EARLY_RS = 2
+MU_RS_BANKS = ((4, 6), (5, 7))
+RESULT_BANKS = (6, 7, 0, 3)
+PAIR = 2
 
 X_BYTES = 4 * T
-TABLE_BYTES = 4 * U
-AT_RS = PASSES * X_BYTES
-AT_W2_WORDS = AT_RS + (PACK - EARLY_RS) * TABLE_BYTES
+AT_W2_WORDS = X_BYTES
 AT_W2_SCALES = AT_W2_WORDS + 2 * N
-AT_W1_SCALES = AT_W2_SCALES + N
-AT_W1_WORDS = AT_W1_SCALES + PASSES * H
-LATE_BYTES = AT_W1_WORDS + 2 * H
+AT_W1_WORDS = AT_W2_SCALES + N
+LATE_BYTES = AT_W1_WORDS + PASSES * 2 * H
 
 
 def tile_picked_clnorm_gelu_po_kernel(
@@ -47,78 +46,68 @@ def tile_picked_clnorm_gelu_po_kernel(
     with ExitStack() as ctx:
         keep = ctx.enter_context(tc.tile_pool(name="keep", bufs=1))
         psum = ctx.enter_context(tc.psum_pool(name="psum", bufs=1))
+        rs_pool = ctx.enter_context(tc.tile_pool(name="rs_pool", bufs=1))
         late = ctx.enter_context(tc.tile_pool(name="late", bufs=1))
 
         offs_sb = keep.tile([P, S // LIST_ROWS], U16, name="offs_sb")
         cl_sb = keep.tile([P, S // LIST_ROWS], U16, name="cl_sb")
         xs_tile = late.tile([P, LATE_BYTES], U8, name="xs_tile", offset=0, align_bytes=64)
         xs_picked = keep.tile([P, S], U8, name="xs_picked", align_bytes=64)
-        w1w = [keep.tile([P, 2 * H], U8, name="w1w0", align_bytes=64)]
         x_planes = keep.tile([P, PASSES * S], U8, name="x_planes", align_bytes=64)
         mu_win = [keep.tile([P, U], F32, name=f"mu_win{t}", tag=f"mu_win{t}", align_bytes=64) for t in range(PACK)]
-        rs_win = [keep.tile([P, U], F32, name=f"rs_win{t}", align_bytes=64) for t in range(EARLY_RS)]
+        rs_win = [rs_pool.tile([P, U], F32, name=f"rs_win{t}", offset=4 * U * t + (2 * U if t == LAST else 0)) for t in range(PACK)]
 
         nc.vector.memset(xs_tile[32:64, 0:T].bitcast(I32), 0)
         nc.vector.memset(xs_tile[64:128, 0:T].bitcast(I32), 0)
         ident = keep.tile([P, P], F32, name="ident", align_bytes=64)
         make_identity(nc, ident[:])
+        w1s = keep.tile([P, PASSES * H], U8, name="w1s", align_bytes=64)
+        nc.gpsimd.memset(w1s[:].bitcast(I32), 0)
         nc.gpsimd.memset(x_planes[:].bitcast(I32), 0)
 
         warm = keep.tile([P, 2], F32, name="warm")
         nc.vector.memset(warm[:, 0:1], 0.0)
         nc.scalar.activation(out=warm[:, 1:2], in_=warm[:, 0:1], func=ACT.Gelu_apprx_tanh)
 
+        def load_scale_rows(plane, scales, q):
+            nc.sync.dma_start(
+                out=plane[32 * q : 32 * q + 4, :].bitcast(I32).rearrange("r (g c) -> r g c", g=scales.shape[0]),
+                in_=scales[:, 4 * q : 4 * q + 4, :].bitcast(I32).rearrange("g r c -> r g c"),
+            )
+
         def load_x(g):
             nc.sync.dma_start(out=x_win[g][:], in_=x_words[g].rearrange("p n t -> p (n t)").bitcast(I32))
-
-        def load_w1_words(g):
-            nc.sync.dma_start(out=w1w[g][:].bitcast(I32), in_=w1_words[g].bitcast(I32))
-
-        def load_scale_rows(plane, scales):
-            for q in range(QUADS):
-                nc.sync.dma_start(
-                    out=plane[32 * q : 32 * q + 4, :].bitcast(I32).rearrange("r (g c) -> r g c", g=scales.shape[0]),
-                    in_=scales[:, 4 * q : 4 * q + 4, :].bitcast(I32).rearrange("g r c -> r g c"),
-                )
 
         mu_rows = mu.rearrange("(p t) u -> p t u", t=PACK)
         rs_rows = rs.rearrange("(p t) u -> p t u", t=PACK)
 
-        def load_table(win, rows, t):
-            nc.sync.dma_start(out=win[t][:], in_=rows[:, t, :])
-
         nc.sync.dma_start(offs_sb[:], offs)
         nc.sync.dma_start(out=xs_tile[0:32, 0:T].bitcast(I32), in_=x_scales.bitcast(I32).rearrange("g a c -> a g c"))
         nc.sync.dma_start(cl_sb[:], cl)
-        for t in range(PACK):
-            load_table(mu_win, mu_rows, t)
-            if t == 1:
-                load_w1_words(0)
-        for t in range(EARLY_RS):
-            load_table(rs_win, rs_rows, t)
+        tables = [(win[t], rows[:, t, :]) for t in range(PACK) for win, rows in ((rs_win, rs_rows), (mu_win, mu_rows))]
+        for n, (win, rows) in enumerate(tables):
+            nc.sync.dma_start(out=win[:], in_=rows)
+            if n >= len(tables) - QUADS:
+                load_scale_rows(w1s, w1_scales, n - len(tables) + QUADS)
+        x_win = [keep.tile([P, T], I32, name="x_win0")]
+        load_x(0)
         nc.vector.tensor_copy(out=xs_picked[:], in_=xs_tile[:, 0:T].indirect(offs_sb[:]))
         for q in range(QUADS):
             nc.sync.dma_start(
                 out=x_planes[32 * q : 32 * q + 4, :].bitcast(I32).rearrange("r (g c) -> r g c", g=PASSES),
                 in_=xs_picked[8 * q : 8 * q + 8, :].bitcast(I32),
             )
-        x_win = [late.tile([P, T], I32, name=f"x_win{g}", offset=X_BYTES * g) for g in range(PASSES)]
-        w1s = late.tile([P, PASSES * H], U8, name="w1s", offset=AT_W1_SCALES, align_bytes=64)
-        nc.gpsimd.memset(w1s[:].bitcast(I32), 0)
-        for t in range(EARLY_RS, PACK):
-            rs_win.append(late.tile([P, U], F32, name=f"rs_win{t}", offset=AT_RS + TABLE_BYTES * (t - EARLY_RS)))
-        load_x(0)
-        load_scale_rows(w1s, w1_scales)
-        load_table(rs_win, rs_rows, EARLY_RS)
+        x_win.append(late.tile([P, T], I32, name="x_win1", offset=0))
+        w1w = [late.tile([P, 2 * H], U8, name=f"w1w{g}", offset=AT_W1_WORDS + 2 * H * g, align_bytes=64) for g in range(PASSES)]
+        nc.sync.dma_start(out=w1w[0][:].bitcast(I32), in_=w1_words[0].bitcast(I32))
         load_x(1)
-        w1w.append(late.tile([P, 2 * H], U8, name="w1w1", offset=AT_W1_WORDS, align_bytes=64))
-        load_w1_words(1)
-        load_table(rs_win, rs_rows, LAST)
+        nc.sync.dma_start(out=w1w[1][:].bitcast(I32), in_=w1_words[1].bitcast(I32))
         w2w_raw = late.tile([P, 2 * N], U8, name="w2w_raw", offset=AT_W2_WORDS)
         w2s_raw = late.tile([P, N], U8, name="w2s_raw", offset=AT_W2_SCALES)
         nc.gpsimd.memset(w2s_raw[:].bitcast(I32), 0)
         nc.sync.dma_start(out=w2w_raw[:].bitcast(I32), in_=w2_words[0].bitcast(I32))
-        load_scale_rows(w2s_raw, w2_scales)
+        for q in range(QUADS):
+            load_scale_rows(w2s_raw, w2_scales, q)
 
         def cols(u):
             return slice(u * UNIT, (u + 1) * UNIT)
@@ -129,31 +118,66 @@ def tile_picked_clnorm_gelu_po_kernel(
         def entries(lists, tokens):
             return lists[:, tokens.start // LIST_ROWS : tokens.stop // LIST_ROWS]
 
-        y_ps = [psum.tile([P, PACK, UNIT], F32, name=f"y_ps{u}", tag=f"y_ps{u}") for u in range(UNITS)]
+        negated = {}
+        rs_banks = {}
+        y_ps = []
 
-        def pick(win, out, h, on_scalar):
-            looked_up = win[:].indirect(entries(cl_sb, half(h)))
-            if on_scalar:
-                nc.scalar.activation(out=out, in_=looked_up, func=ACT.Copy)
+        def open_unit(u, bank):
+            y_ps.append(psum.tile([P, PACK, UNIT], F32, name=f"y_ps{u}", tag=f"bank{bank}"))
+
+        def add_negated(u, k):
+            for i in range(PAIR):
+                t = PAIR * k + i
+                nc.tensor.matmul(
+                    y_ps[u][:, t, :], lhsT=negated[k, u // PAIR][:, u % PAIR, i, :], rhs=ident[:], is_transpose=True, start=(t == 0), stop=False
+                )
+
+        rs_turned = rs_pool.tile([P, UNITS, PACK, P], F32, name="rs_turned", offset=0)
+
+        def turn(picked, h, name, slot):
+            bank = psum.tile([P, PAIR, PAIR, P], F32, name=name, tag=f"bank{slot}")
+            for i in range(PAIR):
+                for v in range(PAIR):
+                    nc.tensor.transpose(bank[:, v, i, :], picked[i][:, cols(PAIR * h + v)], ident[:])
+            return bank
+
+        mu_rs_banks = {}
+
+        def negate(k, h, on_vector):
+            if (k, h) == (0, 0):
+                negated[k, h] = rs_pool.tile([P, PAIR, PAIR, P], F32, name="negated00", offset=4 * U * PACK)
+            elif (k, h) == (0, 1):
+                negated[k, h] = keep.tile([P, PAIR, PAIR, P], F32, name="negated01", tag=f"mu_win{LAST}", align_bytes=64)
             else:
-                nc.vector.tensor_copy(out=out, in_=looked_up)
+                negated[k, h] = keep.tile([P, PAIR, PAIR, P], F32, name=f"negated{k}{h}", align_bytes=64)
+            if on_vector:
+                nc.vector.tensor_scalar(negated[k, h][:], mu_rs_banks[k, h][:], -1.0, None, ALU.mult)
+            else:
+                nc.scalar.activation(out=negated[k, h][:], in_=mu_rs_banks[k, h][:], func=ACT.Copy, scale=-1.0)
 
-        def pick_mu(t):
-            picked = keep.tile([P, S], F32, name=f"mu_picked{t}", align_bytes=64)
+        for k in range(PACK // PAIR):
+            tiles = range(PAIR * k, PAIR * (k + 1))
+            rs_picked = [keep.tile([P, S], F32, name=f"rs_picked{t}", align_bytes=64) for t in tiles]
+            mu_rs = [keep.tile([P, S], F32, name=f"mu_rs{t}", align_bytes=64) for t in tiles]
+            for i, t in enumerate(tiles):
+                for h in range(HALVES):
+                    nc.scalar.activation(out=rs_picked[i][:, half(h)], in_=rs_win[t][:].indirect(entries(cl_sb, half(h))), func=ACT.Copy)
+                for h in range(HALVES):
+                    nc.vector.tensor_tensor(mu_rs[i][:, half(h)], mu_win[t][:].indirect(entries(cl_sb, half(h))), rs_picked[i][:, half(h)], ALU.mult)
             for h in range(HALVES):
-                pick(mu_win[t], picked[:, half(h)], h, t % 2 == 0)
-            bank = psum.tile([P, UNITS, P], F32, name=f"mu_ps{t}", tag=f"turned{t}")
-            for u in range(UNITS):
-                nc.tensor.transpose(bank[:, u, :], picked[:, cols(u)], ident[:])
-            neg_mu = keep.tile([P, UNITS, P], F32, name=f"neg_mu{t}", tag=("mu_win2" if t == 0 else f"neg_mu{t}"), align_bytes=64)
-            nc.scalar.activation(out=neg_mu[:], in_=bank[:], func=ACT.Copy, scale=-1.0)
-            for u in range(UNITS):
-                nc.tensor.matmul(y_ps[u][:, t, :], lhsT=neg_mu[:, u, :], rhs=ident[:], is_transpose=True, start=(t == 0), stop=False)
-
-        rs_picked = keep.tile([P, PACK, S], F32, name="rs_picked", align_bytes=64)
-
-        def pick_rs(t, h, on_scalar):
-            pick(rs_win[t], rs_picked[:, t, half(h)], h, on_scalar)
+                rs_banks[k, h] = turn(rs_picked, h, f"rs_ps{k}{h}", PAIR * h + k)
+                mu_rs_banks[k, h] = turn(mu_rs, h, f"mu_rs_ps{k}{h}", MU_RS_BANKS[k][h])
+        for k in range(PACK // PAIR):
+            negate(k, 0, k == 1)
+        for u in range(PAIR):
+            open_unit(u, UNITS + u)
+            for k in range(PACK // PAIR):
+                add_negated(u, k)
+        for h in range(HALVES):
+            for k in range(PACK // PAIR):
+                nc.scalar.copy(out=rs_turned[:, PAIR * h : PAIR * (h + 1), PAIR * k : PAIR * (k + 1), :], in_=rs_banks[k, h][:])
+        for k in range(PACK // PAIR):
+            negate(k, 1, False)
 
         x_picked = [keep.tile([P, S], U32, name=f"x_picked{g}", align_bytes=64) for g in range(PASSES)]
 
@@ -162,16 +186,10 @@ def tile_picked_clnorm_gelu_po_kernel(
                 tokens = slice(lo, lo + step)
                 nc.vector.tensor_copy(out=x_picked[g][:, tokens], in_=x_win[g][:].bitcast(U32).indirect(entries(offs_sb, tokens)))
 
-        for t in range(PACK):
-            pick_mu(t)
-        for t in range(LAST):
-            for h in range(HALVES):
-                pick_rs(t, h, (t, h) == (EARLY_RS - 1, HALVES - 1))
         pick_x(0, HALF)
         pick_x(1, UNIT)
-        pick_rs(LAST, 0, True)
 
-        turned = [psum.tile([P, H], F32, name=f"turned{u}", tag=f"turned{u}") for u in range(UNITS)]
+        turned = [psum.tile([P, H], F32, name=f"turned{u}", tag=f"bank{u}") for u in range(UNITS)]
         for g in range(PASSES):
             for u in range(UNITS):
                 nc.tensor.matmul_mx(
@@ -184,15 +202,14 @@ def tile_picked_clnorm_gelu_po_kernel(
                     stop=(g == PASSES - 1),
                 )
         for u in range(UNITS):
-            y_dealt = keep.tile([P, PACK, P], F32, name=f"y_dealt{u}", align_bytes=64)
-            y_columns = turned[u][:].rearrange("j (m t) -> j t m", t=PACK)
-            if u == 0:
-                nc.vector.tensor_copy(out=y_dealt[:], in_=y_columns)
-                pick_rs(LAST, 1, False)
-            else:
-                nc.scalar.copy(out=y_dealt[:], in_=y_columns)
+            y_rs = keep.tile([P, PACK, P], F32, name=f"y_rs{u}", align_bytes=64)
+            nc.vector.tensor_tensor(y_rs[:], rs_turned[:, u, :, :], turned[u][:].rearrange("j (m t) -> j t m", t=PACK), ALU.mult)
             for t in range(PACK):
-                nc.tensor.matmul(y_ps[u][:, t, :], lhsT=y_dealt[:, t, :], rhs=ident[:], is_transpose=True, start=False, stop=(t == LAST))
+                nc.tensor.matmul(y_ps[u][:, t, :], lhsT=y_rs[:, t, :], rhs=ident[:], is_transpose=True, start=False, stop=(t == LAST))
+            if 0 < u < UNITS - 1:
+                open_unit(u + 1, u)
+                for k in range(PACK // PAIR):
+                    add_negated(u + 1, k)
 
         w2w = keep.tile([P, 2 * N], U8, name="w2w", align_bytes=64)
         w2s = keep.tile([P, N], U8, name="w2s", align_bytes=64)
@@ -218,14 +235,12 @@ def tile_picked_clnorm_gelu_po_kernel(
             return ap.rearrange("p (c i) t -> p c t i", i=LINE)
 
         def second_layer(u):
-            normed = keep.tile([P, PACK, UNIT], F32, name=f"normed{u}", align_bytes=64)
-            nc.vector.tensor_tensor(normed[:], rs_picked[:, :, cols(u)], y_ps[u][:], ALU.mult)
             z = keep.tile([P, UNIT, PACK], BF16, name=f"z{u}", align_bytes=64)
-            nc.scalar.activation(out=by_token(z[:]), in_=by_tile(normed[:]), func=ACT.Gelu_apprx_tanh)
-            z_words = keep.tile([P, UNIT], U32, name=f"z_words{u}", align_bytes=64)
+            nc.scalar.activation(out=by_token(z[:]), in_=by_tile(y_ps[u][:]), func=ACT.Gelu_apprx_tanh)
+            z_words = keep.tile([P, UNIT], U32, name=f"z_words{u}", tag=f"z_words{u % (UNITS - 1)}", align_bytes=64)
             z_scales = keep.tile([P, UNIT], U8, name=f"z_scales{u}", align_bytes=64)
             nc.vector.quantize_mx(out=z_words[:].bitcast(FP8X4), scales=z_scales[:], in_=z[:].rearrange("p j t -> p (j t)"))
-            o_ps = psum.tile([P, PACK, UNIT], F32, name=f"o_ps{u}", tag=f"turned{u}")
+            o_ps = psum.tile([P, PACK, UNIT], F32, name=f"o_ps{u}", tag=f"bank{RESULT_BANKS[u]}")
             for t in range(PACK):
                 nc.tensor.matmul_mx(
                     out=o_ps[:, t, :],
@@ -238,14 +253,18 @@ def tile_picked_clnorm_gelu_po_kernel(
                 )
             return o_ps
 
-        def store_and_round(u, o_ps):
-            o_sb = keep.tile([P, PACK, UNIT], F32, name=f"o_sb{u}", align_bytes=64)
+        o_sb = []
+
+        def store(u):
+            o_sb.append(keep.tile([P, PACK, UNIT], F32, name=f"o_sb{u}", align_bytes=64))
             if u == 0:
-                nc.vector.tensor_copy(out=o_sb[:], in_=o_ps[:])
+                nc.vector.tensor_copy(out=o_sb[u][:], in_=results[u][:])
             else:
-                nc.scalar.copy(out=o_sb[:], in_=o_ps[:])
-            nc.sync.dma_start(out=out_rows[:, :, cols(u)], in_=o_sb[:])
-            nc.vector.tensor_copy(out=by_token(o_bf[:, cols(u), :]), in_=by_tile(o_sb[:]))
+                nc.scalar.copy(out=o_sb[u][:], in_=results[u][:])
+            nc.sync.dma_start(out=out_rows[:, :, cols(u)], in_=o_sb[u][:])
+
+        def round_result(u):
+            nc.vector.tensor_copy(out=by_token(o_bf[:, cols(u), :]), in_=by_tile(o_sb[u][:]))
 
         def quantise_results(tokens):
             nc.vector.quantize_mx(
@@ -255,13 +274,17 @@ def tile_picked_clnorm_gelu_po_kernel(
         def store_words(tokens):
             nc.sync.dma_start(out=out_words[:, tokens], in_=o_words[:, tokens])
 
-        results = [second_layer(u) for u in range(UNITS)]
-        for u in range(UNITS // 2):
-            store_and_round(u, results[u])
+        results = [second_layer(u) for u in range(UNITS - 1)]
+        store(0)
+        results.append(second_layer(UNITS - 1))
+        round_result(0)
+        store(1)
+        round_result(1)
         quantise_results(half(0))
         store_words(half(0))
-        for u in range(UNITS // 2, UNITS):
-            store_and_round(u, results[u])
+        for u in range(PAIR, UNITS):
+            store(u)
+            round_result(u)
             quantise_results(cols(u))
         store_words(half(1))
 

@@ -29,14 +29,11 @@ HALVES = S // HALF
 LAST = PACK - 1
 LINE = 4
 MU_RS_BANKS = ((4, 6), (5, 7))
-RESULT_BANKS = (6, 7, 0, 3)
+RESULT_BANKS = (6, 7, 1, 0)
+SHARED = 2
+ORDER = (0, SHARED, 1, 3)
+DONE = (0, 1, 3, SHARED)
 PAIR = 2
-
-X_BYTES = 4 * T
-AT_W2_WORDS = X_BYTES
-AT_W2_SCALES = AT_W2_WORDS + 2 * N
-AT_W1_WORDS = AT_W2_SCALES + N
-LATE_BYTES = AT_W1_WORDS + PASSES * 2 * H
 
 
 def tile_picked_clnorm_gelu_po_kernel(
@@ -47,23 +44,29 @@ def tile_picked_clnorm_gelu_po_kernel(
         keep = ctx.enter_context(tc.tile_pool(name="keep", bufs=1))
         psum = ctx.enter_context(tc.psum_pool(name="psum", bufs=1))
         rs_pool = ctx.enter_context(tc.tile_pool(name="rs_pool", bufs=1))
-        late = ctx.enter_context(tc.tile_pool(name="late", bufs=1))
+        mu_pool = ctx.enter_context(tc.tile_pool(name="mu_pool", bufs=1))
 
         offs_sb = keep.tile([P, S // LIST_ROWS], U16, name="offs_sb")
         cl_sb = keep.tile([P, S // LIST_ROWS], U16, name="cl_sb")
-        xs_tile = late.tile([P, LATE_BYTES], U8, name="xs_tile", offset=0, align_bytes=64)
+        xs_win = keep.tile([P, T], U8, name="xs_win", align_bytes=64)
         xs_picked = keep.tile([P, S], U8, name="xs_picked", align_bytes=64)
         x_planes = keep.tile([P, PASSES * S], U8, name="x_planes", align_bytes=64)
-        mu_win = [keep.tile([P, U], F32, name=f"mu_win{t}", tag=f"mu_win{t}", align_bytes=64) for t in range(PACK)]
+        w1s = keep.tile([P, PASSES * H], U8, name="w1s", align_bytes=64)
+        w2s_raw = keep.tile([P, N], U8, name="w2s_raw", align_bytes=64)
+        w1w = [keep.tile([P, 2 * H], U8, name=f"w1w{g}", align_bytes=64) for g in range(PASSES)]
+        w2w_raw = keep.tile([P, 2 * N], U8, name="w2w_raw", align_bytes=64)
+        x_win = [keep.tile([P, T], I32, name=f"x_win{g}") for g in range(PASSES)]
+        mu_win = [keep.tile([P, U], F32, name=f"mu_win{t}", align_bytes=64) for t in range(LAST)]
+        mu_win.append(mu_pool.tile([P, U], F32, name=f"mu_win{LAST}", offset=0, align_bytes=64))
         rs_win = [rs_pool.tile([P, U], F32, name=f"rs_win{t}", offset=4 * U * t + (2 * U if t == LAST else 0)) for t in range(PACK)]
 
-        nc.vector.memset(xs_tile[32:64, 0:T].bitcast(I32), 0)
-        nc.vector.memset(xs_tile[64:128, 0:T].bitcast(I32), 0)
+        nc.vector.memset(xs_win[32:64, :].bitcast(I32), 0)
+        nc.vector.memset(xs_win[64:128, :].bitcast(I32), 0)
+        nc.gpsimd.memset(w1s[:].bitcast(I32), 0)
         ident = keep.tile([P, P], F32, name="ident", align_bytes=64)
         make_identity(nc, ident[:])
-        w1s = keep.tile([P, PASSES * H], U8, name="w1s", align_bytes=64)
-        nc.gpsimd.memset(w1s[:].bitcast(I32), 0)
         nc.gpsimd.memset(x_planes[:].bitcast(I32), 0)
+        nc.gpsimd.memset(w2s_raw[:].bitcast(I32), 0)
 
         warm = keep.tile([P, 2], F32, name="warm")
         nc.vector.memset(warm[:, 0:1], 0.0)
@@ -75,39 +78,42 @@ def tile_picked_clnorm_gelu_po_kernel(
                 in_=scales[:, 4 * q : 4 * q + 4, :].bitcast(I32).rearrange("g r c -> r g c"),
             )
 
-        def load_x(g):
-            nc.sync.dma_start(out=x_win[g][:], in_=x_words[g].rearrange("p n t -> p (n t)").bitcast(I32))
-
-        mu_rows = mu.rearrange("(p t) u -> p t u", t=PACK)
-        rs_rows = rs.rearrange("(p t) u -> p t u", t=PACK)
-
-        nc.sync.dma_start(offs_sb[:], offs)
-        nc.sync.dma_start(out=xs_tile[0:32, 0:T].bitcast(I32), in_=x_scales.bitcast(I32).rearrange("g a c -> a g c"))
-        nc.sync.dma_start(cl_sb[:], cl)
-        tables = [(win[t], rows[:, t, :]) for t in range(PACK) for win, rows in ((rs_win, rs_rows), (mu_win, mu_rows))]
-        for n, (win, rows) in enumerate(tables):
-            nc.sync.dma_start(out=win[:], in_=rows)
-            if n >= len(tables) - QUADS:
-                load_scale_rows(w1s, w1_scales, n - len(tables) + QUADS)
-        x_win = [keep.tile([P, T], I32, name="x_win0")]
-        load_x(0)
-        nc.vector.tensor_copy(out=xs_picked[:], in_=xs_tile[:, 0:T].indirect(offs_sb[:]))
-        for q in range(QUADS):
+        def move_scale_rows(q):
             nc.sync.dma_start(
                 out=x_planes[32 * q : 32 * q + 4, :].bitcast(I32).rearrange("r (g c) -> r g c", g=PASSES),
                 in_=xs_picked[8 * q : 8 * q + 8, :].bitcast(I32),
             )
-        x_win.append(late.tile([P, T], I32, name="x_win1", offset=0))
-        w1w = [late.tile([P, 2 * H], U8, name=f"w1w{g}", offset=AT_W1_WORDS + 2 * H * g, align_bytes=64) for g in range(PASSES)]
-        nc.sync.dma_start(out=w1w[0][:].bitcast(I32), in_=w1_words[0].bitcast(I32))
-        load_x(1)
-        nc.sync.dma_start(out=w1w[1][:].bitcast(I32), in_=w1_words[1].bitcast(I32))
-        w2w_raw = late.tile([P, 2 * N], U8, name="w2w_raw", offset=AT_W2_WORDS)
-        w2s_raw = late.tile([P, N], U8, name="w2s_raw", offset=AT_W2_SCALES)
-        nc.gpsimd.memset(w2s_raw[:].bitcast(I32), 0)
-        nc.sync.dma_start(out=w2w_raw[:].bitcast(I32), in_=w2_words[0].bitcast(I32))
+
+        def load_x(g):
+            nc.sync.dma_start(out=x_win[g][:], in_=x_words[g].rearrange("p n t -> p (n t)").bitcast(I32))
+
+        def load_w1_words(g):
+            nc.sync.dma_start(out=w1w[g][:].bitcast(I32), in_=w1_words[g].bitcast(I32))
+
+        mu_rows = mu.rearrange("(p t) u -> p t u", t=PACK)
+        rs_rows = rs.rearrange("(p t) u -> p t u", t=PACK)
+        tables = [(win[t], rows[:, t, :]) for t in range(PACK) for win, rows in ((rs_win, rs_rows), (mu_win, mu_rows))]
+
+        nc.sync.dma_start(offs_sb[:], offs)
+        nc.sync.dma_start(out=xs_win[0:32, :].bitcast(I32), in_=x_scales.bitcast(I32).rearrange("g a c -> a g c"))
+        nc.sync.dma_start(cl_sb[:], cl)
+        nc.vector.tensor_copy(out=xs_picked[:], in_=xs_win[:].indirect(offs_sb[:]))
+        for n, (win, rows) in enumerate(tables):
+            nc.sync.dma_start(out=win[:], in_=rows)
+            if 1 <= n <= QUADS:
+                load_scale_rows(w1s, w1_scales, n - 1)
+            elif n == QUADS + 1:
+                load_w1_words(0)
+            elif n > QUADS + 1:
+                move_scale_rows(n - QUADS - 2)
+        load_x(0)
+        for q in range(len(tables) - QUADS - 2, QUADS):
+            move_scale_rows(q)
         for q in range(QUADS):
             load_scale_rows(w2s_raw, w2_scales, q)
+        load_x(1)
+        load_w1_words(1)
+        nc.sync.dma_start(out=w2w_raw[:].bitcast(I32), in_=w2_words[0].bitcast(I32))
 
         def cols(u):
             return slice(u * UNIT, (u + 1) * UNIT)
@@ -120,10 +126,10 @@ def tile_picked_clnorm_gelu_po_kernel(
 
         negated = {}
         rs_banks = {}
-        y_ps = []
+        y_ps = {}
 
         def open_unit(u, bank):
-            y_ps.append(psum.tile([P, PACK, UNIT], F32, name=f"y_ps{u}", tag=f"bank{bank}"))
+            y_ps[u] = psum.tile([P, PACK, UNIT], F32, name=f"y_ps{u}", tag=f"bank{bank}")
 
         def add_negated(u, k):
             for i in range(PAIR):
@@ -147,7 +153,7 @@ def tile_picked_clnorm_gelu_po_kernel(
             if (k, h) == (0, 0):
                 negated[k, h] = rs_pool.tile([P, PAIR, PAIR, P], F32, name="negated00", offset=4 * U * PACK)
             elif (k, h) == (0, 1):
-                negated[k, h] = keep.tile([P, PAIR, PAIR, P], F32, name="negated01", tag=f"mu_win{LAST}", align_bytes=64)
+                negated[k, h] = mu_pool.tile([P, PAIR, PAIR, P], F32, name="negated01", offset=N, align_bytes=64)
             else:
                 negated[k, h] = keep.tile([P, PAIR, PAIR, P], F32, name=f"negated{k}{h}", align_bytes=64)
             if on_vector:
@@ -181,17 +187,17 @@ def tile_picked_clnorm_gelu_po_kernel(
 
         x_picked = [keep.tile([P, S], U32, name=f"x_picked{g}", align_bytes=64) for g in range(PASSES)]
 
-        def pick_x(g, step):
-            for lo in range(0, S, step):
-                tokens = slice(lo, lo + step)
+        def pick_x(g, order, step):
+            for i in order:
+                tokens = slice(i * step, (i + 1) * step)
                 nc.vector.tensor_copy(out=x_picked[g][:, tokens], in_=x_win[g][:].bitcast(U32).indirect(entries(offs_sb, tokens)))
 
-        pick_x(0, HALF)
-        pick_x(1, UNIT)
+        pick_x(0, range(HALVES), HALF)
+        pick_x(1, ORDER, UNIT)
 
         turned = [psum.tile([P, H], F32, name=f"turned{u}", tag=f"bank{u}") for u in range(UNITS)]
         for g in range(PASSES):
-            for u in range(UNITS):
+            for u in ORDER if g == PASSES - 1 else range(UNITS):
                 nc.tensor.matmul_mx(
                     out=turned[u][:],
                     lhsT=x_picked[g][:, cols(u)].bitcast(FP8X4),
@@ -201,18 +207,26 @@ def tile_picked_clnorm_gelu_po_kernel(
                     start=(g == 0),
                     stop=(g == PASSES - 1),
                 )
-        for u in range(UNITS):
-            y_rs = keep.tile([P, PACK, P], F32, name=f"y_rs{u}", align_bytes=64)
-            nc.vector.tensor_tensor(y_rs[:], rs_turned[:, u, :, :], turned[u][:].rearrange("j (m t) -> j t m", t=PACK), ALU.mult)
-            for t in range(PACK):
-                nc.tensor.matmul(y_ps[u][:, t, :], lhsT=y_rs[:, t, :], rhs=ident[:], is_transpose=True, start=False, stop=(t == LAST))
-            if 0 < u < UNITS - 1:
-                open_unit(u + 1, u)
+        y_rs = [keep.tile([P, PACK, P], F32, name=f"y_rs{u}", align_bytes=64) for u in range(UNITS)]
+
+        def y_columns(u):
+            return turned[u][:].rearrange("j (m t) -> j t m", t=PACK)
+
+        y_dealt = keep.tile([P, PACK, P], F32, name="y_dealt", align_bytes=64)
+        nc.scalar.copy(out=y_dealt[:], in_=y_columns(SHARED))
+        nc.gpsimd.tensor_tensor(y_rs[SHARED][:], y_dealt[:], rs_turned[:, SHARED, :, :], ALU.mult)
+        for u in DONE:
+            if u != SHARED:
+                nc.vector.tensor_tensor(y_rs[u][:], rs_turned[:, u, :, :], y_columns(u), ALU.mult)
+            if u >= PAIR:
+                open_unit(u, SHARED + UNITS - 1 - u)
                 for k in range(PACK // PAIR):
-                    add_negated(u + 1, k)
+                    add_negated(u, k)
+            for t in range(PACK):
+                nc.tensor.matmul(y_ps[u][:, t, :], lhsT=y_rs[u][:, t, :], rhs=ident[:], is_transpose=True, start=False, stop=(t == LAST))
 
         w2w = keep.tile([P, 2 * N], U8, name="w2w", align_bytes=64)
-        w2s = keep.tile([P, N], U8, name="w2s", align_bytes=64)
+        w2s = mu_pool.tile([P, N], U8, name="w2s", offset=0, align_bytes=64)
         nc.gpsimd.tensor_copy(
             out=w2w[:].bitcast(U16).rearrange("p (t m) -> p t m", t=PACK),
             in_=w2w_raw[:].bitcast(U16).rearrange("p (m t) -> p t m", t=PACK),
@@ -237,7 +251,7 @@ def tile_picked_clnorm_gelu_po_kernel(
         def second_layer(u):
             z = keep.tile([P, UNIT, PACK], BF16, name=f"z{u}", align_bytes=64)
             nc.scalar.activation(out=by_token(z[:]), in_=by_tile(y_ps[u][:]), func=ACT.Gelu_apprx_tanh)
-            z_words = keep.tile([P, UNIT], U32, name=f"z_words{u}", tag=f"z_words{u % (UNITS - 1)}", align_bytes=64)
+            z_words = keep.tile([P, UNIT], U32, name=f"z_words{u}", tag=f"z_words{0 if u == SHARED else u}", align_bytes=64)
             z_scales = keep.tile([P, UNIT], U8, name=f"z_scales{u}", align_bytes=64)
             nc.vector.quantize_mx(out=z_words[:].bitcast(FP8X4), scales=z_scales[:], in_=z[:].rearrange("p j t -> p (j t)"))
             o_ps = psum.tile([P, PACK, UNIT], F32, name=f"o_ps{u}", tag=f"bank{RESULT_BANKS[u]}")
@@ -253,10 +267,10 @@ def tile_picked_clnorm_gelu_po_kernel(
                 )
             return o_ps
 
-        o_sb = []
+        o_sb = {}
 
         def store(u):
-            o_sb.append(keep.tile([P, PACK, UNIT], F32, name=f"o_sb{u}", align_bytes=64))
+            o_sb[u] = keep.tile([P, PACK, UNIT], F32, name=f"o_sb{u}", align_bytes=64)
             if u == 0:
                 nc.vector.tensor_copy(out=o_sb[u][:], in_=results[u][:])
             else:
@@ -274,15 +288,15 @@ def tile_picked_clnorm_gelu_po_kernel(
         def store_words(tokens):
             nc.sync.dma_start(out=out_words[:, tokens], in_=o_words[:, tokens])
 
-        results = [second_layer(u) for u in range(UNITS - 1)]
+        results = {u: second_layer(u) for u in DONE[:-1]}
         store(0)
-        results.append(second_layer(UNITS - 1))
+        results[SHARED] = second_layer(SHARED)
         round_result(0)
         store(1)
         round_result(1)
         quantise_results(half(0))
         store_words(half(0))
-        for u in range(PAIR, UNITS):
+        for u in DONE[PAIR:]:
             store(u)
             round_result(u)
             quantise_results(cols(u))

from contextlib import ExitStack

import concourse.mybir as mybir
from concourse.masks import make_identity

F32 = mybir.dt.float32
BF16 = mybir.dt.bfloat16
I32 = mybir.dt.int32
U32 = mybir.dt.uint32
U16 = mybir.dt.uint16
U8 = mybir.dt.uint8
FP8X4 = mybir.dt.float8_e4m3fn_x4
FP4X4 = mybir.dt.float4_e2m1fn_x4
ALU = mybir.AluOpType
ACT = mybir.ActivationFunctionType

K, T, S, N, H, U = 1024, 2048, 512, 512, 512, 512
FLOPS = 2 * K * H * S + 2 * H * N * S

P = 128
PACK = 4
PASSES = K // (P * PACK)
QUADS = 4
LIST_ROWS = 16
UNIT = 128
UNITS = S // UNIT
HALF = S // 2
HALVES = S // HALF
LAST = PACK - 1
LINE = 4
MU_RS_BANKS = ((4, 6), (5, 7))
RESULT_BANKS = (6, 7, 1, 0)
SHARED = 2
ORDER = (0, SHARED, 1, 3)
DONE = (0, 1, 3, SHARED)
PAIR = 2


def tile_picked_clnorm_gelu_po_kernel(
    tc, x_words, x_scales, w1_words, w1_scales, mu, rs, w2_words, w2_scales, offs, cl, out_0, out_1, out_2
):
    nc = tc.nc
    with ExitStack() as ctx:
        keep = ctx.enter_context(tc.tile_pool(name="keep", bufs=1))
        psum = ctx.enter_context(tc.psum_pool(name="psum", bufs=1))
        rs_pool = ctx.enter_context(tc.tile_pool(name="rs_pool", bufs=1))
        mu_pool = ctx.enter_context(tc.tile_pool(name="mu_pool", bufs=1))

        offs_sb = keep.tile([P, S // LIST_ROWS], U16, name="offs_sb")
        cl_sb = keep.tile([P, S // LIST_ROWS], U16, name="cl_sb")
        xs_win = keep.tile([P, T], U8, name="xs_win", align_bytes=64)
        xs_picked = keep.tile([P, S], U8, name="xs_picked", align_bytes=64)
        x_planes = keep.tile([P, PASSES * S], U8, name="x_planes", align_bytes=64)
        w1s = keep.tile([P, PASSES * H], U8, name="w1s", align_bytes=64)
        w2s_raw = keep.tile([P, N], U8, name="w2s_raw", align_bytes=64)
        w1w = [keep.tile([P, 2 * H], U8, name=f"w1w{g}", align_bytes=64) for g in range(PASSES)]
        w2w_raw = keep.tile([P, 2 * N], U8, name="w2w_raw", align_bytes=64)
        x_win = [keep.tile([P, T], I32, name=f"x_win{g}") for g in range(PASSES)]
        mu_win = [keep.tile([P, U], F32, name=f"mu_win{t}", align_bytes=64) for t in range(LAST)]
        mu_win.append(mu_pool.tile([P, U], F32, name=f"mu_win{LAST}", offset=0, align_bytes=64))
        rs_win = [rs_pool.tile([P, U], F32, name=f"rs_win{t}", offset=4 * U * t + (2 * U if t == LAST else 0)) for t in range(PACK)]

        nc.vector.memset(xs_win[32:64, :].bitcast(I32), 0)
        nc.vector.memset(xs_win[64:128, :].bitcast(I32), 0)
        nc.gpsimd.memset(w1s[:].bitcast(I32), 0)
        ident = keep.tile([P, P], F32, name="ident", align_bytes=64)
        make_identity(nc, ident[:])
        nc.gpsimd.memset(x_planes[:].bitcast(I32), 0)
        nc.gpsimd.memset(w2s_raw[:].bitcast(I32), 0)

        warm = keep.tile([P, 2], F32, name="warm")
        nc.vector.memset(warm[:, 0:1], 0.0)
        nc.scalar.activation(out=warm[:, 1:2], in_=warm[:, 0:1], func=ACT.Gelu_apprx_tanh)

        def load_scale_rows(plane, scales, q):
            nc.sync.dma_start(
                out=plane[32 * q : 32 * q + 4, :].bitcast(I32).rearrange("r (g c) -> r g c", g=scales.shape[0]),
                in_=scales[:, 4 * q : 4 * q + 4, :].bitcast(I32).rearrange("g r c -> r g c"),
            )

        def move_scale_rows(q):
            nc.sync.dma_start(
                out=x_planes[32 * q : 32 * q + 4, :].bitcast(I32).rearrange("r (g c) -> r g c", g=PASSES),
                in_=xs_picked[8 * q : 8 * q + 8, :].bitcast(I32),
            )

        def load_x(g):
            nc.sync.dma_start(out=x_win[g][:], in_=x_words[g].rearrange("p n t -> p (n t)").bitcast(I32))

        def load_w1_words(g):
            nc.sync.dma_start(out=w1w[g][:].bitcast(I32), in_=w1_words[g].bitcast(I32))

        mu_rows = mu.rearrange("(p t) u -> p t u", t=PACK)
        rs_rows = rs.rearrange("(p t) u -> p t u", t=PACK)
        tables = [(win[t], rows[:, t, :]) for t in range(PACK) for win, rows in ((rs_win, rs_rows), (mu_win, mu_rows))]

        nc.sync.dma_start(offs_sb[:], offs)
        nc.sync.dma_start(out=xs_win[0:32, :].bitcast(I32), in_=x_scales.bitcast(I32).rearrange("g a c -> a g c"))
        nc.sync.dma_start(cl_sb[:], cl)
        nc.vector.tensor_copy(out=xs_picked[:], in_=xs_win[:].indirect(offs_sb[:]))
        for n, (win, rows) in enumerate(tables):
            nc.sync.dma_start(out=win[:], in_=rows)
            if 1 <= n <= QUADS:
                load_scale_rows(w1s, w1_scales, n - 1)
            elif n == QUADS + 1:
                load_w1_words(0)
            elif n > QUADS + 1:
                move_scale_rows(n - QUADS - 2)
        load_x(0)
        for q in range(len(tables) - QUADS - 2, QUADS):
            move_scale_rows(q)
        for q in range(QUADS):
            load_scale_rows(w2s_raw, w2_scales, q)
        load_x(1)
        load_w1_words(1)
        nc.sync.dma_start(out=w2w_raw[:].bitcast(I32), in_=w2_words[0].bitcast(I32))

        def cols(u):
            return slice(u * UNIT, (u + 1) * UNIT)

        def half(h):
            return slice(h * HALF, (h + 1) * HALF)

        def entries(lists, tokens):
            return lists[:, tokens.start // LIST_ROWS : tokens.stop // LIST_ROWS]

        negated = {}
        rs_banks = {}
        y_ps = {}

        def open_unit(u, bank):
            y_ps[u] = psum.tile([P, PACK, UNIT], F32, name=f"y_ps{u}", tag=f"bank{bank}")

        def add_negated(u, k):
            for i in range(PAIR):
                t = PAIR * k + i
                nc.tensor.matmul(
                    y_ps[u][:, t, :], lhsT=negated[k, u // PAIR][:, u % PAIR, i, :], rhs=ident[:], is_transpose=True, start=(t == 0), stop=False
                )

        rs_turned = rs_pool.tile([P, UNITS, PACK, P], F32, name="rs_turned", offset=0)

        def turn(picked, h, name, slot):
            bank = psum.tile([P, PAIR, PAIR, P], F32, name=name, tag=f"bank{slot}")
            for i in range(PAIR):
                for v in range(PAIR):
                    nc.tensor.transpose(bank[:, v, i, :], picked[i][:, cols(PAIR * h + v)], ident[:])
            return bank

        mu_rs_banks = {}

        def negate(k, h, on_vector):
            if (k, h) == (0, 0):
                negated[k, h] = rs_pool.tile([P, PAIR, PAIR, P], F32, name="negated00", offset=4 * U * PACK)
            elif (k, h) == (0, 1):
                negated[k, h] = mu_pool.tile([P, PAIR, PAIR, P], F32, name="negated01", offset=N, align_bytes=64)
            else:
                negated[k, h] = keep.tile([P, PAIR, PAIR, P], F32, name=f"negated{k}{h}", align_bytes=64)
            if on_vector:
                nc.vector.tensor_scalar(negated[k, h][:], mu_rs_banks[k, h][:], -1.0, None, ALU.mult)
            else:
                nc.scalar.activation(out=negated[k, h][:], in_=mu_rs_banks[k, h][:], func=ACT.Copy, scale=-1.0)

        for k in range(PACK // PAIR):
            tiles = range(PAIR * k, PAIR * (k + 1))
            rs_picked = [keep.tile([P, S], F32, name=f"rs_picked{t}", align_bytes=64) for t in tiles]
            mu_rs = [keep.tile([P, S], F32, name=f"mu_rs{t}", align_bytes=64) for t in tiles]
            for i, t in enumerate(tiles):
                for h in range(HALVES):
                    nc.scalar.activation(out=rs_picked[i][:, half(h)], in_=rs_win[t][:].indirect(entries(cl_sb, half(h))), func=ACT.Copy)
                for h in range(HALVES):
                    nc.vector.tensor_tensor(mu_rs[i][:, half(h)], mu_win[t][:].indirect(entries(cl_sb, half(h))), rs_picked[i][:, half(h)], ALU.mult)
            for h in range(HALVES):
                rs_banks[k, h] = turn(rs_picked, h, f"rs_ps{k}{h}", PAIR * h + k)
                mu_rs_banks[k, h] = turn(mu_rs, h, f"mu_rs_ps{k}{h}", MU_RS_BANKS[k][h])
        for k in range(PACK // PAIR):
            negate(k, 0, k == 1)
        for u in range(PAIR):
            open_unit(u, UNITS + u)
            for k in range(PACK // PAIR):
                add_negated(u, k)
        for h in range(HALVES):
            for k in range(PACK // PAIR):
                nc.scalar.copy(out=rs_turned[:, PAIR * h : PAIR * (h + 1), PAIR * k : PAIR * (k + 1), :], in_=rs_banks[k, h][:])
        for k in range(PACK // PAIR):
            negate(k, 1, False)

        x_picked = [keep.tile([P, S], U32, name=f"x_picked{g}", align_bytes=64) for g in range(PASSES)]

        def pick_x(g, order, step):
            for i in order:
                tokens = slice(i * step, (i + 1) * step)
                nc.vector.tensor_copy(out=x_picked[g][:, tokens], in_=x_win[g][:].bitcast(U32).indirect(entries(offs_sb, tokens)))

        pick_x(0, range(HALVES), HALF)
        pick_x(1, ORDER, UNIT)

        turned = [psum.tile([P, H], F32, name=f"turned{u}", tag=f"bank{u}") for u in range(UNITS)]
        for g in range(PASSES):
            for u in ORDER if g == PASSES - 1 else range(UNITS):
                nc.tensor.matmul_mx(
                    out=turned[u][:],
                    lhsT=x_picked[g][:, cols(u)].bitcast(FP8X4),
                    lhsT_scale=x_planes[:, g * S + u * UNIT : g * S + (u + 1) * UNIT],
                    rhs=w1w[g][:].bitcast(FP4X4),
                    rhs_scale=w1s[:, g * H : (g + 1) * H],
                    start=(g == 0),
                    stop=(g == PASSES - 1),
                )
        y_rs = [keep.tile([P, PACK, P], F32, name=f"y_rs{u}", align_bytes=64) for u in range(UNITS)]

        def y_columns(u):
            return turned[u][:].rearrange("j (m t) -> j t m", t=PACK)

        y_dealt = keep.tile([P, PACK, P], F32, name="y_dealt", align_bytes=64)
        nc.scalar.copy(out=y_dealt[:], in_=y_columns(SHARED))
        nc.gpsimd.tensor_tensor(y_rs[SHARED][:], y_dealt[:], rs_turned[:, SHARED, :, :], ALU.mult)
        for u in DONE:
            if u != SHARED:
                nc.vector.tensor_tensor(y_rs[u][:], rs_turned[:, u, :, :], y_columns(u), ALU.mult)
            if u >= PAIR:
                open_unit(u, SHARED + UNITS - 1 - u)
                for k in range(PACK // PAIR):
                    add_negated(u, k)
            for t in range(PACK):
                nc.tensor.matmul(y_ps[u][:, t, :], lhsT=y_rs[u][:, t, :], rhs=ident[:], is_transpose=True, start=False, stop=(t == LAST))

        w2w = keep.tile([P, 2 * N], U8, name="w2w", align_bytes=64)
        w2s = mu_pool.tile([P, N], U8, name="w2s", offset=0, align_bytes=64)
        nc.gpsimd.tensor_copy(
            out=w2w[:].bitcast(U16).rearrange("p (t m) -> p t m", t=PACK),
            in_=w2w_raw[:].bitcast(U16).rearrange("p (m t) -> p t m", t=PACK),
        )
        nc.gpsimd.tensor_copy(
            out=w2s[:].rearrange("p (t m) -> p t m", t=PACK),
            in_=w2s_raw[:].rearrange("p (m t) -> p t m", t=PACK),
        )

        out_rows = out_0.rearrange("(p t) j -> p t j", t=PACK)
        out_words = out_1[0].rearrange("p n t -> p (n t)").bitcast(I32)
        o_scales = keep.tile([P, S], U8, name="o_scales", align_bytes=64)
        o_words = keep.tile([P, S], I32, name="o_words", align_bytes=64)
        o_bf = keep.tile([P, S, PACK], BF16, name="o_bf", align_bytes=64)

        def by_tile(ap):
            return ap.rearrange("p t (c i) -> p c t i", i=LINE)

        def by_token(ap):
            return ap.rearrange("p (c i) t -> p c t i", i=LINE)

        def second_layer(u):
            z = keep.tile([P, UNIT, PACK], BF16, name=f"z{u}", align_bytes=64)
            nc.scalar.activation(out=by_token(z[:]), in_=by_tile(y_ps[u][:]), func=ACT.Gelu_apprx_tanh)
            z_words = keep.tile([P, UNIT], U32, name=f"z_words{u}", tag=f"z_words{0 if u == SHARED else u}", align_bytes=64)
            z_scales = keep.tile([P, UNIT], U8, name=f"z_scales{u}", align_bytes=64)
            nc.vector.quantize_mx(out=z_words[:].bitcast(FP8X4), scales=z_scales[:], in_=z[:].rearrange("p j t -> p (j t)"))
            o_ps = psum.tile([P, PACK, UNIT], F32, name=f"o_ps{u}", tag=f"bank{RESULT_BANKS[u]}")
            for t in range(PACK):
                nc.tensor.matmul_mx(
                    out=o_ps[:, t, :],
                    lhsT=w2w[:, 2 * t * P : 2 * (t + 1) * P].bitcast(FP4X4),
                    lhsT_scale=w2s[:, t * P : (t + 1) * P],
                    rhs=z_words[:].bitcast(FP8X4),
                    rhs_scale=z_scales[:],
                    start=True,
                    stop=True,
                )
            return o_ps

        o_sb = {}

        def store(u):
            o_sb[u] = keep.tile([P, PACK, UNIT], F32, name=f"o_sb{u}", align_bytes=64)
            if u == 0:
                nc.vector.tensor_copy(out=o_sb[u][:], in_=results[u][:])
            else:
                nc.scalar.copy(out=o_sb[u][:], in_=results[u][:])
            nc.sync.dma_start(out=out_rows[:, :, cols(u)], in_=o_sb[u][:])

        def round_result(u):
            nc.vector.tensor_copy(out=by_token(o_bf[:, cols(u), :]), in_=by_tile(o_sb[u][:]))

        def quantise_results(tokens):
            nc.vector.quantize_mx(
                out=o_words[:, tokens].bitcast(FP8X4), scales=o_scales[:, tokens], in_=o_bf[:, tokens, :].rearrange("p j t -> p (j t)")
            )

        def store_words(tokens):
            nc.sync.dma_start(out=out_words[:, tokens], in_=o_words[:, tokens])

        results = {u: second_layer(u) for u in DONE[:-1]}
        store(0)
        results[SHARED] = second_layer(SHARED)
        round_result(0)
        store(1)
        round_result(1)
        quantise_results(half(0))
        store_words(half(0))
        for u in DONE[PAIR:]:
            store(u)
            round_result(u)
            quantise_results(cols(u))
        store_words(half(1))

        for q in range(QUADS):
            (nc.scalar if q % 2 else nc.sync).dma_start(
                out=out_2[0, 4 * q : 4 * q + 4, :].bitcast(I32), in_=o_scales[32 * q : 32 * q + 4, :].bitcast(I32)
            )
